import numpy as np
import ml_dtypes


def mxq(x, axis, fmt="e4m3"):
    dtype, down = {"e4m3": (ml_dtypes.float8_e4m3fn, 7), "e5m2": (ml_dtypes.float8_e5m2, 14)}[fmt]
    v = np.moveaxis(np.asarray(x, np.float32).astype(ml_dtypes.bfloat16).astype(np.float64), axis, -1)
    blocks = v.reshape(v.shape[:-1] + (-1, 32))
    amax = np.abs(blocks).max(-1, keepdims=True)
    byte = np.maximum(np.where(amax > 0, np.frexp(amax)[1] - 1 + 127, 0) - down, 1)
    scale = np.exp2(byte - 127.0)
    codes = (blocks / scale).astype(np.float32).astype(dtype).astype(np.float64)
    return np.moveaxis((codes * scale).reshape(v.shape), -1, axis)


WIDE = False


def mx_kscale(k):
    if not WIDE:
        return np.ones(k)
    levels = np.array([10, -10, 5, -5, 0])
    if k % 512:
        return np.exp2(np.random.permutation(np.resize(levels, k // 32))).repeat(32)
    a = np.empty((k // 512, 16))
    for p in range(k // 512):
        a[p, :8] = np.random.permutation(np.resize(levels, 8))
        for g in range(8):
            far = levels[np.abs(levels - a[p, g]) >= 10]
            a[p, g + 8] = far[np.random.randint(len(far))]
    return np.exp2(a.ravel()).repeat(32)


def f64(x):
    return np.asarray(x).astype(np.float64)


def striped(idx):
    return np.tile(idx.reshape(-1, 16).T, (8, 1)).astype(np.uint16)


def unstriped(offs):
    return offs[:16].T.reshape(-1).astype(np.int64)


E2M1 = np.array([0.0, 0.5, 1.0, 1.5, 2.0, 3.0, 4.0, 6.0, -0.0, -0.5, -1.0, -1.5, -2.0, -3.0, -4.0, -6.0])


def pack_weight(w, fmt):
    k, n = w.shape
    w = f64(np.asarray(w, np.float32).astype(ml_dtypes.bfloat16)).reshape(k // 32, 32, n)
    amax = np.abs(w).max(1)
    if fmt == "e4m3":
        byte = np.frexp(amax)[1] - 1 + 127 - 7
    else:
        mant, ex = np.frexp(amax / 6.0)
        byte = np.where(mant > 0.5, ex, ex - 1) + 127
    byte = np.clip(np.where(amax > 0, byte, 1), 1, 254)
    scaled = (w * np.exp2(127.0 - byte)[:, None, :]).reshape(k, n).astype(np.float32)
    by_word = np.ascontiguousarray(scaled.reshape(k // 512, 128, 4, n).transpose(0, 1, 3, 2))
    if fmt == "e4m3":
        words = by_word.astype(ml_dtypes.float8_e4m3fn).view(np.uint8)
    else:
        c = by_word.astype(ml_dtypes.float4_e2m1fn).view(np.uint8) & 0xF
        words = (c[..., 0::2] | (c[..., 1::2] << 4)).reshape(k // 512, 128, 2 * n)
    return np.ascontiguousarray(words), np.ascontiguousarray(byte.astype(np.uint8).reshape(k // 512, 16, n))


def unpack_weight(words, scales, fmt):
    g, _, n = scales.shape
    words = np.ascontiguousarray(words).reshape(g, 128, n, -1)
    if fmt == "e4m3":
        vals = words.view(ml_dtypes.float8_e4m3fn).astype(np.float64)
    else:
        nib = np.empty((g, 128, n, 4), np.uint8)
        nib[..., 0::2] = words & 0xF
        nib[..., 1::2] = words >> 4
        vals = E2M1[nib]
    vals = vals * np.repeat(np.exp2(scales.astype(np.float64) - 127.0), 8, axis=1)[..., None]
    return vals.transpose(0, 1, 3, 2).reshape(g * 512, n)


def gelu(v):
    return 0.5 * v * (1.0 + np.tanh(np.sqrt(2.0 / np.pi) * (v + 0.044715 * v**3)))


K, H, N, T, S, T2, P = 1024, 512, 768, 2048, 1024, 2048, 1024

def setup_inputs():
    n = np.random.standard_normal
    s = mx_kscale(K)[:, None]
    u = mx_kscale(H)[:, None]
    tab_words, tab_scales = pack_weight(n((K, T)) * s, "e4m3")
    wb_words, wb_scales = pack_weight(n((K, H)) / np.sqrt(K) * u.T / s, "e2m1")
    wo_words, wo_scales = pack_weight(n((H, N)) / np.sqrt(H) / u, "e4m3")
    return {
        "tab_words": tab_words, "tab_scales": tab_scales,
        "offs": striped(np.random.permutation(T)[:S]),
        "wa": (n((K, H)) / np.sqrt(K) * u.T / s).astype(np.float32),
        "wb_words": wb_words, "wb_scales": wb_scales,
        "offs2": striped(np.random.permutation(T2)[:S]),
        "wgs": np.exp(0.3 * n((128, S))).astype(np.float32),
        "tol": (np.exp(0.4 * n((H, T2))) * u).astype(np.float32),
        "wo_words": wo_words, "wo_scales": wo_scales,
        "offs3": striped(np.random.permutation(T2)[:P]),
        "bay": np.exp(0.5 * n(N)).astype(np.float32),
        "offs4": striped(np.random.permutation(T2)[:P]),
        "wgo": np.exp(0.3 * n((128, P))).astype(np.float32),
    }

def reference(tab_words, tab_scales, offs, wa, wb_words, wb_scales, offs2, wgs, tol,
              wo_words, wo_scales, offs3, bay, offs4, wgo):
    v = unpack_weight(tab_words, tab_scales, "e4m3")[:, unstriped(offs)]
    wb = unpack_weight(wb_words, wb_scales, "e2m1")
    wo = unpack_weight(wo_words, wo_scales, "e4m3")
    h = np.abs((mxq(f64(wa), 0, "e4m3").T @ v) - (wb.T @ v))
    page = np.zeros((H, T2))
    page[:, unstriped(offs2)] = np.tile(f64(wgs), (H // 128, 1)) * h
    z = f64(tol) - page
    y = wo.T @ mxq(z, 0, "e4m3")
    x = y[:, unstriped(offs3)]
    x = np.exp(-0.4 * np.square(x)) * f64(bay)[:, None]
    out = np.zeros((N, T2))
    out[:, unstriped(offs4)] = np.tile(f64(wgo), (N // 128, 1)) * x
    return out

@@ -1,0 +1,328 @@
+from contextlib import ExitStack
+
+import concourse.mybir as mybir
+from concourse.masks import make_identity
+
+K, H, N, T, S, T2, PICK = 1024, 512, 768, 2048, 1024, 2048, 1024
+FLOPS = 2 * 2 * K * H * S + 2 * H * N * T2
+
+F32 = mybir.dt.float32
+BF16 = mybir.dt.bfloat16
+I32 = mybir.dt.int32
+U32 = mybir.dt.uint32
+U16 = mybir.dt.uint16
+U8 = mybir.dt.uint8
+E4M3 = mybir.dt.float8_e4m3fn_x4
+E2M1 = mybir.dt.float4_e2m1fn_x4
+ACT = mybir.ActivationFunctionType
+MULT = mybir.AluOpType.mult
+
+P = 128
+BANK = 512
+PASSES = K // 512
+ROW_BLOCKS = H // P
+OUT_BLOCKS = N // P
+CHUNKS = T2 // BANK
+TAIL = 768
+
+
+def tile_list_rework_bay_scores_kernel(
+    tc, tab_words, tab_scales, offs, wa, wb_words, wb_scales, offs2, wgs, tol,
+    wo_words, wo_scales, offs3, bay, offs4, wgo, out,
+):
+    nc = tc.nc
+    with ExitStack() as ctx:
+        lists = ctx.enter_context(tc.tile_pool(name="lists", bufs=1))
+        keep = ctx.enter_context(tc.tile_pool(name="keep", bufs=1))
+        ring = ctx.enter_context(tc.tile_pool(name="ring", bufs=3))
+        psum = ctx.enter_context(tc.psum_pool(name="psum", bufs=1))
+
+        idx = lists.tile([P, S // 16], U16, name="idx")
+        idx2 = lists.tile([P, S // 16], U16, name="idx2")
+        idx3 = lists.tile([P, PICK // 16], U16, name="idx3")
+        idx4 = lists.tile([P, PICK // 16], U16, name="idx4")
+
+        tab_plane = keep.tile([P, T], U8, name="tab_plane", align_bytes=64)
+        wb_plane = keep.tile([P, PASSES, H], U8, name="wb_plane", align_bytes=64)
+        wo_plane = keep.tile([P, N], U8, name="wo_plane", align_bytes=64)
+        v_plane = keep.tile([P, S], U8, name="v_plane", align_bytes=64)
+        v_plane1 = keep.tile([P, S], U8, name="v_plane1", align_bytes=64)
+        pages = [keep.tile([P, T2], F32, name="page0")]
+        for plane in (tab_plane[:], wb_plane[:], v_plane1[:], wo_plane[:]):
+            nc.vector.memset(plane.bitcast(I32), 0)
+        nc.vector.memset(pages[0][:], 0.0)
+        ident = keep.tile([P, P], F32, name="ident")
+        make_identity(nc, ident[:])
+        warm = keep.tile([P, 1], F32, name="warm")
+        nc.scalar.activation(out=warm[:], in_=ident[:, 0:1], func=ACT.Exp)
+
+        nc.sync.dma_start(idx[:], offs)
+        nc.sync.dma_start(idx2[:], offs2)
+        for q in range(4):
+            nc.sync.dma_start(
+                out=tab_plane[32 * q : 32 * q + 8, :].bitcast(I32),
+                in_=tab_scales[:, 4 * q : 4 * q + 4, :].bitcast(I32),
+            )
+        tab = [keep.tile([P, T], U32, name="tab%d" % a, tag="tab%d" % a) for a in range(PASSES)]
+        wa_rows = wa.rearrange("(a p j) c -> a p j c", a=PASSES, j=4)
+        wa_raw = [keep.tile([P, PASSES, 4, w], F32, name="wa_raw%d" % i, tag="wa_raw%d" % i) for i, w in enumerate((P, P, 2 * P))]
+
+        def load_tab(a):
+            nc.sync.dma_start(out=tab[a][:].bitcast(I32), in_=tab_words[a].rearrange("p t i -> p (t i)").bitcast(I32))
+
+        def load_wa(i, c0, c1):
+            for a in range(PASSES):
+                nc.sync.dma_start(out=wa_raw[i][:, a, :, :], in_=wa_rows[a][:, :, c0:c1])
+
+        load_tab(0)
+        load_wa(0, 0, P)
+        load_tab(1)
+        wb_codes = keep.tile([P, PASSES, 2 * H], U8, name="wb_codes", align_bytes=64)
+        nc.sync.dma_start(out=wb_codes[:].bitcast(I32), in_=wb_words.rearrange("a p n -> p a n").bitcast(I32))
+        for q in range(4):
+            nc.gpsimd.dma_start(
+                out=wb_plane[32 * q : 32 * q + 4, :, :].bitcast(I32),
+                in_=wb_scales[:, 4 * q : 4 * q + 4, :].rearrange("a r c -> r a c").bitcast(I32),
+            )
+        gain = keep.tile([P, S], F32, name="gain")
+        nc.sync.dma_start(out=gain[:, 0:BANK], in_=wgs[:, 0:BANK])
+        load_wa(1, P, 2 * P)
+        nc.sync.dma_start(out=gain[:, BANK:S], in_=wgs[:, BANK:S])
+        load_wa(2, 2 * P, 4 * P)
+        tols = []
+        for b in range(ROW_BLOCKS):
+            tols.append(ring.tile([P, T2], F32, name="tol%d" % b, tag="rows", bufs=4))
+        for b in range(2):
+            nc.sync.dma_start(out=tols[b][:], in_=tol[b * P : (b + 1) * P, :])
+        wgo_sb = keep.tile([P, PICK], F32, name="wgo_sb")
+        nc.sync.dma_start(out=wgo_sb[:], in_=wgo)
+        bay_sb = keep.tile([P, OUT_BLOCKS], F32, name="bay_sb")
+        with nc.allow_non_contiguous_dma(reason="one value of bay for each partition"):
+            nc.sync.dma_start(out=bay_sb[:], in_=bay.rearrange("(n p) -> p n", p=P))
+        for b in (3, 2):
+            nc.sync.dma_start(out=tols[b][:], in_=tol[b * P : (b + 1) * P, :])
+        wo_codes = keep.tile([P, N], U32, name="wo_codes", align_bytes=64)
+        nc.sync.dma_start(out=wo_codes[:].bitcast(I32), in_=wo_words[0].rearrange("p c i -> p (c i)").bitcast(I32))
+        for q in range(4):
+            nc.sync.dma_start(
+                out=wo_plane[32 * q : 32 * q + 4, :].bitcast(I32),
+                in_=wo_scales[0, 4 * q : 4 * q + 4, :].bitcast(I32),
+            )
+        nc.sync.dma_start(idx3[:], offs3)
+        nc.sync.dma_start(idx4[:], offs4)
+
+        v_codes = [keep.tile([P, S], U32, name="v_codes%d" % a, align_bytes=64) for a in range(PASSES)]
+        halves = [slice(0, BANK), slice(BANK, S)]
+        list_halves = [slice(0, BANK // 16), slice(BANK // 16, S // 16)]
+        nc.vector.tensor_copy(v_plane[:], tab_plane[:].indirect(idx[:]))
+        for q in range(4):
+            nc.scalar.dma_start(
+                out=v_plane1[32 * q : 32 * q + 4, :].bitcast(I32), in_=v_plane[32 * q + 4 : 32 * q + 8, :].bitcast(I32)
+            )
+        nc.vector.tensor_copy(v_codes[0][:], tab[0][:].indirect(idx[:]))
+        nc.vector.tensor_copy(v_codes[1][:, halves[0]], tab[1][:].indirect(idx[:, list_halves[0]]))
+
+        wa_bf = [keep.tile([P, w * PASSES * 4], BF16, name="wa_bf%d" % i, align_bytes=64) for i, w in enumerate((P, P, 2 * P))]
+        wa_codes = [keep.tile([P, w * PASSES], U32, name="wa_codes%d" % i, align_bytes=64) for i, w in enumerate((P, P, 2 * P))]
+        wa_plane = [keep.tile([P, w * PASSES], U8, name="wa_plane%d" % i, align_bytes=64) for i, w in enumerate((P, P, 2 * P))]
+
+        def round_wa(i, part):
+            width = PASSES * P * 4
+            nc.scalar.activation(
+                out=wa_bf[i][:, part * width : (part + 1) * width].rearrange("p (a c j) -> p a c j", a=PASSES, j=4),
+                in_=wa_raw[i][:, :, :, part * P : (part + 1) * P].rearrange("p a j c -> p a c j"),
+                func=ACT.Copy,
+                scale=-1.0,
+            )
+
+        def quantize_wa(i):
+            nc.vector.quantize_mx(out=wa_codes[i][:].bitcast(E4M3), scales=wa_plane[i][:], in_=wa_bf[i][:])
+
+        hs = [keep.tile([P, S], F32, name="h%d" % b) for b in range(ROW_BLOCKS)]
+
+        def features(b, c0, c1, tag="a"):
+            i, part = min(b, 2), max(b - 2, 0)
+            acc = psum.tile([P, BANK], F32, name="acc", tag=tag, bufs=4)
+            step = BANK if c1 - c0 == BANK else P
+            for g0 in range(c0, c1, step):
+                cols = slice(g0, g0 + step)
+                group = acc[:, g0 - c0 : g0 - c0 + step]
+                for a in range(PASSES):
+                    w_cols = slice((part * PASSES + a) * P, (part * PASSES + a + 1) * P)
+                    nc.tensor.matmul_mx(
+                        out=group,
+                        lhsT=wa_codes[i][:, w_cols].bitcast(E4M3),
+                        lhsT_scale=wa_plane[i][:, w_cols],
+                        rhs=v_codes[a][:, cols].bitcast(E4M3),
+                        rhs_scale=v_plane[4 * a : P, cols],
+                        start=(a == 0),
+                        stop=False,
+                    )
+                    nc.tensor.matmul_mx(
+                        out=group,
+                        lhsT=wb_codes[:, a, 2 * b * P : 2 * (b + 1) * P].bitcast(E2M1),
+                        lhsT_scale=wb_plane[:, a, b * P : (b + 1) * P],
+                        rhs=v_codes[a][:, cols].bitcast(E4M3),
+                        rhs_scale=(v_plane, v_plane1)[a][:, cols],
+                        start=False,
+                        stop=(a == PASSES - 1),
+                    )
+            nc.scalar.activation(out=hs[b][:, c0:c1], in_=acc[:, 0 : c1 - c0], func=ACT.Abs)
+
+        def negate_gain(half):
+            nc.scalar.activation(out=gain[:, halves[half]], in_=gain[:, halves[half]], func=ACT.Copy, scale=-1.0)
+
+        def fill_cells(b, c0, c1):
+            window = pages[b % 3][:].indirect(idx2[:, c0 // 16 : c1 // 16])
+            nc.vector.tensor_tensor(window, hs[b][:, c0:c1], gain[:, c0:c1], MULT)
+
+        round_wa(0, 0)
+        quantize_wa(0)
+        nc.vector.tensor_copy(v_codes[1][:, halves[1]], tab[1][:].indirect(idx[:, list_halves[1]]))
+        pages.append(keep.tile([P, T2], F32, name="page1", tag="tab1"))
+        nc.gpsimd.memset(pages[1][:], 0.0)
+        negate_gain(0)
+        features(0, 0, BANK)
+        round_wa(1, 0)
+        negate_gain(1)
+        features(0, BANK, S)
+        fill_cells(0, 0, BANK)
+        quantize_wa(1)
+        fill_cells(0, BANK, S)
+        round_wa(2, 0)
+        round_wa(2, 1)
+        pages.append(keep.tile([P, T2], F32, name="page2", tag="wa_raw2"))
+        nc.gpsimd.memset(pages[2][:], 0.0)
+        features(1, 0, BANK)
+        features(1, BANK, S)
+        fill_cells(1, 0, BANK)
+        quantize_wa(2)
+        fill_cells(1, BANK, S)
+
+        z_t = [keep.tile([P, 4, 2, P, 2], BF16, name="z_t%d" % c) for c in range(CHUNKS)]
+
+        def open_turned(b, c, tag="b"):
+            bank = psum.tile([P, 4, P], F32, name="turned", tag=tag, bufs=4)
+            for s in range(4):
+                cols = slice(c * BANK + s * P, c * BANK + (s + 1) * P)
+                nc.tensor.matmul(bank[:, s, :], tols[b][:, cols], ident[:], start=(s == 0), stop=False, is_transpose=True)
+            return bank
+
+        def close_turned(b, c, bank, copy):
+            for s in range(4):
+                cols = slice(c * BANK + s * P, c * BANK + (s + 1) * P)
+                nc.tensor.matmul(bank[:, s, :], pages[b % 3][:, cols], ident[:], start=False, stop=(s == 3), is_transpose=True)
+            copy(
+                out=z_t[c][:, :, :, 32 * b : 32 * (b + 1), :],
+                in_=bank[:].rearrange("t s (p u e) -> t s u p e", u=2, e=2),
+            )
+
+        weights = []
+
+        def weigh(n):
+            w = ring.tile([P, PICK], F32, name="bay_weight", tag="bay_weight", bufs=2)
+            nc.scalar.activation(out=w[:], in_=wgo_sb[:], func=ACT.Copy, scale=bay_sb[:, n : n + 1])
+            weights.append(w)
+
+        last = ROW_BLOCKS - 1
+        features(2, 0, BANK)
+        features(2, BANK, S)
+        features(last, 0, BANK)
+        features(last, BANK, TAIL)
+        for c in range(CHUNKS):
+            close_turned(0, c, open_turned(0, c), nc.scalar.copy)
+        fill_cells(2, 0, S)
+        weigh(0)
+        for c in range(CHUNKS):
+            close_turned(1, c, open_turned(1, c), nc.scalar.copy)
+        fill_cells(last, 0, TAIL)
+        weigh(1)
+        banks = [open_turned(last, c, "a") for c in range(CHUNKS)]
+        for c in range(CHUNKS):
+            close_turned(2, c, open_turned(2, c), nc.scalar.copy)
+        features(last, TAIL, S, "b")
+        fill_cells(last, TAIL, S)
+        bays = [ring.tile([P, T2], F32, name="bays%d" % i, tag="rows", bufs=4) for i in range(2)]
+        for page in bays:
+            nc.gpsimd.memset(page[:], 0.0)
+
+        z_bf = [keep.tile([P, 4 * BANK], BF16, name="z_bf%d" % c, align_bytes=64) for c in range(CHUNKS)]
+        z_codes = [keep.tile([P, BANK], U32, name="z_codes%d" % c, align_bytes=64) for c in range(CHUNKS)]
+        z_plane = [keep.tile([P, BANK], U8, name="z_plane%d" % c, align_bytes=64) for c in range(CHUNKS)]
+
+        def turn_back(c):
+            words = z_t[c][:].rearrange("t s u p e -> t (s u p e)").bitcast(F32)
+            for half, copy in enumerate((nc.scalar.copy, nc.vector.tensor_copy)):
+                bank = psum.tile([P, 2, 2 * P], F32, name="turned", tag="b", bufs=4)
+                for s in range(2):
+                    for u in range(2):
+                        w0 = ((2 * half + s) * 2 + u) * P
+                        nc.tensor.transpose(bank[:, u, s * P : (s + 1) * P], words[:, w0 : w0 + P], ident[:])
+                copy(
+                    out=z_bf[c][:].bitcast(F32)[:, half * BANK : (half + 1) * BANK].rearrange("p (t u) -> p t u", u=2),
+                    in_=bank[:].rearrange("p u t -> p t u"),
+                )
+            nc.vector.quantize_mx(out=z_codes[c][:].bitcast(E4M3), scales=z_plane[c][:], in_=z_bf[c][:])
+
+        def score(n, c, y, copy):
+            acc = psum.tile([P, BANK], F32, name="acc", tag="a", bufs=4)
+            nc.tensor.matmul_mx(
+                out=acc[:],
+                lhsT=wo_codes[:, n * P : (n + 1) * P].bitcast(E4M3),
+                lhsT_scale=wo_plane[:, n * P : (n + 1) * P],
+                rhs=z_codes[c][:].bitcast(E4M3),
+                rhs_scale=z_plane[c][:],
+                start=True,
+                stop=True,
+            )
+            copy(out=y[:, c * BANK : (c + 1) * BANK], in_=acc[:])
+
+        ys = [ring.tile([P, T2], F32, name="y", tag="y")]
+        close_turned(last, 0, banks[0], nc.scalar.copy)
+        close_turned(last, 1, banks[1], nc.vector.tensor_copy)
+        turn_back(0)
+        close_turned(last, 2, banks[2], nc.scalar.copy)
+        close_turned(last, 3, banks[3], nc.scalar.copy)
+        turn_back(1)
+        score(0, 0, ys[0], nc.scalar.copy)
+        turn_back(2)
+        score(0, 1, ys[0], nc.scalar.copy)
+        turn_back(3)
+        score(0, 2, ys[0], nc.scalar.copy)
+        score(0, 3, ys[0], nc.vector.tensor_copy)
+
+        picked = []
+
+        def products(n):
+            y = ring.tile([P, T2], F32, name="y", tag="y")
+            for c in range(CHUNKS):
+                score(n, c, y, nc.scalar.copy)
+            ys.append(y)
+
+        def pick(n):
+            x = ring.tile([P, PICK], F32, name="x", tag="x")
+            nc.vector.tensor_copy(x[:], ys[n][:].indirect(idx3[:]))
+            picked.append(x)
+
+        def bell(n):
+            x = picked[n]
+            nc.scalar.activation(out=x[:], in_=x[:], func=ACT.Square)
+            nc.scalar.activation(out=x[:], in_=x[:], func=ACT.Exp, scale=-0.4)
+
+        def place(n):
+            page = bays[n % 2]
+            nc.vector.tensor_tensor(page[:].indirect(idx4[:]), picked[n][:], weights[n][:], MULT)
+            nc.sync.dma_start(out=out[n * P : (n + 1) * P, :], in_=page[:])
+
+        products(1)
+        pick(0)
+        bell(0)
+        for n in range(OUT_BLOCKS):
+            if n + 2 < OUT_BLOCKS:
+                products(n + 2)
+            if n + 1 < OUT_BLOCKS:
+                pick(n + 1)
+                bell(n + 1)
+            place(n)
+            if n + 2 < OUT_BLOCKS:
+                weigh(n + 2)

@@ -24,6 +24,7 @@ ROW_BLOCKS = H // P
 OUT_BLOCKS = N // P
 CHUNKS = T2 // BANK
 TAIL = 768
+BANKS = {"a": 4, "b": 3, "c": 1}
 
 
 def tile_list_rework_bay_scores_kernel(
@@ -47,14 +48,16 @@ def tile_list_rework_bay_scores_kernel(
         wo_plane = keep.tile([P, N], U8, name="wo_plane", align_bytes=64)
         v_plane = keep.tile([P, S], U8, name="v_plane", align_bytes=64)
         v_plane1 = keep.tile([P, S], U8, name="v_plane1", align_bytes=64)
-        pages = [keep.tile([P, T2], F32, name="page0")]
+        pages = [keep.tile([P, T2], F32, name="page0", tag="page0")]
+        warm = keep.tile([P, 2], F32, name="warm")
+        nc.vector.memset(warm[:, 0:1], 0.0)
+        nc.scalar.activation(out=warm[:, 1:2], in_=warm[:, 0:1], func=ACT.Exp)
         for plane in (tab_plane[:], wb_plane[:], v_plane1[:], wo_plane[:]):
             nc.vector.memset(plane.bitcast(I32), 0)
         nc.vector.memset(pages[0][:], 0.0)
         ident = keep.tile([P, P], F32, name="ident")
-        make_identity(nc, ident[:])
-        warm = keep.tile([P, 1], F32, name="warm")
-        nc.scalar.activation(out=warm[:], in_=ident[:, 0:1], func=ACT.Exp)
+        nc.vector.memset(ident[:], 0.0)
+        make_identity(nc, ident[:], nomemset=True)
 
         nc.sync.dma_start(idx[:], offs)
         nc.sync.dma_start(idx2[:], offs2)
@@ -75,16 +78,16 @@ def tile_list_rework_bay_scores_kernel(
                 nc.sync.dma_start(out=wa_raw[i][:, a, :, :], in_=wa_rows[a][:, :, c0:c1])
 
         load_tab(0)
-        load_wa(0, 0, P)
-        load_tab(1)
-        wb_codes = keep.tile([P, PASSES, 2 * H], U8, name="wb_codes", align_bytes=64)
-        nc.sync.dma_start(out=wb_codes[:].bitcast(I32), in_=wb_words.rearrange("a p n -> p a n").bitcast(I32))
         for q in range(4):
             nc.gpsimd.dma_start(
                 out=wb_plane[32 * q : 32 * q + 4, :, :].bitcast(I32),
                 in_=wb_scales[:, 4 * q : 4 * q + 4, :].rearrange("a r c -> r a c").bitcast(I32),
             )
-        gain = keep.tile([P, S], F32, name="gain")
+        load_wa(0, 0, P)
+        load_tab(1)
+        wb_codes = keep.tile([P, PASSES, 2 * H], U8, name="wb_codes", align_bytes=64)
+        nc.sync.dma_start(out=wb_codes[:].bitcast(I32), in_=wb_words.rearrange("a p n -> p a n").bitcast(I32))
+        gain = keep.tile([P, S], F32, name="gain", tag="gain")
         nc.sync.dma_start(out=gain[:, 0:BANK], in_=wgs[:, 0:BANK])
         load_wa(1, P, 2 * P)
         nc.sync.dma_start(out=gain[:, BANK:S], in_=wgs[:, BANK:S])
@@ -92,15 +95,14 @@ def tile_list_rework_bay_scores_kernel(
         tols = []
         for b in range(ROW_BLOCKS):
             tols.append(ring.tile([P, T2], F32, name="tol%d" % b, tag="rows", bufs=4))
-        for b in range(2):
+        for b in range(3):
             nc.sync.dma_start(out=tols[b][:], in_=tol[b * P : (b + 1) * P, :])
         wgo_sb = keep.tile([P, PICK], F32, name="wgo_sb")
         nc.sync.dma_start(out=wgo_sb[:], in_=wgo)
         bay_sb = keep.tile([P, OUT_BLOCKS], F32, name="bay_sb")
         with nc.allow_non_contiguous_dma(reason="one value of bay for each partition"):
             nc.sync.dma_start(out=bay_sb[:], in_=bay.rearrange("(n p) -> p n", p=P))
-        for b in (3, 2):
-            nc.sync.dma_start(out=tols[b][:], in_=tol[b * P : (b + 1) * P, :])
+        nc.sync.dma_start(out=tols[3][:], in_=tol[3 * P : 4 * P, :])
         wo_codes = keep.tile([P, N], U32, name="wo_codes", align_bytes=64)
         nc.sync.dma_start(out=wo_codes[:].bitcast(I32), in_=wo_words[0].rearrange("p c i -> p (c i)").bitcast(I32))
         for q in range(4):
@@ -140,9 +142,12 @@ def tile_list_rework_bay_scores_kernel(
 
         hs = [keep.tile([P, S], F32, name="h%d" % b) for b in range(ROW_BLOCKS)]
 
-        def features(b, c0, c1, tag="a"):
+        def take_bank(tag, shape):
+            return psum.tile(shape, F32, name="bank_" + tag, tag=tag, bufs=BANKS[tag])
+
+        def differences(b, c0, c1, tag):
             i, part = min(b, 2), max(b - 2, 0)
-            acc = psum.tile([P, BANK], F32, name="acc", tag=tag, bufs=4)
+            acc = take_bank(tag, [P, BANK])
             step = BANK if c1 - c0 == BANK else P
             for g0 in range(c0, c1, step):
                 cols = slice(g0, g0 + step)
@@ -167,20 +172,24 @@ def tile_list_rework_bay_scores_kernel(
                         start=False,
                         stop=(a == PASSES - 1),
                     )
+            return acc
+
+        def features(b, c0, c1):
+            acc = differences(b, c0, c1, "a")
             nc.scalar.activation(out=hs[b][:, c0:c1], in_=acc[:, 0 : c1 - c0], func=ACT.Abs)
 
         def negate_gain(half):
             nc.scalar.activation(out=gain[:, halves[half]], in_=gain[:, halves[half]], func=ACT.Copy, scale=-1.0)
 
         def fill_cells(b, c0, c1):
-            window = pages[b % 3][:].indirect(idx2[:, c0 // 16 : c1 // 16])
+            window = pages[b % 2][:].indirect(idx2[:, c0 // 16 : c1 // 16])
             nc.vector.tensor_tensor(window, hs[b][:, c0:c1], gain[:, c0:c1], MULT)
 
         round_wa(0, 0)
         quantize_wa(0)
         nc.vector.tensor_copy(v_codes[1][:, halves[1]], tab[1][:].indirect(idx[:, list_halves[1]]))
         pages.append(keep.tile([P, T2], F32, name="page1", tag="tab1"))
-        nc.gpsimd.memset(pages[1][:], 0.0)
+        nc.vector.memset(pages[1][:], 0.0)
         negate_gain(0)
         features(0, 0, BANK)
         round_wa(1, 0)
@@ -191,8 +200,6 @@ def tile_list_rework_bay_scores_kernel(
         fill_cells(0, BANK, S)
         round_wa(2, 0)
         round_wa(2, 1)
-        pages.append(keep.tile([P, T2], F32, name="page2", tag="wa_raw2"))
-        nc.gpsimd.memset(pages[2][:], 0.0)
         features(1, 0, BANK)
         features(1, BANK, S)
         fill_cells(1, 0, BANK)
@@ -202,7 +209,7 @@ def tile_list_rework_bay_scores_kernel(
         z_t = [keep.tile([P, 4, 2, P, 2], BF16, name="z_t%d" % c) for c in range(CHUNKS)]
 
         def open_turned(b, c, tag="b"):
-            bank = psum.tile([P, 4, P], F32, name="turned", tag=tag, bufs=4)
+            bank = take_bank(tag, [P, 4, P])
             for s in range(4):
                 cols = slice(c * BANK + s * P, c * BANK + (s + 1) * P)
                 nc.tensor.matmul(bank[:, s, :], tols[b][:, cols], ident[:], start=(s == 0), stop=False, is_transpose=True)
@@ -211,7 +218,7 @@ def tile_list_rework_bay_scores_kernel(
         def close_turned(b, c, bank, copy):
             for s in range(4):
                 cols = slice(c * BANK + s * P, c * BANK + (s + 1) * P)
-                nc.tensor.matmul(bank[:, s, :], pages[b % 3][:, cols], ident[:], start=False, stop=(s == 3), is_transpose=True)
+                nc.tensor.matmul(bank[:, s, :], pages[b % 2][:, cols], ident[:], start=False, stop=(s == 3), is_transpose=True)
             copy(
                 out=z_t[c][:, :, :, 32 * b : 32 * (b + 1), :],
                 in_=bank[:].rearrange("t s (p u e) -> t s u p e", u=2, e=2),
@@ -227,33 +234,36 @@ def tile_list_rework_bay_scores_kernel(
         last = ROW_BLOCKS - 1
         features(2, 0, BANK)
         features(2, BANK, S)
-        features(last, 0, BANK)
-        features(last, BANK, TAIL)
         for c in range(CHUNKS):
             close_turned(0, c, open_turned(0, c), nc.scalar.copy)
+        features(last, 0, BANK)
+        features(last, BANK, TAIL)
+        tail_acc = differences(last, TAIL, S, "c")
         fill_cells(2, 0, S)
         weigh(0)
         for c in range(CHUNKS):
             close_turned(1, c, open_turned(1, c), nc.scalar.copy)
         fill_cells(last, 0, TAIL)
         weigh(1)
-        banks = [open_turned(last, c, "a") for c in range(CHUNKS)]
+        banks = [open_turned(2, c, "a") for c in range(CHUNKS)]
         for c in range(CHUNKS):
-            close_turned(2, c, open_turned(2, c), nc.scalar.copy)
-        features(last, TAIL, S, "b")
-        fill_cells(last, TAIL, S)
-        bays = [ring.tile([P, T2], F32, name="bays%d" % i, tag="rows", bufs=4) for i in range(2)]
+            close_turned(2, c, banks[c], nc.scalar.copy)
+        banks = [open_turned(last, c, "a" if c == CHUNKS - 1 else "b") for c in range(CHUNKS)]
+        h_tail = keep.tile([P, S - TAIL], F32, name="h_tail", tag="page0")
+        nc.scalar.activation(out=h_tail[:], in_=tail_acc[:, 0 : S - TAIL], func=ACT.Abs)
+        nc.vector.tensor_tensor(pages[1][:].indirect(idx2[:, TAIL // 16 : S // 16]), h_tail[:], gain[:, TAIL:S], MULT)
+        bays = [keep.tile([P, T2], F32, name="bays_" + tag, tag=tag) for tag in ("page0", "gain")]
         for page in bays:
-            nc.gpsimd.memset(page[:], 0.0)
+            nc.vector.memset(page[:], 0.0)
 
-        z_bf = [keep.tile([P, 4 * BANK], BF16, name="z_bf%d" % c, align_bytes=64) for c in range(CHUNKS)]
+        z_bf = [keep.tile([P, 4 * BANK], BF16, name="z_bf%d" % c, tag="z_bf%d" % c, align_bytes=64) for c in range(CHUNKS)]
         z_codes = [keep.tile([P, BANK], U32, name="z_codes%d" % c, align_bytes=64) for c in range(CHUNKS)]
         z_plane = [keep.tile([P, BANK], U8, name="z_plane%d" % c, align_bytes=64) for c in range(CHUNKS)]
 
         def turn_back(c):
             words = z_t[c][:].rearrange("t s u p e -> t (s u p e)").bitcast(F32)
-            for half, copy in enumerate((nc.scalar.copy, nc.vector.tensor_copy)):
-                bank = psum.tile([P, 2, 2 * P], F32, name="turned", tag="b", bufs=4)
+            for half, copy in enumerate((nc.scalar.copy, nc.vector.tensor_copy if c == 0 else nc.scalar.copy)):
+                bank = take_bank("aaacbbba"[2 * c + half], [P, 2, 2 * P])
                 for s in range(2):
                     for u in range(2):
                         w0 = ((2 * half + s) * 2 + u) * P
@@ -265,7 +275,7 @@ def tile_list_rework_bay_scores_kernel(
             nc.vector.quantize_mx(out=z_codes[c][:].bitcast(E4M3), scales=z_plane[c][:], in_=z_bf[c][:])
 
         def score(n, c, y, copy):
-            acc = psum.tile([P, BANK], F32, name="acc", tag="a", bufs=4)
+            acc = take_bank("a", [P, BANK])
             nc.tensor.matmul_mx(
                 out=acc[:],
                 lhsT=wo_codes[:, n * P : (n + 1) * P].bitcast(E4M3),
@@ -279,22 +289,25 @@ def tile_list_rework_bay_scores_kernel(
 
         ys = [ring.tile([P, T2], F32, name="y", tag="y")]
         close_turned(last, 0, banks[0], nc.scalar.copy)
-        close_turned(last, 1, banks[1], nc.vector.tensor_copy)
+        close_turned(last, 1, banks[1], nc.scalar.copy)
         turn_back(0)
         close_turned(last, 2, banks[2], nc.scalar.copy)
         close_turned(last, 3, banks[3], nc.scalar.copy)
         turn_back(1)
-        score(0, 0, ys[0], nc.scalar.copy)
         turn_back(2)
-        score(0, 1, ys[0], nc.scalar.copy)
         turn_back(3)
+        score(0, 0, ys[0], nc.scalar.copy)
+        score(0, 1, ys[0], nc.scalar.copy)
         score(0, 2, ys[0], nc.scalar.copy)
         score(0, 3, ys[0], nc.vector.tensor_copy)
 
         picked = []
 
         def products(n):
-            y = ring.tile([P, T2], F32, name="y", tag="y")
+            if n == 1:
+                y = keep.tile([P, T2], F32, name="y1", tag="z_bf3", align_bytes=64)
+            else:
+                y = ring.tile([P, T2], F32, name="y", tag="y")
             for c in range(CHUNKS):
                 score(n, c, y, nc.scalar.copy)
             ys.append(y)

@@ -24,6 +24,7 @@ ROW_BLOCKS = H // P
 OUT_BLOCKS = N // P
 CHUNKS = T2 // BANK
 TAIL = 768
+WARM_PASSES = 3
 BANKS = {"a": 4, "b": 3, "c": 1}
 
 
@@ -189,7 +190,7 @@ def tile_list_rework_bay_scores_kernel(
         quantize_wa(0)
         nc.vector.tensor_copy(v_codes[1][:, halves[1]], tab[1][:].indirect(idx[:, list_halves[1]]))
         pages.append(keep.tile([P, T2], F32, name="page1", tag="tab1"))
-        nc.vector.memset(pages[1][:], 0.0)
+        nc.gpsimd.memset(pages[1][:], 0.0)
         negate_gain(0)
         features(0, 0, BANK)
         round_wa(1, 0)
@@ -252,54 +253,64 @@ def tile_list_rework_bay_scores_kernel(
         h_tail = keep.tile([P, S - TAIL], F32, name="h_tail", tag="page0")
         nc.scalar.activation(out=h_tail[:], in_=tail_acc[:, 0 : S - TAIL], func=ACT.Abs)
         nc.vector.tensor_tensor(pages[1][:].indirect(idx2[:, TAIL // 16 : S // 16]), h_tail[:], gain[:, TAIL:S], MULT)
-        bays = [keep.tile([P, T2], F32, name="bays_" + tag, tag=tag) for tag in ("page0", "gain")]
+        bays = [ring.tile([P, T2], F32, name="bays%d" % i, tag="rows", bufs=4) for i in range(2)]
         for page in bays:
-            nc.vector.memset(page[:], 0.0)
+            nc.gpsimd.memset(page[:], 0.0)
 
         z_bf = [keep.tile([P, 4 * BANK], BF16, name="z_bf%d" % c, tag="z_bf%d" % c, align_bytes=64) for c in range(CHUNKS)]
         z_codes = [keep.tile([P, BANK], U32, name="z_codes%d" % c, align_bytes=64) for c in range(CHUNKS)]
         z_plane = [keep.tile([P, BANK], U8, name="z_plane%d" % c, align_bytes=64) for c in range(CHUNKS)]
 
-        def turn_back(c):
+        def turn_back(c, half, copy):
             words = z_t[c][:].rearrange("t s u p e -> t (s u p e)").bitcast(F32)
-            for half, copy in enumerate((nc.scalar.copy, nc.vector.tensor_copy if c == 0 else nc.scalar.copy)):
-                bank = take_bank("aaacbbba"[2 * c + half], [P, 2, 2 * P])
-                for s in range(2):
-                    for u in range(2):
-                        w0 = ((2 * half + s) * 2 + u) * P
-                        nc.tensor.transpose(bank[:, u, s * P : (s + 1) * P], words[:, w0 : w0 + P], ident[:])
-                copy(
-                    out=z_bf[c][:].bitcast(F32)[:, half * BANK : (half + 1) * BANK].rearrange("p (t u) -> p t u", u=2),
-                    in_=bank[:].rearrange("p u t -> p t u"),
-                )
-            nc.vector.quantize_mx(out=z_codes[c][:].bitcast(E4M3), scales=z_plane[c][:], in_=z_bf[c][:])
+            bank = take_bank("aaacbbba"[2 * c + half], [P, 2, 2 * P])
+            for s in range(2):
+                for u in range(2):
+                    w0 = ((2 * half + s) * 2 + u) * P
+                    nc.tensor.transpose(bank[:, u, s * P : (s + 1) * P], words[:, w0 : w0 + P], ident[:])
+            copy(
+                out=z_bf[c][:].bitcast(F32)[:, half * BANK : (half + 1) * BANK].rearrange("p (t u) -> p t u", u=2),
+                in_=bank[:].rearrange("p u t -> p t u"),
+            )
 
-        def score(n, c, y, copy):
+        def quantize_z(c, c0, c1):
+            nc.vector.quantize_mx(
+                out=z_codes[c][:, c0:c1].bitcast(E4M3), scales=z_plane[c][:, c0:c1], in_=z_bf[c][:, 4 * c0 : 4 * c1]
+            )
+
+        def score(n, c, c0, c1, y, copy):
             acc = take_bank("a", [P, BANK])
             nc.tensor.matmul_mx(
-                out=acc[:],
+                out=acc[:, 0 : c1 - c0],
                 lhsT=wo_codes[:, n * P : (n + 1) * P].bitcast(E4M3),
                 lhsT_scale=wo_plane[:, n * P : (n + 1) * P],
-                rhs=z_codes[c][:].bitcast(E4M3),
-                rhs_scale=z_plane[c][:],
+                rhs=z_codes[c][:, c0:c1].bitcast(E4M3),
+                rhs_scale=z_plane[c][:, c0:c1],
                 start=True,
                 stop=True,
             )
-            copy(out=y[:, c * BANK : (c + 1) * BANK], in_=acc[:])
+            copy(out=y[:, c * BANK + c0 : c * BANK + c1], in_=acc[:, 0 : c1 - c0])
 
+        idle = take_bank("c", [P, BANK])
+        for i in range(WARM_PASSES):
+            nc.tensor.matmul_mx(
+                out=idle[:],
+                lhsT=wa_codes[0][:, 0:P].bitcast(E4M3),
+                lhsT_scale=wa_plane[0][:, 0:P],
+                rhs=v_codes[0][:, 0:BANK].bitcast(E4M3),
+                rhs_scale=v_plane[:, 0:BANK],
+                start=True,
+                stop=True,
+            )
         ys = [ring.tile([P, T2], F32, name="y", tag="y")]
-        close_turned(last, 0, banks[0], nc.scalar.copy)
-        close_turned(last, 1, banks[1], nc.scalar.copy)
-        turn_back(0)
-        close_turned(last, 2, banks[2], nc.scalar.copy)
-        close_turned(last, 3, banks[3], nc.scalar.copy)
-        turn_back(1)
-        turn_back(2)
-        turn_back(3)
-        score(0, 0, ys[0], nc.scalar.copy)
-        score(0, 1, ys[0], nc.scalar.copy)
-        score(0, 2, ys[0], nc.scalar.copy)
-        score(0, 3, ys[0], nc.vector.tensor_copy)
+        for c in range(CHUNKS):
+            close_turned(last, c, banks[c], nc.vector.tensor_copy if c % 2 == 1 else nc.scalar.copy)
+        for c in range(CHUNKS):
+            turn_back(c, 0, nc.scalar.copy)
+            turn_back(c, 1, nc.vector.tensor_copy if c % 2 == 0 else nc.scalar.copy)
+            quantize_z(c, 0, BANK)
+        for c in range(CHUNKS):
+            score(0, c, 0, BANK, ys[0], nc.vector.tensor_copy if c == CHUNKS - 1 else nc.scalar.copy)
 
         picked = []
 
@@ -309,18 +320,22 @@ def tile_list_rework_bay_scores_kernel(
             else:
                 y = ring.tile([P, T2], F32, name="y", tag="y")
             for c in range(CHUNKS):
-                score(n, c, y, nc.scalar.copy)
+                score(n, c, 0, BANK, y, nc.scalar.copy)
             ys.append(y)
 
-        def pick(n):
+        def pick(n, pieces=1):
             x = ring.tile([P, PICK], F32, name="x", tag="x")
-            nc.vector.tensor_copy(x[:], ys[n][:].indirect(idx3[:]))
+            width = PICK // pieces
+            for m0 in range(0, PICK, width):
+                nc.vector.tensor_copy(x[:, m0 : m0 + width], ys[n][:].indirect(idx3[:, m0 // 16 : (m0 + width) // 16]))
             picked.append(x)
 
-        def bell(n):
-            x = picked[n]
-            nc.scalar.activation(out=x[:], in_=x[:], func=ACT.Square)
-            nc.scalar.activation(out=x[:], in_=x[:], func=ACT.Exp, scale=-0.4)
+        def bell(n, pieces=1):
+            width = PICK // pieces
+            for m0 in range(0, PICK, width):
+                x = picked[n][:, m0 : m0 + width]
+                nc.scalar.activation(out=x, in_=x, func=ACT.Square)
+                nc.scalar.activation(out=x, in_=x, func=ACT.Exp, scale=-0.4)
 
         def place(n):
             page = bays[n % 2]
@@ -328,8 +343,8 @@ def tile_list_rework_bay_scores_kernel(
             nc.sync.dma_start(out=out[n * P : (n + 1) * P, :], in_=page[:])
 
         products(1)
-        pick(0)
-        bell(0)
+        pick(0, 2)
+        bell(0, 2)
         for n in range(OUT_BLOCKS):
             if n + 2 < OUT_BLOCKS:
                 products(n + 2)

@@ -24,8 +24,10 @@ ROW_BLOCKS = H // P
 OUT_BLOCKS = N // P
 CHUNKS = T2 // BANK
 TAIL = 768
-WARM_PASSES = 3
-BANKS = {"a": 4, "b": 3, "c": 1}
+FIRST, SECOND = 256, 640
+LEAD = 384
+HALF = P // 2
+WIDE = T2 // 2
 
 
 def tile_list_rework_bay_scores_kernel(
@@ -44,66 +46,80 @@ def tile_list_rework_bay_scores_kernel(
         idx3 = lists.tile([P, PICK // 16], U16, name="idx3")
         idx4 = lists.tile([P, PICK // 16], U16, name="idx4")
 
-        tab_plane = keep.tile([P, T], U8, name="tab_plane", align_bytes=64)
+        tab_plane = keep.tile([P, T], U8, name="tab_plane", tag="first", align_bytes=64)
         wb_plane = keep.tile([P, PASSES, H], U8, name="wb_plane", align_bytes=64)
         wo_plane = keep.tile([P, N], U8, name="wo_plane", align_bytes=64)
         v_plane = keep.tile([P, S], U8, name="v_plane", align_bytes=64)
         v_plane1 = keep.tile([P, S], U8, name="v_plane1", align_bytes=64)
-        pages = [keep.tile([P, T2], F32, name="page0", tag="page0")]
-        warm = keep.tile([P, 2], F32, name="warm")
-        nc.vector.memset(warm[:, 0:1], 0.0)
-        nc.scalar.activation(out=warm[:, 1:2], in_=warm[:, 0:1], func=ACT.Exp)
-        for plane in (tab_plane[:], wb_plane[:], v_plane1[:], wo_plane[:]):
+        pad_codes = keep.tile([P, 4, P], U32, name="pad_codes", align_bytes=64)
+        pad_plane = keep.tile([P, P], U8, name="pad_plane", align_bytes=64)
+        z_plane = [keep.tile([P, WIDE], U8, name="z_plane%d" % h, align_bytes=64) for h in range(2)]
+        nc.gpsimd.memset(tab_plane[:].bitcast(I32), 0)
+        for plane in (wb_plane[:], v_plane1[:], wo_plane[:], pad_codes[:], pad_plane[:], z_plane[0][:], z_plane[1][:]):
             nc.vector.memset(plane.bitcast(I32), 0)
-        nc.vector.memset(pages[0][:], 0.0)
-        ident = keep.tile([P, P], F32, name="ident")
-        nc.vector.memset(ident[:], 0.0)
-        make_identity(nc, ident[:], nomemset=True)
+        warm = keep.tile([P, 2], F32, name="warm", tag="page0", align_bytes=64)
+        nc.vector.memset(warm[:, 0:1], 0.0)
 
-        nc.sync.dma_start(idx[:], offs)
-        nc.sync.dma_start(idx2[:], offs2)
-        for q in range(4):
-            nc.sync.dma_start(
-                out=tab_plane[32 * q : 32 * q + 8, :].bitcast(I32),
-                in_=tab_scales[:, 4 * q : 4 * q + 4, :].bitcast(I32),
-            )
         tab = [keep.tile([P, T], U32, name="tab%d" % a, tag="tab%d" % a) for a in range(PASSES)]
         wa_rows = wa.rearrange("(a p j) c -> a p j c", a=PASSES, j=4)
-        wa_raw = [keep.tile([P, PASSES, 4, w], F32, name="wa_raw%d" % i, tag="wa_raw%d" % i) for i, w in enumerate((P, P, 2 * P))]
+        wa_raw = [keep.tile([P, PASSES, 4, P], F32, name="wa_raw%d" % b, tag="wa_raw%d" % b, align_bytes=64) for b in range(ROW_BLOCKS)]
+        wb_codes = [keep.tile([P, PASSES, 2 * w], U8, name="wb_codes%d" % i, align_bytes=64) for i, w in enumerate((P, H - P))]
+        wb_rows = wb_words.rearrange("a p n -> p a n")
+        gain = keep.tile([P, S], F32, name="gain", tag="gain")
+        tols = [ring.tile([P, T2], F32, name="tol%d" % b, tag="rows", bufs=4) for b in range(ROW_BLOCKS)]
 
         def load_tab(a):
             nc.sync.dma_start(out=tab[a][:].bitcast(I32), in_=tab_words[a].rearrange("p t i -> p (t i)").bitcast(I32))
 
-        def load_wa(i, c0, c1):
+        def load_wa(b):
             for a in range(PASSES):
-                nc.sync.dma_start(out=wa_raw[i][:, a, :, :], in_=wa_rows[a][:, :, c0:c1])
+                nc.sync.dma_start(out=wa_raw[b][:, a, :, :], in_=wa_rows[a][:, :, b * P : (b + 1) * P])
 
+        def load_tol(b):
+            nc.sync.dma_start(out=tols[b][:], in_=tol[b * P : (b + 1) * P, :])
+
+        nc.sync.dma_start(idx[:], offs)
+        nc.sync.dma_start(idx2[:], offs2)
+        nc.sync.dma_start(out=tab_plane[8:24, :].bitcast(I32), in_=tab_scales[1].bitcast(I32))
+        for q in range(4):
+            nc.sync.dma_start(
+                out=tab_plane[32 * q : 32 * q + 4, :].bitcast(I32),
+                in_=tab_scales[0, 4 * q : 4 * q + 4, :].bitcast(I32),
+            )
         load_tab(0)
+        nc.scalar.activation(out=warm[:, 1:2], in_=warm[:, 0:1], func=ACT.Exp)
         for q in range(4):
             nc.gpsimd.dma_start(
                 out=wb_plane[32 * q : 32 * q + 4, :, :].bitcast(I32),
                 in_=wb_scales[:, 4 * q : 4 * q + 4, :].rearrange("a r c -> r a c").bitcast(I32),
             )
-        load_wa(0, 0, P)
+        ident = keep.tile([P, P], F32, name="ident")
+        make_identity(nc, ident[:])
+        pages = [keep.tile([P, T2], F32, name="page0", tag="page0", align_bytes=64)]
+        nc.gpsimd.memset(pages[0][:], 0.0)
+        load_wa(0)
+        nc.sync.dma_start(out=wb_codes[0][:].bitcast(I32), in_=wb_rows[:, :, 0 : 2 * P].bitcast(I32))
         load_tab(1)
-        wb_codes = keep.tile([P, PASSES, 2 * H], U8, name="wb_codes", align_bytes=64)
-        nc.sync.dma_start(out=wb_codes[:].bitcast(I32), in_=wb_words.rearrange("a p n -> p a n").bitcast(I32))
-        gain = keep.tile([P, S], F32, name="gain", tag="gain")
-        nc.sync.dma_start(out=gain[:, 0:BANK], in_=wgs[:, 0:BANK])
-        load_wa(1, P, 2 * P)
-        nc.sync.dma_start(out=gain[:, BANK:S], in_=wgs[:, BANK:S])
-        load_wa(2, 2 * P, 4 * P)
-        tols = []
-        for b in range(ROW_BLOCKS):
-            tols.append(ring.tile([P, T2], F32, name="tol%d" % b, tag="rows", bufs=4))
-        for b in range(3):
-            nc.sync.dma_start(out=tols[b][:], in_=tol[b * P : (b + 1) * P, :])
+        nc.vector.tensor_copy(v_plane[:], tab_plane[:].indirect(idx[:]))
+        for q in range(4):
+            nc.scalar.dma_start(
+                out=v_plane1[32 * q : 32 * q + 4, :].bitcast(I32), in_=v_plane[8 + 4 * q : 12 + 4 * q, :].bitcast(I32)
+            )
+        nc.sync.dma_start(out=gain[:, 0:FIRST], in_=wgs[:, 0:FIRST])
+        nc.sync.dma_start(out=gain[:, FIRST:S], in_=wgs[:, FIRST:S])
+        load_wa(1)
+        nc.sync.dma_start(out=wb_codes[1][:].bitcast(I32), in_=wb_rows[:, :, 2 * P : 2 * H].bitcast(I32))
+        load_wa(2)
+        load_tol(0)
+        load_wa(3)
+        load_tol(1)
+        load_tol(2)
         wgo_sb = keep.tile([P, PICK], F32, name="wgo_sb")
         nc.sync.dma_start(out=wgo_sb[:], in_=wgo)
         bay_sb = keep.tile([P, OUT_BLOCKS], F32, name="bay_sb")
         with nc.allow_non_contiguous_dma(reason="one value of bay for each partition"):
             nc.sync.dma_start(out=bay_sb[:], in_=bay.rearrange("(n p) -> p n", p=P))
-        nc.sync.dma_start(out=tols[3][:], in_=tol[3 * P : 4 * P, :])
+        load_tol(3)
         wo_codes = keep.tile([P, N], U32, name="wo_codes", align_bytes=64)
         nc.sync.dma_start(out=wo_codes[:].bitcast(I32), in_=wo_words[0].rearrange("p c i -> p (c i)").bitcast(I32))
         for q in range(4):
@@ -111,106 +127,123 @@ def tile_list_rework_bay_scores_kernel(
                 out=wo_plane[32 * q : 32 * q + 4, :].bitcast(I32),
                 in_=wo_scales[0, 4 * q : 4 * q + 4, :].bitcast(I32),
             )
+        wo_first = wo_words[0].rearrange("(h p) c i -> p h (c i)", h=2)[:, :, 0 : 4 * P].bitcast(I32)
+        for g in range(2):
+            nc.sync.dma_start(out=pad_codes[g * HALF : (g + 1) * HALF, g:4:2, :].bitcast(I32), in_=wo_first)
+        for q in range(4):
+            r0 = 4 * ((q + 2) % 4)
+            nc.sync.dma_start(out=pad_plane[32 * q : 32 * q + 4, :].bitcast(I32), in_=wo_scales[0, r0 : r0 + 4, 0:P].bitcast(I32))
         nc.sync.dma_start(idx3[:], offs3)
         nc.sync.dma_start(idx4[:], offs4)
 
-        v_codes = [keep.tile([P, S], U32, name="v_codes%d" % a, align_bytes=64) for a in range(PASSES)]
-        halves = [slice(0, BANK), slice(BANK, S)]
-        list_halves = [slice(0, BANK // 16), slice(BANK // 16, S // 16)]
-        nc.vector.tensor_copy(v_plane[:], tab_plane[:].indirect(idx[:]))
-        for q in range(4):
-            nc.scalar.dma_start(
-                out=v_plane1[32 * q : 32 * q + 4, :].bitcast(I32), in_=v_plane[32 * q + 4 : 32 * q + 8, :].bitcast(I32)
-            )
-        nc.vector.tensor_copy(v_codes[0][:], tab[0][:].indirect(idx[:]))
-        nc.vector.tensor_copy(v_codes[1][:, halves[0]], tab[1][:].indirect(idx[:, list_halves[0]]))
+        v_codes = [keep.tile([P, S], U32, name="v_codes0", tag="first", align_bytes=64)]
+        v_planes = (v_plane, v_plane1)
 
-        wa_bf = [keep.tile([P, w * PASSES * 4], BF16, name="wa_bf%d" % i, align_bytes=64) for i, w in enumerate((P, P, 2 * P))]
-        wa_codes = [keep.tile([P, w * PASSES], U32, name="wa_codes%d" % i, align_bytes=64) for i, w in enumerate((P, P, 2 * P))]
-        wa_plane = [keep.tile([P, w * PASSES], U8, name="wa_plane%d" % i, align_bytes=64) for i, w in enumerate((P, P, 2 * P))]
+        def entries(c0, c1):
+            return slice(c0 // 16, c1 // 16)
 
-        def round_wa(i, part):
-            width = PASSES * P * 4
+        wa_bf = [keep.tile([P, P * PASSES * 4], BF16, name="wa_bf%d" % b, align_bytes=64) for b in range(ROW_BLOCKS)]
+        wa_codes = [keep.tile([P, P * PASSES], U32, name="wa_codes%d" % b, align_bytes=64) for b in range(ROW_BLOCKS)]
+        wa_plane = [keep.tile([P, P * PASSES], U8, name="wa_plane%d" % b, align_bytes=64) for b in range(ROW_BLOCKS)]
+
+        def round_wa(b):
             nc.scalar.activation(
-                out=wa_bf[i][:, part * width : (part + 1) * width].rearrange("p (a c j) -> p a c j", a=PASSES, j=4),
-                in_=wa_raw[i][:, :, :, part * P : (part + 1) * P].rearrange("p a j c -> p a c j"),
+                out=wa_bf[b][:].rearrange("p (a c j) -> p a c j", a=PASSES, j=4),
+                in_=wa_raw[b][:].rearrange("p a j c -> p a c j"),
                 func=ACT.Copy,
                 scale=-1.0,
             )
 
-        def quantize_wa(i):
-            nc.vector.quantize_mx(out=wa_codes[i][:].bitcast(E4M3), scales=wa_plane[i][:], in_=wa_bf[i][:])
-
-        hs = [keep.tile([P, S], F32, name="h%d" % b) for b in range(ROW_BLOCKS)]
+        def quantize_wa(b):
+            nc.vector.quantize_mx(out=wa_codes[b][:].bitcast(E4M3), scales=wa_plane[b][:], in_=wa_bf[b][:])
 
         def take_bank(tag, shape):
-            return psum.tile(shape, F32, name="bank_" + tag, tag=tag, bufs=BANKS[tag])
+            return psum.tile(shape, F32, name="bank_" + tag, tag=tag, bufs=4)
 
         def differences(b, c0, c1, tag):
-            i, part = min(b, 2), max(b - 2, 0)
             acc = take_bank(tag, [P, BANK])
             step = BANK if c1 - c0 == BANK else P
-            for g0 in range(c0, c1, step):
+            pairs = [(is_wa, a) for is_wa in (False, True) for a in range(PASSES)]
+            if b == 0:
+                pairs = sorted(pairs, key=lambda pair: pair[1])
+            passes = [(is_wa, a, g0) for is_wa, a in pairs for g0 in range(c0, c1, step)]
+            wb_tile, wb_col = (wb_codes[0], 0) if b == 0 else (wb_codes[1], (b - 1) * P)
+            for k, (is_wa, a, g0) in enumerate(passes):
                 cols = slice(g0, g0 + step)
-                group = acc[:, g0 - c0 : g0 - c0 + step]
-                for a in range(PASSES):
-                    w_cols = slice((part * PASSES + a) * P, (part * PASSES + a + 1) * P)
-                    nc.tensor.matmul_mx(
-                        out=group,
-                        lhsT=wa_codes[i][:, w_cols].bitcast(E4M3),
-                        lhsT_scale=wa_plane[i][:, w_cols],
-                        rhs=v_codes[a][:, cols].bitcast(E4M3),
-                        rhs_scale=v_plane[4 * a : P, cols],
-                        start=(a == 0),
-                        stop=False,
-                    )
-                    nc.tensor.matmul_mx(
-                        out=group,
-                        lhsT=wb_codes[:, a, 2 * b * P : 2 * (b + 1) * P].bitcast(E2M1),
-                        lhsT_scale=wb_plane[:, a, b * P : (b + 1) * P],
-                        rhs=v_codes[a][:, cols].bitcast(E4M3),
-                        rhs_scale=(v_plane, v_plane1)[a][:, cols],
-                        start=False,
-                        stop=(a == PASSES - 1),
-                    )
+                if is_wa:
+                    codes = wa_codes[b][:, a * P : (a + 1) * P].bitcast(E4M3)
+                    scale = wa_plane[b][:, a * P : (a + 1) * P]
+                else:
+                    codes = wb_tile[:, a, 2 * wb_col : 2 * (wb_col + P)].bitcast(E2M1)
+                    scale = wb_plane[:, a, b * P : (b + 1) * P]
+                nc.tensor.matmul_mx(
+                    out=acc[:, g0 - c0 : g0 - c0 + step],
+                    lhsT=codes,
+                    lhsT_scale=scale,
+                    rhs=v_codes[a][:, cols].bitcast(E4M3),
+                    rhs_scale=v_planes[a][:, cols],
+                    start=(k == 0),
+                    stop=(k == len(passes) - 1),
+                )
             return acc
 
-        def features(b, c0, c1):
+        def features(b, c0, c1, h, h0):
             acc = differences(b, c0, c1, "a")
-            nc.scalar.activation(out=hs[b][:, c0:c1], in_=acc[:, 0 : c1 - c0], func=ACT.Abs)
+            nc.scalar.activation(out=h[:, c0 - h0 : c1 - h0], in_=acc[:, 0 : c1 - c0], func=ACT.Abs)
 
-        def negate_gain(half):
-            nc.scalar.activation(out=gain[:, halves[half]], in_=gain[:, halves[half]], func=ACT.Copy, scale=-1.0)
+        def negate_gain(c0, c1):
+            nc.scalar.activation(out=gain[:, c0:c1], in_=gain[:, c0:c1], func=ACT.Copy, scale=-1.0)
 
-        def fill_cells(b, c0, c1):
-            window = pages[b % 2][:].indirect(idx2[:, c0 // 16 : c1 // 16])
-            nc.vector.tensor_tensor(window, hs[b][:, c0:c1], gain[:, c0:c1], MULT)
+        def fill_cells(b, c0, c1, h, h0):
+            window = pages[b % 2][:].indirect(idx2[:, entries(c0, c1)])
+            nc.vector.tensor_tensor(window, h[:, c0 - h0 : c1 - h0], gain[:, c0:c1], MULT)
 
-        round_wa(0, 0)
+        def features_tile(name, width, tag):
+            return keep.tile([P, width], F32, name=name, tag=tag, align_bytes=64)
+
+        cuts = (0, FIRST, SECOND, S)
+
+        def gather_words(a):
+            for c0, c1 in zip(cuts, cuts[1:]):
+                nc.vector.tensor_copy(v_codes[a][:, c0:c1], tab[a][:].indirect(idx[:, entries(c0, c1)]))
+
+        gather_words(0)
+        round_wa(0)
         quantize_wa(0)
-        nc.vector.tensor_copy(v_codes[1][:, halves[1]], tab[1][:].indirect(idx[:, list_halves[1]]))
+        v_codes.append(keep.tile([P, S], U32, name="v_codes1", tag="wa_bf0", align_bytes=64))
+        gather_words(1)
+        negate_gain(0, FIRST)
         pages.append(keep.tile([P, T2], F32, name="page1", tag="tab1"))
         nc.gpsimd.memset(pages[1][:], 0.0)
-        negate_gain(0)
-        features(0, 0, BANK)
-        round_wa(1, 0)
-        negate_gain(1)
-        features(0, BANK, S)
-        fill_cells(0, 0, BANK)
+        h_head = features_tile("h0_head", SECOND, "h_even")
+        features(0, 0, FIRST, h_head, 0)
+        fill_cells(0, 0, FIRST, h_head, 0)
+        features(0, FIRST, SECOND, h_head, 0)
+        negate_gain(FIRST, S)
+        fill_cells(0, FIRST, SECOND, h_head, 0)
+        round_wa(1)
         quantize_wa(1)
-        fill_cells(0, BANK, S)
-        round_wa(2, 0)
-        round_wa(2, 1)
-        features(1, 0, BANK)
-        features(1, BANK, S)
-        fill_cells(1, 0, BANK)
+        h_last = features_tile("h0_last", S - SECOND, "wa_raw1")
+        features(0, SECOND, S, h_last, SECOND)
+        fill_cells(0, SECOND, S, h_last, SECOND)
+        h_head = features_tile("h1_head", BANK, "h_odd")
+        features(1, 0, BANK, h_head, 0)
+        round_wa(2)
         quantize_wa(2)
-        fill_cells(1, BANK, S)
+        fill_cells(1, 0, BANK, h_head, 0)
+        round_wa(3)
+        quantize_wa(3)
+        h_late = features_tile("h_late", 2 * S - BANK, "wa_raw3")
+        features(1, BANK, S, h_late, BANK)
+        fill_cells(1, BANK, S, h_late, BANK)
+        h2 = h_late[:, S - BANK : 2 * S - BANK]
+        h3 = features_tile("h3", TAIL, "h_even")
 
-        z_t = [keep.tile([P, 4, 2, P, 2], BF16, name="z_t%d" % c) for c in range(CHUNKS)]
+        z_t = [[keep.tile([P, 2, 4, 2, HALF], BF16, name="z_t%d_%d" % (h, c), align_bytes=64) for c in range(CHUNKS)] for h in range(2)]
+        z_bf = [[keep.tile([P, WIDE], BF16, name="z_bf%d_%d" % (h, c), align_bytes=64) for c in range(CHUNKS)] for h in range(2)]
 
-        def open_turned(b, c, tag="b"):
-            bank = take_bank(tag, [P, 4, P])
+        def open_turned(b, c):
+            bank = take_bank("b", [P, 4, P])
             for s in range(4):
                 cols = slice(c * BANK + s * P, c * BANK + (s + 1) * P)
                 nc.tensor.matmul(bank[:, s, :], tols[b][:, cols], ident[:], start=(s == 0), stop=False, is_transpose=True)
@@ -221,136 +254,172 @@ def tile_list_rework_bay_scores_kernel(
                 cols = slice(c * BANK + s * P, c * BANK + (s + 1) * P)
                 nc.tensor.matmul(bank[:, s, :], pages[b % 2][:, cols], ident[:], start=False, stop=(s == 3), is_transpose=True)
             copy(
-                out=z_t[c][:, :, :, 32 * b : 32 * (b + 1), :],
-                in_=bank[:].rearrange("t s (p u e) -> t s u p e", u=2, e=2),
+                out=z_t[b // 2][c][:, :, :, b % 2, :].rearrange("t u s (p e) -> t u s p e", e=2),
+                in_=bank[:].rearrange("t s (p u e) -> t u s p e", u=2, e=2),
             )
+
+        def turn(b):
+            banks = [open_turned(b, c) for c in range(CHUNKS)]
+            for c in range(CHUNKS):
+                close_turned(b, c, banks[c], nc.scalar.copy)
+
+        def turn_back(h, c, copy):
+            words = z_t[h][c][:].rearrange("t u s b x -> t (u s b x)").bitcast(F32)
+            bank = take_bank("b", [P, 2, 2 * P])
+            for u in range(2):
+                for m in range(2):
+                    w0 = (2 * u + m) * P
+                    nc.tensor.transpose(bank[:, u, m * P : (m + 1) * P], words[:, w0 : w0 + P], ident[:])
+            copy(
+                out=z_bf[h][c][:].bitcast(F32).rearrange("p (t u) -> p t u", u=2),
+                in_=bank[:].rearrange("p u t -> p t u"),
+            )
+
+        z_codes = []
+
+        def quantize_z(h, c):
+            cols = slice(c * 2 * P, (c + 1) * 2 * P)
+            nc.vector.quantize_mx(out=z_codes[h][:, cols].bitcast(E4M3), scales=z_plane[h][:, cols], in_=z_bf[h][c][:])
+
+        def half_scores(h, c, acc):
+            cols = slice(c * 2 * P, (c + 1) * 2 * P)
+            for g in range(2):
+                nc.tensor.matmul_mx(
+                    out=acc[:, g, :],
+                    lhsT=pad_codes[:, 2 * h + g, :].bitcast(E4M3),
+                    lhsT_scale=wo_plane[:, 0:P] if h == g else pad_plane[:],
+                    rhs=z_codes[h][:, cols].bitcast(E4M3),
+                    rhs_scale=z_plane[h][:, cols],
+                    start=(h == 0 and g == 0),
+                    stop=(h == 1 and g == 1),
+                )
 
         weights = []
 
-        def weigh(n):
-            w = ring.tile([P, PICK], F32, name="bay_weight", tag="bay_weight", bufs=2)
-            nc.scalar.activation(out=w[:], in_=wgo_sb[:], func=ACT.Copy, scale=bay_sb[:, n : n + 1])
+        def weigh(w):
+            n = len(weights)
+            nc.scalar.activation(out=w, in_=wgo_sb[:], func=ACT.Copy, scale=bay_sb[:, n : n + 1])
             weights.append(w)
 
+        def weight_tile(tag):
+            return keep.tile([P, PICK], F32, name="weight%d" % len(weights), tag=tag, align_bytes=64)[:]
+
         last = ROW_BLOCKS - 1
-        features(2, 0, BANK)
-        features(2, BANK, S)
+        features(2, 0, BANK, h2, 0)
+        features(2, BANK, S, h2, 0)
+        turn(0)
+        fill_cells(2, 0, S, h2, 0)
+        features(last, 0, BANK, h3, 0)
+        features(last, BANK, TAIL, h3, 0)
+        tail_acc = differences(last, TAIL, S, "a")
+        turn(1)
         for c in range(CHUNKS):
-            close_turned(0, c, open_turned(0, c), nc.scalar.copy)
-        features(last, 0, BANK)
-        features(last, BANK, TAIL)
-        tail_acc = differences(last, TAIL, S, "c")
-        fill_cells(2, 0, S)
-        weigh(0)
+            turn_back(0, c, nc.scalar.copy)
+        fill_cells(last, 0, TAIL, h3, 0)
+        weigh(weight_tile("z_t0_3"))
+        turn(2)
+        banks = [open_turned(last, c) for c in range(CHUNKS)]
+        h_tail = keep.tile([P, T2], F32, name="h_tail", tag="page0", align_bytes=64)
+        nc.scalar.activation(out=h_tail[:, 0 : S - TAIL], in_=tail_acc[:, 0 : S - TAIL], func=ACT.Abs)
+        weigh(h_tail[:, PICK : 2 * PICK])
+        z_codes.append(keep.tile([P, WIDE], U32, name="z_codes0", tag="h_even", align_bytes=64))
+        z_codes.append(keep.tile([P, WIDE], U32, name="z_codes1", align_bytes=64))
+        first = [take_bank("a", [P, 2, 2 * P]) for c in range(CHUNKS)]
         for c in range(CHUNKS):
-            close_turned(1, c, open_turned(1, c), nc.scalar.copy)
-        fill_cells(last, 0, TAIL)
-        weigh(1)
-        banks = [open_turned(2, c, "a") for c in range(CHUNKS)]
-        for c in range(CHUNKS):
-            close_turned(2, c, banks[c], nc.scalar.copy)
-        banks = [open_turned(last, c, "a" if c == CHUNKS - 1 else "b") for c in range(CHUNKS)]
-        h_tail = keep.tile([P, S - TAIL], F32, name="h_tail", tag="page0")
-        nc.scalar.activation(out=h_tail[:], in_=tail_acc[:, 0 : S - TAIL], func=ACT.Abs)
-        nc.vector.tensor_tensor(pages[1][:].indirect(idx2[:, TAIL // 16 : S // 16]), h_tail[:], gain[:, TAIL:S], MULT)
+            quantize_z(0, c)
+            half_scores(0, c, first[c])
+        fill_cells(last, TAIL, S, h_tail, TAIL)
         bays = [ring.tile([P, T2], F32, name="bays%d" % i, tag="rows", bufs=4) for i in range(2)]
         for page in bays:
             nc.gpsimd.memset(page[:], 0.0)
 
-        z_bf = [keep.tile([P, 4 * BANK], BF16, name="z_bf%d" % c, tag="z_bf%d" % c, align_bytes=64) for c in range(CHUNKS)]
-        z_codes = [keep.tile([P, BANK], U32, name="z_codes%d" % c, align_bytes=64) for c in range(CHUNKS)]
-        z_plane = [keep.tile([P, BANK], U8, name="z_plane%d" % c, align_bytes=64) for c in range(CHUNKS)]
+        joined_codes = keep.tile([P, WIDE], U32, name="joined_codes", align_bytes=64)
+        joined_plane = keep.tile([P, WIDE], U8, name="joined_plane", align_bytes=64)
+        lower, upper = slice(0, HALF), slice(HALF, P)
 
-        def turn_back(c, half, copy):
-            words = z_t[c][:].rearrange("t s u p e -> t (s u p e)").bitcast(F32)
-            bank = take_bank("aaacbbba"[2 * c + half], [P, 2, 2 * P])
-            for s in range(2):
-                for u in range(2):
-                    w0 = ((2 * half + s) * 2 + u) * P
-                    nc.tensor.transpose(bank[:, u, s * P : (s + 1) * P], words[:, w0 : w0 + P], ident[:])
-            copy(
-                out=z_bf[c][:].bitcast(F32)[:, half * BANK : (half + 1) * BANK].rearrange("p (t u) -> p t u", u=2),
-                in_=bank[:].rearrange("p u t -> p t u"),
-            )
+        def move(dst, dst_rows, h, src_rows):
+            for to, of in zip(dst, (z_codes[h], z_plane[h])):
+                nc.sync.dma_start(out=to[dst_rows, :].bitcast(I32), in_=of[src_rows, :].bitcast(I32))
 
-        def quantize_z(c, c0, c1):
-            nc.vector.quantize_mx(
-                out=z_codes[c][:, c0:c1].bitcast(E4M3), scales=z_plane[c][:, c0:c1], in_=z_bf[c][:, 4 * c0 : 4 * c1]
-            )
-
-        def score(n, c, c0, c1, y, copy):
-            acc = take_bank("a", [P, BANK])
-            nc.tensor.matmul_mx(
-                out=acc[:, 0 : c1 - c0],
-                lhsT=wo_codes[:, n * P : (n + 1) * P].bitcast(E4M3),
-                lhsT_scale=wo_plane[:, n * P : (n + 1) * P],
-                rhs=z_codes[c][:, c0:c1].bitcast(E4M3),
-                rhs_scale=z_plane[c][:, c0:c1],
-                start=True,
-                stop=True,
-            )
-            copy(out=y[:, c * BANK + c0 : c * BANK + c1], in_=acc[:, 0 : c1 - c0])
-
-        idle = take_bank("c", [P, BANK])
-        for i in range(WARM_PASSES):
-            nc.tensor.matmul_mx(
-                out=idle[:],
-                lhsT=wa_codes[0][:, 0:P].bitcast(E4M3),
-                lhsT_scale=wa_plane[0][:, 0:P],
-                rhs=v_codes[0][:, 0:BANK].bitcast(E4M3),
-                rhs_scale=v_plane[:, 0:BANK],
-                start=True,
-                stop=True,
-            )
-        ys = [ring.tile([P, T2], F32, name="y", tag="y")]
+        groups = ((z_codes[0], z_plane[0]), (joined_codes, joined_plane))
+        move(groups[1], lower, 0, upper)
+        by_turns = (nc.scalar.copy, nc.vector.tensor_copy)
+        ys = [keep.tile([P, T2], F32, name="y0", tag="y0")]
         for c in range(CHUNKS):
-            close_turned(last, c, banks[c], nc.vector.tensor_copy if c % 2 == 1 else nc.scalar.copy)
+            close_turned(last, c, banks[c], by_turns[c % 2])
         for c in range(CHUNKS):
-            turn_back(c, 0, nc.scalar.copy)
-            turn_back(c, 1, nc.vector.tensor_copy if c % 2 == 0 else nc.scalar.copy)
-            quantize_z(c, 0, BANK)
+            turn_back(1, c, by_turns[c == 1])
+            quantize_z(1, c)
+            half_scores(1, c, first[c])
         for c in range(CHUNKS):
-            score(0, c, 0, BANK, ys[0], nc.vector.tensor_copy if c == CHUNKS - 1 else nc.scalar.copy)
+            by_turns[c % 2](
+                out=ys[0][:, c * BANK : (c + 1) * BANK].rearrange("p (m g t) -> p m g t", m=2, g=2),
+                in_=first[c][:].rearrange("p g (m t) -> p m g t", m=2),
+            )
+        weigh(weight_tile("z_bf1_3"))
+        move(groups[0], upper, 1, lower)
+        move(groups[1], upper, 1, upper)
 
         picked = []
+        squares = [keep.tile([P, PICK], F32, name="squares%d" % i, tag=tag) for i, tag in enumerate(("y3", "late", "squares"))]
 
         def products(n):
-            if n == 1:
-                y = keep.tile([P, T2], F32, name="y1", tag="z_bf3", align_bytes=64)
-            else:
-                y = ring.tile([P, T2], F32, name="y", tag="y")
-            for c in range(CHUNKS):
-                score(n, c, 0, BANK, y, nc.scalar.copy)
+            y = keep.tile([P, T2], F32, name="y%d" % n, tag="y%d" % (n % 4))
+            cells = y[:].rearrange("p (k g t) -> p g k t", g=2, t=P)
+            for g, (codes, plane) in enumerate(groups):
+                for j in range(2):
+                    acc = take_bank("b", [P, 4, P])
+                    nc.tensor.matmul_mx(
+                        out=acc[:].rearrange("p k t -> p (k t)"),
+                        lhsT=wo_codes[:, n * P : (n + 1) * P].bitcast(E4M3),
+                        lhsT_scale=wo_plane[:, n * P : (n + 1) * P],
+                        rhs=codes[:, j * BANK : (j + 1) * BANK].bitcast(E4M3),
+                        rhs_scale=plane[:, j * BANK : (j + 1) * BANK],
+                        start=True,
+                        stop=True,
+                    )
+                    nc.scalar.copy(out=cells[:, g, 4 * j : 4 * (j + 1), :], in_=acc[:])
             ys.append(y)
 
-        def pick(n, pieces=1):
-            x = ring.tile([P, PICK], F32, name="x", tag="x")
-            width = PICK // pieces
-            for m0 in range(0, PICK, width):
-                nc.vector.tensor_copy(x[:, m0 : m0 + width], ys[n][:].indirect(idx3[:, m0 // 16 : (m0 + width) // 16]))
-            picked.append(x)
+        def pick(n, m0, m1):
+            nc.vector.tensor_copy(picked[n][:, m0:m1], ys[n][:].indirect(idx3[:, entries(m0, m1)]))
 
-        def bell(n, pieces=1):
-            width = PICK // pieces
-            for m0 in range(0, PICK, width):
-                x = picked[n][:, m0 : m0 + width]
-                nc.scalar.activation(out=x, in_=x, func=ACT.Square)
-                nc.scalar.activation(out=x, in_=x, func=ACT.Exp, scale=-0.4)
+        def bell(n, m0, m1):
+            x = picked[n][:, m0:m1]
+            scratch = squares[(2, 0, 1)[(n < 2) + (n == 1 and m0 > 0)]][:, 0 : m1 - m0]
+            nc.scalar.activation(out=scratch, in_=x, func=ACT.Square)
+            nc.scalar.activation(out=x, in_=scratch, func=ACT.Exp, scale=-0.4)
 
-        def place(n):
-            page = bays[n % 2]
-            nc.vector.tensor_tensor(page[:].indirect(idx4[:]), picked[n][:], weights[n][:], MULT)
-            nc.sync.dma_start(out=out[n * P : (n + 1) * P, :], in_=page[:])
+        def place(n, m0, m1):
+            nc.vector.tensor_tensor(bays[n % 2][:].indirect(idx4[:, entries(m0, m1)]), picked[n][:, m0:m1], weights[n][:, m0:m1], MULT)
 
+        def store(n):
+            nc.sync.dma_start(out=out[n * P : (n + 1) * P, :], in_=bays[n % 2][:])
+
+        def pick_block(n):
+            picked.append(ring.tile([P, PICK], F32, name="x", tag="x"))
+            pieces = ((0, LEAD), (LEAD, PICK)) if n < 2 else ((0, PICK),)
+            for m0, m1 in pieces:
+                pick(n, m0, m1)
+            for m0, m1 in pieces:
+                bell(n, m0, m1)
+
+        pick_block(0)
+        place(0, 0, LEAD)
+        place(0, LEAD, PICK)
+        store(0)
         products(1)
-        pick(0, 2)
-        bell(0, 2)
-        for n in range(OUT_BLOCKS):
+        products(2)
+        pick_block(1)
+        weigh(weight_tile("z_codes1"))
+        for n in range(1, OUT_BLOCKS):
             if n + 2 < OUT_BLOCKS:
                 products(n + 2)
             if n + 1 < OUT_BLOCKS:
-                pick(n + 1)
-                bell(n + 1)
-            place(n)
-            if n + 2 < OUT_BLOCKS:
-                weigh(n + 2)
+                pick_block(n + 1)
+            place(n, 0, PICK)
+            store(n)
+            if n == 1:
+                late = keep.tile([P, 2, PICK], F32, name="late", tag="late")
+            if n + 3 < OUT_BLOCKS:
+                weigh(late[:, n - 1, :])

@@ -57,8 +57,6 @@ def tile_list_rework_bay_scores_kernel(
         nc.gpsimd.memset(tab_plane[:].bitcast(I32), 0)
         for plane in (wb_plane[:], v_plane1[:], wo_plane[:], pad_codes[:], pad_plane[:], z_plane[0][:], z_plane[1][:]):
             nc.vector.memset(plane.bitcast(I32), 0)
-        warm = keep.tile([P, 2], F32, name="warm", tag="page0", align_bytes=64)
-        nc.vector.memset(warm[:, 0:1], 0.0)
 
         tab = [keep.tile([P, T], U32, name="tab%d" % a, tag="tab%d" % a) for a in range(PASSES)]
         wa_rows = wa.rearrange("(a p j) c -> a p j c", a=PASSES, j=4)
@@ -79,15 +77,15 @@ def tile_list_rework_bay_scores_kernel(
             nc.sync.dma_start(out=tols[b][:], in_=tol[b * P : (b + 1) * P, :])
 
         nc.sync.dma_start(idx[:], offs)
-        nc.sync.dma_start(idx2[:], offs2)
-        nc.sync.dma_start(out=tab_plane[8:24, :].bitcast(I32), in_=tab_scales[1].bitcast(I32))
+        load_tab(0)
+        nc.scalar.dma_start(out=tab_plane[8:24, :].bitcast(I32), in_=tab_scales[1].bitcast(I32))
         for q in range(4):
-            nc.sync.dma_start(
+            nc.scalar.dma_start(
                 out=tab_plane[32 * q : 32 * q + 4, :].bitcast(I32),
                 in_=tab_scales[0, 4 * q : 4 * q + 4, :].bitcast(I32),
             )
-        load_tab(0)
-        nc.scalar.activation(out=warm[:, 1:2], in_=warm[:, 0:1], func=ACT.Exp)
+        nc.gpsimd.dma_start(out=gain[:, 0:FIRST], in_=wgs[:, 0:FIRST])
+        nc.gpsimd.dma_start(out=wb_codes[0][:].bitcast(I32), in_=wb_rows[:, :, 0 : 2 * P].bitcast(I32))
         for q in range(4):
             nc.gpsimd.dma_start(
                 out=wb_plane[32 * q : 32 * q + 4, :, :].bitcast(I32),
@@ -98,14 +96,13 @@ def tile_list_rework_bay_scores_kernel(
         pages = [keep.tile([P, T2], F32, name="page0", tag="page0", align_bytes=64)]
         nc.gpsimd.memset(pages[0][:], 0.0)
         load_wa(0)
-        nc.sync.dma_start(out=wb_codes[0][:].bitcast(I32), in_=wb_rows[:, :, 0 : 2 * P].bitcast(I32))
         load_tab(1)
         nc.vector.tensor_copy(v_plane[:], tab_plane[:].indirect(idx[:]))
         for q in range(4):
-            nc.scalar.dma_start(
+            nc.sync.dma_start(
                 out=v_plane1[32 * q : 32 * q + 4, :].bitcast(I32), in_=v_plane[8 + 4 * q : 12 + 4 * q, :].bitcast(I32)
             )
-        nc.sync.dma_start(out=gain[:, 0:FIRST], in_=wgs[:, 0:FIRST])
+        nc.sync.dma_start(idx2[:], offs2)
         nc.sync.dma_start(out=gain[:, FIRST:S], in_=wgs[:, FIRST:S])
         load_wa(1)
         nc.sync.dma_start(out=wb_codes[1][:].bitcast(I32), in_=wb_rows[:, :, 2 * P : 2 * H].bitcast(I32))
@@ -207,12 +204,12 @@ def tile_list_rework_bay_scores_kernel(
             for c0, c1 in zip(cuts, cuts[1:]):
                 nc.vector.tensor_copy(v_codes[a][:, c0:c1], tab[a][:].indirect(idx[:, entries(c0, c1)]))
 
+        negate_gain(0, FIRST)
         gather_words(0)
         round_wa(0)
         quantize_wa(0)
         v_codes.append(keep.tile([P, S], U32, name="v_codes1", tag="wa_bf0", align_bytes=64))
         gather_words(1)
-        negate_gain(0, FIRST)
         pages.append(keep.tile([P, T2], F32, name="page1", tag="tab1"))
         nc.gpsimd.memset(pages[1][:], 0.0)
         h_head = features_tile("h0_head", SECOND, "h_even")
@@ -356,7 +353,6 @@ def tile_list_rework_bay_scores_kernel(
                 out=ys[0][:, c * BANK : (c + 1) * BANK].rearrange("p (m g t) -> p m g t", m=2, g=2),
                 in_=first[c][:].rearrange("p g (m t) -> p m g t", m=2),
             )
-        weigh(weight_tile("z_bf1_3"))
         move(groups[0], upper, 1, lower)
         move(groups[1], upper, 1, upper)
 
@@ -411,7 +407,7 @@ def tile_list_rework_bay_scores_kernel(
         products(1)
         products(2)
         pick_block(1)
-        weigh(weight_tile("z_codes1"))
+        late = keep.tile([P, OUT_BLOCKS - 2, PICK], F32, name="late", tag="late")
         for n in range(1, OUT_BLOCKS):
             if n + 2 < OUT_BLOCKS:
                 products(n + 2)
@@ -419,7 +415,5 @@ def tile_list_rework_bay_scores_kernel(
                 pick_block(n + 1)
             place(n, 0, PICK)
             store(n)
-            if n == 1:
-                late = keep.tile([P, 2, PICK], F32, name="late", tag="late")
-            if n + 3 < OUT_BLOCKS:
+            if n + 1 < OUT_BLOCKS:
                 weigh(late[:, n - 1, :])

@@ -54,9 +54,8 @@ def tile_list_rework_bay_scores_kernel(
         pad_codes = keep.tile([P, 4, P], U32, name="pad_codes", align_bytes=64)
         pad_plane = keep.tile([P, P], U8, name="pad_plane", align_bytes=64)
         z_plane = [keep.tile([P, WIDE], U8, name="z_plane%d" % h, align_bytes=64) for h in range(2)]
-        nc.gpsimd.memset(tab_plane[:].bitcast(I32), 0)
-        for plane in (wb_plane[:], v_plane1[:], wo_plane[:], pad_codes[:], pad_plane[:], z_plane[0][:], z_plane[1][:]):
-            nc.vector.memset(plane.bitcast(I32), 0)
+        for plane in (tab_plane[:], wb_plane[:], v_plane1[:], wo_plane[:], pad_codes[:], pad_plane[:], z_plane[0][:], z_plane[1][:]):
+            nc.gpsimd.memset(plane.bitcast(I32), 0)
 
         tab = [keep.tile([P, T], U32, name="tab%d" % a, tag="tab%d" % a) for a in range(PASSES)]
         wa_rows = wa.rearrange("(a p j) c -> a p j c", a=PASSES, j=4)
@@ -64,30 +63,29 @@ def tile_list_rework_bay_scores_kernel(
         wb_codes = [keep.tile([P, PASSES, 2 * w], U8, name="wb_codes%d" % i, align_bytes=64) for i, w in enumerate((P, H - P))]
         wb_rows = wb_words.rearrange("a p n -> p a n")
         gain = keep.tile([P, S], F32, name="gain", tag="gain")
-        tols = [ring.tile([P, T2], F32, name="tol%d" % b, tag="rows", bufs=4) for b in range(ROW_BLOCKS)]
+        tols = [keep.tile([P, T2], F32, name="tol%d" % b) for b in range(ROW_BLOCKS)]
 
         def load_tab(a):
             nc.sync.dma_start(out=tab[a][:].bitcast(I32), in_=tab_words[a].rearrange("p t i -> p (t i)").bitcast(I32))
 
-        def load_wa(b):
-            for a in range(PASSES):
+        def load_wa(b, passes=range(PASSES)):
+            for a in passes:
                 nc.sync.dma_start(out=wa_raw[b][:, a, :, :], in_=wa_rows[a][:, :, b * P : (b + 1) * P])
 
         def load_tol(b):
             nc.sync.dma_start(out=tols[b][:], in_=tol[b * P : (b + 1) * P, :])
 
         nc.sync.dma_start(idx[:], offs)
-        load_tab(0)
-        nc.scalar.dma_start(out=tab_plane[8:24, :].bitcast(I32), in_=tab_scales[1].bitcast(I32))
+        load_wa(0, [0])
+        nc.sync.dma_start(out=tab_plane[8:24, :].bitcast(I32), in_=tab_scales[1].bitcast(I32))
         for q in range(4):
-            nc.scalar.dma_start(
+            nc.sync.dma_start(
                 out=tab_plane[32 * q : 32 * q + 4, :].bitcast(I32),
                 in_=tab_scales[0, 4 * q : 4 * q + 4, :].bitcast(I32),
             )
-        nc.gpsimd.dma_start(out=gain[:, 0:FIRST], in_=wgs[:, 0:FIRST])
-        nc.gpsimd.dma_start(out=wb_codes[0][:].bitcast(I32), in_=wb_rows[:, :, 0 : 2 * P].bitcast(I32))
+        load_tab(0)
         for q in range(4):
-            nc.gpsimd.dma_start(
+            nc.sync.dma_start(
                 out=wb_plane[32 * q : 32 * q + 4, :, :].bitcast(I32),
                 in_=wb_scales[:, 4 * q : 4 * q + 4, :].rearrange("a r c -> r a c").bitcast(I32),
             )
@@ -95,13 +93,15 @@ def tile_list_rework_bay_scores_kernel(
         make_identity(nc, ident[:])
         pages = [keep.tile([P, T2], F32, name="page0", tag="page0", align_bytes=64)]
         nc.gpsimd.memset(pages[0][:], 0.0)
-        load_wa(0)
+        load_wa(0, [1])
+        nc.sync.dma_start(out=wb_codes[0][:].bitcast(I32), in_=wb_rows[:, :, 0 : 2 * P].bitcast(I32))
         load_tab(1)
         nc.vector.tensor_copy(v_plane[:], tab_plane[:].indirect(idx[:]))
         for q in range(4):
             nc.sync.dma_start(
                 out=v_plane1[32 * q : 32 * q + 4, :].bitcast(I32), in_=v_plane[8 + 4 * q : 12 + 4 * q, :].bitcast(I32)
             )
+        nc.sync.dma_start(out=gain[:, 0:FIRST], in_=wgs[:, 0:FIRST])
         nc.sync.dma_start(idx2[:], offs2)
         nc.sync.dma_start(out=gain[:, FIRST:S], in_=wgs[:, FIRST:S])
         load_wa(1)
@@ -144,12 +144,14 @@ def tile_list_rework_bay_scores_kernel(
         wa_plane = [keep.tile([P, P * PASSES], U8, name="wa_plane%d" % b, align_bytes=64) for b in range(ROW_BLOCKS)]
 
         def round_wa(b):
-            nc.scalar.activation(
-                out=wa_bf[b][:].rearrange("p (a c j) -> p a c j", a=PASSES, j=4),
-                in_=wa_raw[b][:].rearrange("p a j c -> p a c j"),
-                func=ACT.Copy,
-                scale=-1.0,
-            )
+            step = 1 if b == 0 else PASSES
+            for a in range(0, PASSES, step):
+                nc.scalar.activation(
+                    out=wa_bf[b][:].rearrange("p (a c j) -> p a c j", a=PASSES, j=4)[:, a : a + step],
+                    in_=wa_raw[b][:].rearrange("p a j c -> p a c j")[:, a : a + step],
+                    func=ACT.Copy,
+                    scale=-1.0,
+                )
 
         def quantize_wa(b):
             nc.vector.quantize_mx(out=wa_codes[b][:].bitcast(E4M3), scales=wa_plane[b][:], in_=wa_bf[b][:])
@@ -204,12 +206,12 @@ def tile_list_rework_bay_scores_kernel(
             for c0, c1 in zip(cuts, cuts[1:]):
                 nc.vector.tensor_copy(v_codes[a][:, c0:c1], tab[a][:].indirect(idx[:, entries(c0, c1)]))
 
-        negate_gain(0, FIRST)
         gather_words(0)
         round_wa(0)
         quantize_wa(0)
         v_codes.append(keep.tile([P, S], U32, name="v_codes1", tag="wa_bf0", align_bytes=64))
         gather_words(1)
+        negate_gain(0, FIRST)
         pages.append(keep.tile([P, T2], F32, name="page1", tag="tab1"))
         nc.gpsimd.memset(pages[1][:], 0.0)
         h_head = features_tile("h0_head", SECOND, "h_even")
@@ -326,7 +328,7 @@ def tile_list_rework_bay_scores_kernel(
             quantize_z(0, c)
             half_scores(0, c, first[c])
         fill_cells(last, TAIL, S, h_tail, TAIL)
-        bays = [ring.tile([P, T2], F32, name="bays%d" % i, tag="rows", bufs=4) for i in range(2)]
+        bays = [keep.tile([P, T2], F32, name="bays%d" % i, tag="tol%d" % (i + 1)) for i in range(2)]
         for page in bays:
             nc.gpsimd.memset(page[:], 0.0)
 
@@ -390,7 +392,11 @@ def tile_list_rework_bay_scores_kernel(
             nc.vector.tensor_tensor(bays[n % 2][:].indirect(idx4[:, entries(m0, m1)]), picked[n][:, m0:m1], weights[n][:, m0:m1], MULT)
 
         def store(n):
-            nc.sync.dma_start(out=out[n * P : (n + 1) * P, :], in_=bays[n % 2][:])
+            if n + 1 < OUT_BLOCKS:
+                nc.sync.dma_start(out=out[n * P : (n + 1) * P, :], in_=bays[n % 2][:])
+            else:
+                for queue, cols in ((nc.sync, slice(0, WIDE)), (nc.scalar, slice(WIDE, T2))):
+                    queue.dma_start(out=out[n * P : (n + 1) * P, cols], in_=bays[n % 2][:, cols])
 
         def pick_block(n):
             picked.append(ring.tile([P, PICK], F32, name="x", tag="x"))

@@ -23,11 +23,12 @@ PASSES = K // 512
 ROW_BLOCKS = H // P
 OUT_BLOCKS = N // P
 CHUNKS = T2 // BANK
-TAIL = 768
-FIRST, SECOND = 256, 640
-LEAD = 384
 HALF = P // 2
 WIDE = T2 // 2
+PASS1_ROW = 8
+FIRST, SECOND = 256, 640
+TAIL = 768
+LEAD = 352
 
 
 def tile_list_rework_bay_scores_kernel(
@@ -46,7 +47,7 @@ def tile_list_rework_bay_scores_kernel(
         idx3 = lists.tile([P, PICK // 16], U16, name="idx3")
         idx4 = lists.tile([P, PICK // 16], U16, name="idx4")
 
-        tab_plane = keep.tile([P, T], U8, name="tab_plane", tag="first", align_bytes=64)
+        tab_plane = keep.tile([P, T], U8, name="tab_plane", align_bytes=64)
         wb_plane = keep.tile([P, PASSES, H], U8, name="wb_plane", align_bytes=64)
         wo_plane = keep.tile([P, N], U8, name="wo_plane", align_bytes=64)
         v_plane = keep.tile([P, S], U8, name="v_plane", align_bytes=64)
@@ -54,15 +55,15 @@ def tile_list_rework_bay_scores_kernel(
         pad_codes = keep.tile([P, 4, P], U32, name="pad_codes", align_bytes=64)
         pad_plane = keep.tile([P, P], U8, name="pad_plane", align_bytes=64)
         z_plane = [keep.tile([P, WIDE], U8, name="z_plane%d" % h, align_bytes=64) for h in range(2)]
-        for plane in (tab_plane[:], wb_plane[:], v_plane1[:], wo_plane[:], pad_codes[:], pad_plane[:], z_plane[0][:], z_plane[1][:]):
-            nc.gpsimd.memset(plane.bitcast(I32), 0)
+        for zeroed in (tab_plane, wb_plane, v_plane1, wo_plane, pad_codes, pad_plane, z_plane[0], z_plane[1]):
+            nc.gpsimd.memset(zeroed[:].bitcast(I32), 0)
 
         tab = [keep.tile([P, T], U32, name="tab%d" % a, tag="tab%d" % a) for a in range(PASSES)]
         wa_rows = wa.rearrange("(a p j) c -> a p j c", a=PASSES, j=4)
         wa_raw = [keep.tile([P, PASSES, 4, P], F32, name="wa_raw%d" % b, tag="wa_raw%d" % b, align_bytes=64) for b in range(ROW_BLOCKS)]
         wb_codes = [keep.tile([P, PASSES, 2 * w], U8, name="wb_codes%d" % i, align_bytes=64) for i, w in enumerate((P, H - P))]
         wb_rows = wb_words.rearrange("a p n -> p a n")
-        gain = keep.tile([P, S], F32, name="gain", tag="gain")
+        gain = keep.tile([P, S], F32, name="gain")
         tols = [keep.tile([P, T2], F32, name="tol%d" % b) for b in range(ROW_BLOCKS)]
 
         def load_tab(a):
@@ -77,7 +78,7 @@ def tile_list_rework_bay_scores_kernel(
 
         nc.sync.dma_start(idx[:], offs)
         load_wa(0, [0])
-        nc.sync.dma_start(out=tab_plane[8:24, :].bitcast(I32), in_=tab_scales[1].bitcast(I32))
+        nc.sync.dma_start(out=tab_plane[PASS1_ROW : PASS1_ROW + 16, :].bitcast(I32), in_=tab_scales[1].bitcast(I32))
         for q in range(4):
             nc.sync.dma_start(
                 out=tab_plane[32 * q : 32 * q + 4, :].bitcast(I32),
@@ -98,9 +99,8 @@ def tile_list_rework_bay_scores_kernel(
         load_tab(1)
         nc.vector.tensor_copy(v_plane[:], tab_plane[:].indirect(idx[:]))
         for q in range(4):
-            nc.sync.dma_start(
-                out=v_plane1[32 * q : 32 * q + 4, :].bitcast(I32), in_=v_plane[8 + 4 * q : 12 + 4 * q, :].bitcast(I32)
-            )
+            r0 = PASS1_ROW + 4 * q
+            nc.sync.dma_start(out=v_plane1[32 * q : 32 * q + 4, :].bitcast(I32), in_=v_plane[r0 : r0 + 4, :].bitcast(I32))
         nc.sync.dma_start(out=gain[:, 0:FIRST], in_=wgs[:, 0:FIRST])
         nc.sync.dma_start(idx2[:], offs2)
         nc.sync.dma_start(out=gain[:, FIRST:S], in_=wgs[:, FIRST:S])
@@ -133,7 +133,7 @@ def tile_list_rework_bay_scores_kernel(
         nc.sync.dma_start(idx3[:], offs3)
         nc.sync.dma_start(idx4[:], offs4)
 
-        v_codes = [keep.tile([P, S], U32, name="v_codes0", tag="first", align_bytes=64)]
+        v_codes = [keep.tile([P, S], U32, name="v_codes0", align_bytes=64)]
         v_planes = (v_plane, v_plane1)
 
         def entries(c0, c1):
@@ -159,8 +159,8 @@ def tile_list_rework_bay_scores_kernel(
         def take_bank(tag, shape):
             return psum.tile(shape, F32, name="bank_" + tag, tag=tag, bufs=4)
 
-        def differences(b, c0, c1, tag):
-            acc = take_bank(tag, [P, BANK])
+        def differences(b, c0, c1):
+            acc = take_bank("a", [P, BANK])
             step = BANK if c1 - c0 == BANK else P
             pairs = [(is_wa, a) for is_wa in (False, True) for a in range(PASSES)]
             if b == 0:
@@ -186,16 +186,16 @@ def tile_list_rework_bay_scores_kernel(
                 )
             return acc
 
-        def features(b, c0, c1, h, h0):
-            acc = differences(b, c0, c1, "a")
-            nc.scalar.activation(out=h[:, c0 - h0 : c1 - h0], in_=acc[:, 0 : c1 - c0], func=ACT.Abs)
+        def features(b, c0, c1, feat, f0):
+            acc = differences(b, c0, c1)
+            nc.scalar.activation(out=feat[:, c0 - f0 : c1 - f0], in_=acc[:, 0 : c1 - c0], func=ACT.Abs)
 
         def negate_gain(c0, c1):
             nc.scalar.activation(out=gain[:, c0:c1], in_=gain[:, c0:c1], func=ACT.Copy, scale=-1.0)
 
-        def fill_cells(b, c0, c1, h, h0):
+        def fill_cells(b, c0, c1, feat, f0):
             window = pages[b % 2][:].indirect(idx2[:, entries(c0, c1)])
-            nc.vector.tensor_tensor(window, h[:, c0 - h0 : c1 - h0], gain[:, c0:c1], MULT)
+            nc.vector.tensor_tensor(window, feat[:, c0 - f0 : c1 - f0], gain[:, c0:c1], MULT)
 
         def features_tile(name, width, tag):
             return keep.tile([P, width], F32, name=name, tag=tag, align_bytes=64)
@@ -209,7 +209,7 @@ def tile_list_rework_bay_scores_kernel(
         gather_words(0)
         round_wa(0)
         quantize_wa(0)
-        v_codes.append(keep.tile([P, S], U32, name="v_codes1", tag="wa_bf0", align_bytes=64))
+        v_codes.append(keep.tile([P, S], U32, name="v_codes1", align_bytes=64))
         gather_words(1)
         negate_gain(0, FIRST)
         pages.append(keep.tile([P, T2], F32, name="page1", tag="tab1"))
@@ -300,9 +300,6 @@ def tile_list_rework_bay_scores_kernel(
             nc.scalar.activation(out=w, in_=wgo_sb[:], func=ACT.Copy, scale=bay_sb[:, n : n + 1])
             weights.append(w)
 
-        def weight_tile(tag):
-            return keep.tile([P, PICK], F32, name="weight%d" % len(weights), tag=tag, align_bytes=64)[:]
-
         last = ROW_BLOCKS - 1
         features(2, 0, BANK, h2, 0)
         features(2, BANK, S, h2, 0)
@@ -310,18 +307,19 @@ def tile_list_rework_bay_scores_kernel(
         fill_cells(2, 0, S, h2, 0)
         features(last, 0, BANK, h3, 0)
         features(last, BANK, TAIL, h3, 0)
-        tail_acc = differences(last, TAIL, S, "a")
+        tail_acc = differences(last, TAIL, S)
         turn(1)
         for c in range(CHUNKS):
             turn_back(0, c, nc.scalar.copy)
         fill_cells(last, 0, TAIL, h3, 0)
-        weigh(weight_tile("z_t0_3"))
+        weight0 = keep.tile([P, PICK], F32, name="weight0", tag="z_t0_%d" % (CHUNKS - 1), align_bytes=64)
+        weigh(weight0[:])
         turn(2)
         banks = [open_turned(last, c) for c in range(CHUNKS)]
         h_tail = keep.tile([P, T2], F32, name="h_tail", tag="page0", align_bytes=64)
         nc.scalar.activation(out=h_tail[:, 0 : S - TAIL], in_=tail_acc[:, 0 : S - TAIL], func=ACT.Abs)
         weigh(h_tail[:, PICK : 2 * PICK])
-        z_codes.append(keep.tile([P, WIDE], U32, name="z_codes0", tag="h_even", align_bytes=64))
+        z_codes.append(keep.tile([P, WIDE], U32, name="z_codes0", align_bytes=64))
         z_codes.append(keep.tile([P, WIDE], U32, name="z_codes1", align_bytes=64))
         first = [take_bank("a", [P, 2, 2 * P]) for c in range(CHUNKS)]
         for c in range(CHUNKS):
@@ -343,11 +341,12 @@ def tile_list_rework_bay_scores_kernel(
         groups = ((z_codes[0], z_plane[0]), (joined_codes, joined_plane))
         move(groups[1], lower, 0, upper)
         by_turns = (nc.scalar.copy, nc.vector.tensor_copy)
+        vector_back = 1
         ys = [keep.tile([P, T2], F32, name="y0", tag="y0")]
         for c in range(CHUNKS):
             close_turned(last, c, banks[c], by_turns[c % 2])
         for c in range(CHUNKS):
-            turn_back(1, c, by_turns[c == 1])
+            turn_back(1, c, by_turns[c == vector_back])
             quantize_z(1, c)
             half_scores(1, c, first[c])
         for c in range(CHUNKS):
@@ -359,7 +358,9 @@ def tile_list_rework_bay_scores_kernel(
         move(groups[1], upper, 1, upper)
 
         picked = []
-        squares = [keep.tile([P, PICK], F32, name="squares%d" % i, tag=tag) for i, tag in enumerate(("y3", "late", "squares"))]
+        early_squares = keep.tile([P, PICK], F32, name="early_squares", tag="y3")
+        rest_squares = keep.tile([P, PICK], F32, name="rest_squares", tag="late")
+        squares = keep.tile([P, PICK], F32, name="squares")
 
         def products(n):
             y = keep.tile([P, T2], F32, name="y%d" % n, tag="y%d" % (n % 4))
@@ -384,7 +385,8 @@ def tile_list_rework_bay_scores_kernel(
 
         def bell(n, m0, m1):
             x = picked[n][:, m0:m1]
-            scratch = squares[(2, 0, 1)[(n < 2) + (n == 1 and m0 > 0)]][:, 0 : m1 - m0]
+            whole = squares if n > 1 else rest_squares if (n, m0) == (1, LEAD) else early_squares
+            scratch = whole[:, 0 : m1 - m0]
             nc.scalar.activation(out=scratch, in_=x, func=ACT.Square)
             nc.scalar.activation(out=x, in_=scratch, func=ACT.Exp, scale=-0.4)
 

@@ -27,7 +27,6 @@ HALF = P // 2
 WIDE = T2 // 2
 PASS1_ROW = 8
 FIRST, SECOND = 256, 640
-TAIL = 768
 LEAD = 352
 
 
@@ -236,7 +235,7 @@ def tile_list_rework_bay_scores_kernel(
         features(1, BANK, S, h_late, BANK)
         fill_cells(1, BANK, S, h_late, BANK)
         h2 = h_late[:, S - BANK : 2 * S - BANK]
-        h3 = features_tile("h3", TAIL, "h_even")
+        h3 = features_tile("h3", S, "h_even")
 
         z_t = [[keep.tile([P, 2, 4, 2, HALF], BF16, name="z_t%d_%d" % (h, c), align_bytes=64) for c in range(CHUNKS)] for h in range(2)]
         z_bf = [[keep.tile([P, WIDE], BF16, name="z_bf%d_%d" % (h, c), align_bytes=64) for c in range(CHUNKS)] for h in range(2)]
@@ -306,26 +305,22 @@ def tile_list_rework_bay_scores_kernel(
         turn(0)
         fill_cells(2, 0, S, h2, 0)
         features(last, 0, BANK, h3, 0)
-        features(last, BANK, TAIL, h3, 0)
-        tail_acc = differences(last, TAIL, S)
+        features(last, BANK, S, h3, 0)
         turn(1)
         for c in range(CHUNKS):
             turn_back(0, c, nc.scalar.copy)
-        fill_cells(last, 0, TAIL, h3, 0)
+        fill_cells(last, 0, S, h3, 0)
         weight0 = keep.tile([P, PICK], F32, name="weight0", tag="z_t0_%d" % (CHUNKS - 1), align_bytes=64)
         weigh(weight0[:])
         turn(2)
         banks = [open_turned(last, c) for c in range(CHUNKS)]
-        h_tail = keep.tile([P, T2], F32, name="h_tail", tag="page0", align_bytes=64)
-        nc.scalar.activation(out=h_tail[:, 0 : S - TAIL], in_=tail_acc[:, 0 : S - TAIL], func=ACT.Abs)
-        weigh(h_tail[:, PICK : 2 * PICK])
+        weight1 = keep.tile([P, PICK], F32, name="weight1", tag="page0", align_bytes=64)
+        weigh(weight1[:])
         z_codes.append(keep.tile([P, WIDE], U32, name="z_codes0", align_bytes=64))
         z_codes.append(keep.tile([P, WIDE], U32, name="z_codes1", align_bytes=64))
         first = [take_bank("a", [P, 2, 2 * P]) for c in range(CHUNKS)]
         for c in range(CHUNKS):
             quantize_z(0, c)
-            half_scores(0, c, first[c])
-        fill_cells(last, TAIL, S, h_tail, TAIL)
         bays = [keep.tile([P, T2], F32, name="bays%d" % i, tag="tol%d" % (i + 1)) for i in range(2)]
         for page in bays:
             nc.gpsimd.memset(page[:], 0.0)
@@ -348,7 +343,9 @@ def tile_list_rework_bay_scores_kernel(
         for c in range(CHUNKS):
             turn_back(1, c, by_turns[c == vector_back])
             quantize_z(1, c)
-            half_scores(1, c, first[c])
+        for h in range(2):
+            for c in range(CHUNKS):
+                half_scores(h, c, first[c])
         for c in range(CHUNKS):
             by_turns[c % 2](
                 out=ys[0][:, c * BANK : (c + 1) * BANK].rearrange("p (m g t) -> p m g t", m=2, g=2),

@@ -39,6 +39,7 @@ def tile_list_rework_bay_scores_kernel(
         lists = ctx.enter_context(tc.tile_pool(name="lists", bufs=1))
         keep = ctx.enter_context(tc.tile_pool(name="keep", bufs=1))
         ring = ctx.enter_context(tc.tile_pool(name="ring", bufs=3))
+        shared = ctx.enter_context(tc.tile_pool(name="shared", bufs=1))
         psum = ctx.enter_context(tc.psum_pool(name="psum", bufs=1))
 
         idx = lists.tile([P, S // 16], U16, name="idx")
@@ -48,16 +49,16 @@ def tile_list_rework_bay_scores_kernel(
 
         tab_plane = keep.tile([P, T], U8, name="tab_plane", align_bytes=64)
         wb_plane = keep.tile([P, PASSES, H], U8, name="wb_plane", align_bytes=64)
-        wo_plane = keep.tile([P, N], U8, name="wo_plane", align_bytes=64)
         v_plane = keep.tile([P, S], U8, name="v_plane", align_bytes=64)
         v_plane1 = keep.tile([P, S], U8, name="v_plane1", align_bytes=64)
-        pad_codes = keep.tile([P, 4, P], U32, name="pad_codes", align_bytes=64)
-        pad_plane = keep.tile([P, P], U8, name="pad_plane", align_bytes=64)
-        z_plane = [keep.tile([P, WIDE], U8, name="z_plane%d" % h, align_bytes=64) for h in range(2)]
-        for zeroed in (tab_plane, wb_plane, v_plane1, wo_plane, pad_codes, pad_plane, z_plane[0], z_plane[1]):
-            nc.gpsimd.memset(zeroed[:].bitcast(I32), 0)
+        pages = [keep.tile([P, T2], F32, name="page0", tag="page0", align_bytes=64)]
+        for zeroed in (tab_plane, wb_plane, v_plane1):
+            nc.vector.memset(zeroed[:].bitcast(I32), 0)
+        nc.vector.memset(pages[0][:], 0.0)
+        ident = keep.tile([P, P], F32, name="ident")
+        make_identity(nc, ident[:])
 
-        tab = [keep.tile([P, T], U32, name="tab%d" % a, tag="tab%d" % a) for a in range(PASSES)]
+        tab = [keep.tile([P, T], U32, name="tab0"), shared.tile([P, T], U32, name="tab1", align_bytes=64, offset=0)]
         wa_rows = wa.rearrange("(a p j) c -> a p j c", a=PASSES, j=4)
         wa_raw = [keep.tile([P, PASSES, 4, P], F32, name="wa_raw%d" % b, tag="wa_raw%d" % b, align_bytes=64) for b in range(ROW_BLOCKS)]
         wb_codes = [keep.tile([P, PASSES, 2 * w], U8, name="wb_codes%d" % i, align_bytes=64) for i, w in enumerate((P, H - P))]
@@ -89,10 +90,6 @@ def tile_list_rework_bay_scores_kernel(
                 out=wb_plane[32 * q : 32 * q + 4, :, :].bitcast(I32),
                 in_=wb_scales[:, 4 * q : 4 * q + 4, :].rearrange("a r c -> r a c").bitcast(I32),
             )
-        ident = keep.tile([P, P], F32, name="ident")
-        make_identity(nc, ident[:])
-        pages = [keep.tile([P, T2], F32, name="page0", tag="page0", align_bytes=64)]
-        nc.gpsimd.memset(pages[0][:], 0.0)
         load_wa(0, [1])
         nc.sync.dma_start(out=wb_codes[0][:].bitcast(I32), in_=wb_rows[:, :, 0 : 2 * P].bitcast(I32))
         load_tab(1)
@@ -118,19 +115,6 @@ def tile_list_rework_bay_scores_kernel(
         load_tol(3)
         wo_codes = keep.tile([P, N], U32, name="wo_codes", align_bytes=64)
         nc.sync.dma_start(out=wo_codes[:].bitcast(I32), in_=wo_words[0].rearrange("p c i -> p (c i)").bitcast(I32))
-        for q in range(4):
-            nc.sync.dma_start(
-                out=wo_plane[32 * q : 32 * q + 4, :].bitcast(I32),
-                in_=wo_scales[0, 4 * q : 4 * q + 4, :].bitcast(I32),
-            )
-        wo_first = wo_words[0].rearrange("(h p) c i -> p h (c i)", h=2)[:, :, 0 : 4 * P].bitcast(I32)
-        for g in range(2):
-            nc.sync.dma_start(out=pad_codes[g * HALF : (g + 1) * HALF, g:4:2, :].bitcast(I32), in_=wo_first)
-        for q in range(4):
-            r0 = 4 * ((q + 2) % 4)
-            nc.sync.dma_start(out=pad_plane[32 * q : 32 * q + 4, :].bitcast(I32), in_=wo_scales[0, r0 : r0 + 4, 0:P].bitcast(I32))
-        nc.sync.dma_start(idx3[:], offs3)
-        nc.sync.dma_start(idx4[:], offs4)
 
         v_codes = [keep.tile([P, S], U32, name="v_codes0", align_bytes=64)]
         v_planes = (v_plane, v_plane1)
@@ -211,8 +195,28 @@ def tile_list_rework_bay_scores_kernel(
         v_codes.append(keep.tile([P, S], U32, name="v_codes1", align_bytes=64))
         gather_words(1)
         negate_gain(0, FIRST)
-        pages.append(keep.tile([P, T2], F32, name="page1", tag="tab1"))
+        wo_plane = shared.tile([P, N], U8, name="wo_plane", align_bytes=64, offset=0)
+        pad_plane = shared.tile([P, P], U8, name="pad_plane", align_bytes=64, offset=N)
+        z_plane = [shared.tile([P, WIDE], U8, name="z_plane%d" % h, align_bytes=64, offset=(1 + h) * WIDE) for h in range(2)]
+        pad_codes = shared.tile([P, 4, P], U32, name="pad_codes", align_bytes=64, offset=3 * WIDE)
+        pages.append(shared.tile([P, T2], F32, name="page1", align_bytes=64, offset=5 * WIDE))
         nc.gpsimd.memset(pages[1][:], 0.0)
+        for zeroed in (wo_plane, pad_codes, pad_plane, z_plane[0], z_plane[1]):
+            nc.gpsimd.memset(zeroed[:].bitcast(I32), 0)
+        for q in range(4):
+            nc.sync.dma_start(
+                out=wo_plane[32 * q : 32 * q + 4, :].bitcast(I32),
+                in_=wo_scales[0, 4 * q : 4 * q + 4, :].bitcast(I32),
+            )
+        wo_first = wo_words[0].rearrange("(h p) c i -> p h (c i)", h=2)[:, :, 0 : 4 * P].bitcast(I32)
+        for g in range(2):
+            nc.sync.dma_start(out=pad_codes[g * HALF : (g + 1) * HALF, g:4:2, :].bitcast(I32), in_=wo_first)
+        for q in range(4):
+            r0 = 4 * ((q + 2) % 4)
+            nc.sync.dma_start(out=pad_plane[32 * q : 32 * q + 4, :].bitcast(I32), in_=wo_scales[0, r0 : r0 + 4, 0:P].bitcast(I32))
+        nc.sync.dma_start(idx3[:], offs3)
+        nc.sync.dma_start(idx4[:], offs4)
+
         h_head = features_tile("h0_head", SECOND, "h_even")
         features(0, 0, FIRST, h_head, 0)
         fill_cells(0, 0, FIRST, h_head, 0)
@@ -263,7 +267,7 @@ def tile_list_rework_bay_scores_kernel(
 
         def turn_back(h, c, copy):
             words = z_t[h][c][:].rearrange("t u s b x -> t (u s b x)").bitcast(F32)
-            bank = take_bank("b", [P, 2, 2 * P])
+            bank = take_bank("a" if h else "b", [P, 2, 2 * P])
             for u in range(2):
                 for m in range(2):
                     w0 = (2 * u + m) * P
@@ -318,7 +322,7 @@ def tile_list_rework_bay_scores_kernel(
         weigh(weight1[:])
         z_codes.append(keep.tile([P, WIDE], U32, name="z_codes0", align_bytes=64))
         z_codes.append(keep.tile([P, WIDE], U32, name="z_codes1", align_bytes=64))
-        first = [take_bank("a", [P, 2, 2 * P]) for c in range(CHUNKS)]
+        first = [take_bank("b", [P, 2, 2 * P]) for c in range(CHUNKS)]
         for c in range(CHUNKS):
             quantize_z(0, c)
         bays = [keep.tile([P, T2], F32, name="bays%d" % i, tag="tol%d" % (i + 1)) for i in range(2)]
@@ -364,7 +368,7 @@ def tile_list_rework_bay_scores_kernel(
             cells = y[:].rearrange("p (k g t) -> p g k t", g=2, t=P)
             for g, (codes, plane) in enumerate(groups):
                 for j in range(2):
-                    acc = take_bank("b", [P, 4, P])
+                    acc = take_bank("a", [P, 4, P])
                     nc.tensor.matmul_mx(
                         out=acc[:].rearrange("p k t -> p (k t)"),
                         lhsT=wo_codes[:, n * P : (n + 1) * P].bitcast(E4M3),

@@ -25,6 +25,7 @@ OUT_BLOCKS = N // P
 CHUNKS = T2 // BANK
 HALF = P // 2
 WIDE = T2 // 2
+AHEAD = 1536
 PASS1_ROW = 8
 FIRST, SECOND = 256, 640
 LEAD = 352
@@ -52,7 +53,8 @@ def tile_list_rework_bay_scores_kernel(
         v_plane = keep.tile([P, S], U8, name="v_plane", align_bytes=64)
         v_plane1 = keep.tile([P, S], U8, name="v_plane1", align_bytes=64)
         pages = [keep.tile([P, T2], F32, name="page0", tag="page0", align_bytes=64)]
-        for zeroed in (tab_plane, wb_plane, v_plane1):
+        nc.gpsimd.memset(tab_plane[:].bitcast(I32), 0)
+        for zeroed in (wb_plane, v_plane1):
             nc.vector.memset(zeroed[:].bitcast(I32), 0)
         nc.vector.memset(pages[0][:], 0.0)
         ident = keep.tile([P, P], F32, name="ident")
@@ -66,8 +68,9 @@ def tile_list_rework_bay_scores_kernel(
         gain = keep.tile([P, S], F32, name="gain")
         tols = [keep.tile([P, T2], F32, name="tol%d" % b) for b in range(ROW_BLOCKS)]
 
-        def load_tab(a):
-            nc.sync.dma_start(out=tab[a][:].bitcast(I32), in_=tab_words[a].rearrange("p t i -> p (t i)").bitcast(I32))
+        def load_tab(a, t0, t1):
+            words = tab_words[a].rearrange("p t i -> p (t i)").bitcast(I32)
+            nc.sync.dma_start(out=tab[a][:, t0:t1].bitcast(I32), in_=words[:, t0:t1])
 
         def load_wa(b, passes=range(PASSES)):
             for a in passes:
@@ -84,7 +87,7 @@ def tile_list_rework_bay_scores_kernel(
                 out=tab_plane[32 * q : 32 * q + 4, :].bitcast(I32),
                 in_=tab_scales[0, 4 * q : 4 * q + 4, :].bitcast(I32),
             )
-        load_tab(0)
+        load_tab(0, 0, T)
         for q in range(4):
             nc.sync.dma_start(
                 out=wb_plane[32 * q : 32 * q + 4, :, :].bitcast(I32),
@@ -92,11 +95,12 @@ def tile_list_rework_bay_scores_kernel(
             )
         load_wa(0, [1])
         nc.sync.dma_start(out=wb_codes[0][:].bitcast(I32), in_=wb_rows[:, :, 0 : 2 * P].bitcast(I32))
-        load_tab(1)
+        load_tab(1, 0, AHEAD)
         nc.vector.tensor_copy(v_plane[:], tab_plane[:].indirect(idx[:]))
         for q in range(4):
             r0 = PASS1_ROW + 4 * q
             nc.sync.dma_start(out=v_plane1[32 * q : 32 * q + 4, :].bitcast(I32), in_=v_plane[r0 : r0 + 4, :].bitcast(I32))
+        load_tab(1, AHEAD, T)
         nc.sync.dma_start(out=gain[:, 0:FIRST], in_=wgs[:, 0:FIRST])
         nc.sync.dma_start(idx2[:], offs2)
         nc.sync.dma_start(out=gain[:, FIRST:S], in_=wgs[:, FIRST:S])
@@ -359,6 +363,7 @@ def tile_list_rework_bay_scores_kernel(
         move(groups[1], upper, 1, upper)
 
         picked = []
+        first_squares = keep.tile([P, PICK], F32, name="first_squares", tag="y1")
         early_squares = keep.tile([P, PICK], F32, name="early_squares", tag="y3")
         rest_squares = keep.tile([P, PICK], F32, name="rest_squares", tag="late")
         squares = keep.tile([P, PICK], F32, name="squares")
@@ -386,7 +391,7 @@ def tile_list_rework_bay_scores_kernel(
 
         def bell(n, m0, m1):
             x = picked[n][:, m0:m1]
-            whole = squares if n > 1 else rest_squares if (n, m0) == (1, LEAD) else early_squares
+            whole = squares if n > 1 else first_squares if n == 0 else rest_squares if m0 else early_squares
             scratch = whole[:, 0 : m1 - m0]
             nc.scalar.activation(out=scratch, in_=x, func=ACT.Square)
             nc.scalar.activation(out=x, in_=scratch, func=ACT.Exp, scale=-0.4)

@@ -66,7 +66,9 @@ def tile_list_rework_bay_scores_kernel(
         wb_codes = [keep.tile([P, PASSES, 2 * w], U8, name="wb_codes%d" % i, align_bytes=64) for i, w in enumerate((P, H - P))]
         wb_rows = wb_words.rearrange("a p n -> p a n")
         gain = keep.tile([P, S], F32, name="gain")
-        tols = [keep.tile([P, T2], F32, name="tol%d" % b) for b in range(ROW_BLOCKS)]
+        tols = [keep.tile([P, T2], F32, name="tol%d" % b) for b in range(ROW_BLOCKS - 1)]
+        tols.append(keep.tile([P, T2 - BANK], F32, name="tol3", tag="tol3", align_bytes=64))
+        tol_end = keep.tile([P, BANK], F32, name="tol_end")
 
         def load_tab(a, t0, t1):
             words = tab_words[a].rearrange("p t i -> p (t i)").bitcast(I32)
@@ -77,7 +79,7 @@ def tile_list_rework_bay_scores_kernel(
                 nc.sync.dma_start(out=wa_raw[b][:, a, :, :], in_=wa_rows[a][:, :, b * P : (b + 1) * P])
 
         def load_tol(b):
-            nc.sync.dma_start(out=tols[b][:], in_=tol[b * P : (b + 1) * P, :])
+            nc.sync.dma_start(out=tols[b][:], in_=tol[b * P : (b + 1) * P, 0 : tols[b].shape[1]])
 
         nc.sync.dma_start(idx[:], offs)
         load_wa(0, [0])
@@ -117,6 +119,7 @@ def tile_list_rework_bay_scores_kernel(
         with nc.allow_non_contiguous_dma(reason="one value of bay for each partition"):
             nc.sync.dma_start(out=bay_sb[:], in_=bay.rearrange("(n p) -> p n", p=P))
         load_tol(3)
+        nc.sync.dma_start(out=tol_end[:], in_=tol[H - P : H, T2 - BANK : T2])
         wo_codes = keep.tile([P, N], U32, name="wo_codes", align_bytes=64)
         nc.sync.dma_start(out=wo_codes[:].bitcast(I32), in_=wo_words[0].rearrange("p c i -> p (c i)").bitcast(I32))
 
@@ -143,11 +146,11 @@ def tile_list_rework_bay_scores_kernel(
         def quantize_wa(b):
             nc.vector.quantize_mx(out=wa_codes[b][:].bitcast(E4M3), scales=wa_plane[b][:], in_=wa_bf[b][:])
 
-        def take_bank(tag, shape):
-            return psum.tile(shape, F32, name="bank_" + tag, tag=tag, bufs=4)
+        def take_bank(number, shape):
+            return psum.tile(shape, F32, name="bank", tag="bank%d" % number)
 
-        def differences(b, c0, c1):
-            acc = take_bank("a", [P, BANK])
+        def differences(b, c0, c1, number):
+            acc = take_bank(number, [P, BANK])
             step = BANK if c1 - c0 == BANK else P
             pairs = [(is_wa, a) for is_wa in (False, True) for a in range(PASSES)]
             if b == 0:
@@ -173,8 +176,8 @@ def tile_list_rework_bay_scores_kernel(
                 )
             return acc
 
-        def features(b, c0, c1, feat, f0):
-            acc = differences(b, c0, c1)
+        def features(b, c0, c1, feat, f0, number):
+            acc = differences(b, c0, c1, number)
             nc.scalar.activation(out=feat[:, c0 - f0 : c1 - f0], in_=acc[:, 0 : c1 - c0], func=ACT.Abs)
 
         def negate_gain(c0, c1):
@@ -222,25 +225,25 @@ def tile_list_rework_bay_scores_kernel(
         nc.sync.dma_start(idx4[:], offs4)
 
         h_head = features_tile("h0_head", SECOND, "h_even")
-        features(0, 0, FIRST, h_head, 0)
+        features(0, 0, FIRST, h_head, 0, 4)
         fill_cells(0, 0, FIRST, h_head, 0)
-        features(0, FIRST, SECOND, h_head, 0)
+        features(0, FIRST, SECOND, h_head, 0, 5)
         negate_gain(FIRST, S)
         fill_cells(0, FIRST, SECOND, h_head, 0)
         round_wa(1)
         quantize_wa(1)
         h_last = features_tile("h0_last", S - SECOND, "wa_raw1")
-        features(0, SECOND, S, h_last, SECOND)
+        features(0, SECOND, S, h_last, SECOND, 6)
         fill_cells(0, SECOND, S, h_last, SECOND)
         h_head = features_tile("h1_head", BANK, "h_odd")
-        features(1, 0, BANK, h_head, 0)
+        features(1, 0, BANK, h_head, 0, 7)
         round_wa(2)
         quantize_wa(2)
         fill_cells(1, 0, BANK, h_head, 0)
         round_wa(3)
         quantize_wa(3)
         h_late = features_tile("h_late", 2 * S - BANK, "wa_raw3")
-        features(1, BANK, S, h_late, BANK)
+        features(1, BANK, S, h_late, BANK, 4)
         fill_cells(1, BANK, S, h_late, BANK)
         h2 = h_late[:, S - BANK : 2 * S - BANK]
         h3 = features_tile("h3", S, "h_even")
@@ -248,30 +251,37 @@ def tile_list_rework_bay_scores_kernel(
         z_t = [[keep.tile([P, 2, 4, 2, HALF], BF16, name="z_t%d_%d" % (h, c), align_bytes=64) for c in range(CHUNKS)] for h in range(2)]
         z_bf = [[keep.tile([P, WIDE], BF16, name="z_bf%d_%d" % (h, c), align_bytes=64) for c in range(CHUNKS)] for h in range(2)]
 
-        def open_turned(b, c):
-            bank = take_bank("b", [P, 4, P])
-            for s in range(4):
-                cols = slice(c * BANK + s * P, c * BANK + (s + 1) * P)
-                nc.tensor.matmul(bank[:, s, :], tols[b][:, cols], ident[:], start=(s == 0), stop=False, is_transpose=True)
-            return bank
-
-        def close_turned(b, c, bank, copy):
-            for s in range(4):
-                cols = slice(c * BANK + s * P, c * BANK + (s + 1) * P)
-                nc.tensor.matmul(bank[:, s, :], pages[b % 2][:, cols], ident[:], start=False, stop=(s == 3), is_transpose=True)
-            copy(
-                out=z_t[b // 2][c][:, :, :, b % 2, :].rearrange("t u s (p e) -> t u s p e", e=2),
-                in_=bank[:].rearrange("t s (p u e) -> t u s p e", u=2, e=2),
-            )
-
-        def turn(b):
-            banks = [open_turned(b, c) for c in range(CHUNKS)]
+        def open_turned(b, numbers):
+            banks = []
             for c in range(CHUNKS):
-                close_turned(b, c, banks[c], nc.scalar.copy)
+                bank = take_bank(numbers[c], [P, 4, P])
+                for s in range(4):
+                    if (b, c) == (ROW_BLOCKS - 1, CHUNKS - 1):
+                        cells = tol_end[:, s * P : (s + 1) * P]
+                    else:
+                        cells = tols[b][:, c * BANK + s * P : c * BANK + (s + 1) * P]
+                    nc.tensor.matmul(bank[:, s, :], cells, ident[:], start=(s == 0), stop=False, is_transpose=True)
+                banks.append(bank)
+            return banks
 
-        def turn_back(h, c, copy):
+        def close_turned(b, banks, copies, eye):
+            for c in range(CHUNKS):
+                for s in range(4):
+                    cols = slice(c * BANK + s * P, c * BANK + (s + 1) * P)
+                    nc.tensor.matmul(banks[c][:, s, :], pages[b % 2][:, cols], eye[:], start=False, stop=(s == 3), is_transpose=True)
+                copies[c % 2](
+                    out=z_t[b // 2][c][:, :, :, b % 2, :].rearrange("t u s (p e) -> t u s p e", e=2),
+                    in_=banks[c][:].rearrange("t s (p u e) -> t u s p e", u=2, e=2),
+                )
+
+        def identity_on(tag):
+            eye = keep.tile([P, P], F32, name="eye", tag=tag, align_bytes=64)
+            nc.scalar.copy(out=eye[:], in_=ident[:])
+            return eye
+
+        def turn_back(h, c, copy, number):
             words = z_t[h][c][:].rearrange("t u s b x -> t (u s b x)").bitcast(F32)
-            bank = take_bank("a" if h else "b", [P, 2, 2 * P])
+            bank = take_bank(number, [P, 2, 2 * P])
             for u in range(2):
                 for m in range(2):
                     w0 = (2 * u + m) * P
@@ -308,25 +318,31 @@ def tile_list_rework_bay_scores_kernel(
             weights.append(w)
 
         last = ROW_BLOCKS - 1
-        features(2, 0, BANK, h2, 0)
-        features(2, BANK, S, h2, 0)
-        turn(0)
+        on_scalar = (nc.scalar.copy, nc.scalar.copy)
+        features(2, 0, BANK, h2, 0, 5)
+        banks = open_turned(0, (0, 1, 2, 3))
+        close_turned(0, banks, on_scalar, ident)
+        features(2, BANK, S, h2, 0, 0)
         fill_cells(2, 0, S, h2, 0)
-        features(last, 0, BANK, h3, 0)
-        features(last, BANK, S, h3, 0)
-        turn(1)
+        banks = open_turned(1, (6, 1, 2, 3))
+        features(last, 0, BANK, h3, 0, 0)
+        close_turned(1, banks, on_scalar, ident)
+        features(last, BANK, S, h3, 0, 6)
+        spare_banks, z_banks = (4, 5, 7, 0), (1, 2, 3, 6)
+        eye = identity_on("z_t0_%d" % (CHUNKS - 1))
         for c in range(CHUNKS):
-            turn_back(0, c, nc.scalar.copy)
+            turn_back(0, c, nc.scalar.copy, spare_banks[c])
+        banks = open_turned(2, z_banks)
         fill_cells(last, 0, S, h3, 0)
-        weight0 = keep.tile([P, PICK], F32, name="weight0", tag="z_t0_%d" % (CHUNKS - 1), align_bytes=64)
-        weigh(weight0[:])
-        turn(2)
-        banks = [open_turned(last, c) for c in range(CHUNKS)]
-        weight1 = keep.tile([P, PICK], F32, name="weight1", tag="page0", align_bytes=64)
-        weigh(weight1[:])
+        close_turned(2, banks, on_scalar, eye)
+        banks = open_turned(last, z_banks)
+        eye = identity_on("tol3")
+        early_weights = keep.tile([P, 2, PICK], F32, name="early_weights", tag="page0", align_bytes=64)
+        for n in range(2):
+            weigh(early_weights[:, n, :])
         z_codes.append(keep.tile([P, WIDE], U32, name="z_codes0", align_bytes=64))
         z_codes.append(keep.tile([P, WIDE], U32, name="z_codes1", align_bytes=64))
-        first = [take_bank("b", [P, 2, 2 * P]) for c in range(CHUNKS)]
+        first = [take_bank(z_banks[c], [P, 2, 2 * P]) for c in range(CHUNKS)]
         for c in range(CHUNKS):
             quantize_z(0, c)
         bays = [keep.tile([P, T2], F32, name="bays%d" % i, tag="tol%d" % (i + 1)) for i in range(2)]
@@ -346,10 +362,9 @@ def tile_list_rework_bay_scores_kernel(
         by_turns = (nc.scalar.copy, nc.vector.tensor_copy)
         vector_back = 1
         ys = [keep.tile([P, T2], F32, name="y0", tag="y0")]
+        close_turned(last, banks, by_turns, eye)
         for c in range(CHUNKS):
-            close_turned(last, c, banks[c], by_turns[c % 2])
-        for c in range(CHUNKS):
-            turn_back(1, c, by_turns[c == vector_back])
+            turn_back(1, c, by_turns[c == vector_back], spare_banks[c])
             quantize_z(1, c)
         for h in range(2):
             for c in range(CHUNKS):
@@ -373,7 +388,7 @@ def tile_list_rework_bay_scores_kernel(
             cells = y[:].rearrange("p (k g t) -> p g k t", g=2, t=P)
             for g, (codes, plane) in enumerate(groups):
                 for j in range(2):
-                    acc = take_bank("a", [P, 4, P])
+                    acc = take_bank(spare_banks[2 * g + j], [P, 4, P])
                     nc.tensor.matmul_mx(
                         out=acc[:].rearrange("p k t -> p (k t)"),
                         lhsT=wo_codes[:, n * P : (n + 1) * P].bitcast(E4M3),

@@ -29,6 +29,7 @@ AHEAD = 1536
 PASS1_ROW = 8
 FIRST, SECOND = 256, 640
 LEAD = 352
+LAST_CUT = 640
 
 
 def tile_list_rework_bay_scores_kernel(
@@ -246,7 +247,7 @@ def tile_list_rework_bay_scores_kernel(
         features(1, BANK, S, h_late, BANK, 4)
         fill_cells(1, BANK, S, h_late, BANK)
         h2 = h_late[:, S - BANK : 2 * S - BANK]
-        h3 = features_tile("h3", S, "h_even")
+        h3 = features_tile("h3", LAST_CUT, "h_even")
 
         z_t = [[keep.tile([P, 2, 4, 2, HALF], BF16, name="z_t%d_%d" % (h, c), align_bytes=64) for c in range(CHUNKS)] for h in range(2)]
         z_bf = [[keep.tile([P, WIDE], BF16, name="z_bf%d_%d" % (h, c), align_bytes=64) for c in range(CHUNKS)] for h in range(2)]
@@ -327,23 +328,45 @@ def tile_list_rework_bay_scores_kernel(
         banks = open_turned(1, (6, 1, 2, 3))
         features(last, 0, BANK, h3, 0, 0)
         close_turned(1, banks, on_scalar, ident)
-        features(last, BANK, S, h3, 0, 6)
+        acc = differences(last, BANK, S, 6)
+        nc.scalar.activation(out=h3[:, BANK:LAST_CUT], in_=acc[:, 0 : LAST_CUT - BANK], func=ACT.Abs)
+        fill_cells(last, 0, LAST_CUT, h3, 0)
         spare_banks, z_banks = (4, 5, 7, 0), (1, 2, 3, 6)
-        eye = identity_on("z_t0_%d" % (CHUNKS - 1))
+        z_codes.append(keep.tile([P, WIDE], U32, name="z_codes0", align_bytes=64))
+        z_codes.append(keep.tile([P, WIDE], U32, name="z_codes1", align_bytes=64))
         for c in range(CHUNKS):
             turn_back(0, c, nc.scalar.copy, spare_banks[c])
+            if c == 1:
+                for early in range(2):
+                    quantize_z(0, early)
+                h_end = features_tile("h3_end", S - LAST_CUT, "z_t0_1")
+                nc.scalar.activation(out=h_end[:], in_=acc[:, LAST_CUT - BANK : BANK], func=ACT.Abs)
+                fill_cells(last, LAST_CUT, S, h_end, LAST_CUT)
         banks = open_turned(2, z_banks)
-        fill_cells(last, 0, S, h3, 0)
-        close_turned(2, banks, on_scalar, eye)
-        banks = open_turned(last, z_banks)
+        last_banks = open_turned(last, spare_banks)
         eye = identity_on("tol3")
+        close_turned(2, banks, on_scalar, eye)
+        banks = last_banks
         early_weights = keep.tile([P, 2, PICK], F32, name="early_weights", tag="page0", align_bytes=64)
         for n in range(2):
             weigh(early_weights[:, n, :])
-        z_codes.append(keep.tile([P, WIDE], U32, name="z_codes0", align_bytes=64))
-        z_codes.append(keep.tile([P, WIDE], U32, name="z_codes1", align_bytes=64))
-        first = [take_bank(z_banks[c], [P, 2, 2 * P]) for c in range(CHUNKS)]
-        for c in range(CHUNKS):
+        first = []
+        for c in range(2):
+            for k in range(2 - c):
+                warm = take_bank(z_banks[c], [P, 2 * P])
+                cols = slice(c * 2 * P, (c + 1) * 2 * P)
+                nc.tensor.matmul_mx(
+                    out=warm[:],
+                    lhsT=wo_codes[:, 0:P].bitcast(E4M3),
+                    lhsT_scale=wo_plane[:, 0:P],
+                    rhs=z_codes[0][:, cols].bitcast(E4M3),
+                    rhs_scale=z_plane[0][:, cols],
+                    start=True,
+                    stop=True,
+                )
+            first.append(take_bank(z_banks[c], [P, 2, 2 * P]))
+            half_scores(0, c, first[c])
+        for c in range(2, CHUNKS):
             quantize_z(0, c)
         bays = [keep.tile([P, T2], F32, name="bays%d" % i, tag="tol%d" % (i + 1)) for i in range(2)]
         for page in bays:
@@ -366,9 +389,11 @@ def tile_list_rework_bay_scores_kernel(
         for c in range(CHUNKS):
             turn_back(1, c, by_turns[c == vector_back], spare_banks[c])
             quantize_z(1, c)
-        for h in range(2):
-            for c in range(CHUNKS):
-                half_scores(h, c, first[c])
+        for c in range(2, CHUNKS):
+            first.append(take_bank(z_banks[c], [P, 2, 2 * P]))
+            half_scores(0, c, first[c])
+        for c in range(CHUNKS):
+            half_scores(1, c, first[c])
         for c in range(CHUNKS):
             by_turns[c % 2](
                 out=ys[0][:, c * BANK : (c + 1) * BANK].rearrange("p (m g t) -> p m g t", m=2, g=2),

@@ -29,7 +29,6 @@ AHEAD = 1536
 PASS1_ROW = 8
 FIRST, SECOND = 256, 640
 LEAD = 352
-LAST_CUT = 640
 
 
 def tile_list_rework_bay_scores_kernel(
@@ -67,9 +66,7 @@ def tile_list_rework_bay_scores_kernel(
         wb_codes = [keep.tile([P, PASSES, 2 * w], U8, name="wb_codes%d" % i, align_bytes=64) for i, w in enumerate((P, H - P))]
         wb_rows = wb_words.rearrange("a p n -> p a n")
         gain = keep.tile([P, S], F32, name="gain")
-        tols = [keep.tile([P, T2], F32, name="tol%d" % b) for b in range(ROW_BLOCKS - 1)]
-        tols.append(keep.tile([P, T2 - BANK], F32, name="tol3", tag="tol3", align_bytes=64))
-        tol_end = keep.tile([P, BANK], F32, name="tol_end")
+        tols = [keep.tile([P, T2], F32, name="tol%d" % b) for b in range(ROW_BLOCKS)]
 
         def load_tab(a, t0, t1):
             words = tab_words[a].rearrange("p t i -> p (t i)").bitcast(I32)
@@ -80,7 +77,7 @@ def tile_list_rework_bay_scores_kernel(
                 nc.sync.dma_start(out=wa_raw[b][:, a, :, :], in_=wa_rows[a][:, :, b * P : (b + 1) * P])
 
         def load_tol(b):
-            nc.sync.dma_start(out=tols[b][:], in_=tol[b * P : (b + 1) * P, 0 : tols[b].shape[1]])
+            nc.sync.dma_start(out=tols[b][:], in_=tol[b * P : (b + 1) * P, :])
 
         nc.sync.dma_start(idx[:], offs)
         load_wa(0, [0])
@@ -120,7 +117,6 @@ def tile_list_rework_bay_scores_kernel(
         with nc.allow_non_contiguous_dma(reason="one value of bay for each partition"):
             nc.sync.dma_start(out=bay_sb[:], in_=bay.rearrange("(n p) -> p n", p=P))
         load_tol(3)
-        nc.sync.dma_start(out=tol_end[:], in_=tol[H - P : H, T2 - BANK : T2])
         wo_codes = keep.tile([P, N], U32, name="wo_codes", align_bytes=64)
         nc.sync.dma_start(out=wo_codes[:].bitcast(I32), in_=wo_words[0].rearrange("p c i -> p (c i)").bitcast(I32))
 
@@ -247,38 +243,43 @@ def tile_list_rework_bay_scores_kernel(
         features(1, BANK, S, h_late, BANK, 4)
         fill_cells(1, BANK, S, h_late, BANK)
         h2 = h_late[:, S - BANK : 2 * S - BANK]
-        h3 = features_tile("h3", LAST_CUT, "h_even")
+        h3 = features_tile("h3", S, "h_even")
 
         z_t = [[keep.tile([P, 2, 4, 2, HALF], BF16, name="z_t%d_%d" % (h, c), align_bytes=64) for c in range(CHUNKS)] for h in range(2)]
         z_bf = [[keep.tile([P, WIDE], BF16, name="z_bf%d_%d" % (h, c), align_bytes=64) for c in range(CHUNKS)] for h in range(2)]
 
-        def open_turned(b, numbers):
+        def open_turned(b, numbers, eye):
             banks = []
             for c in range(CHUNKS):
                 bank = take_bank(numbers[c], [P, 4, P])
                 for s in range(4):
-                    if (b, c) == (ROW_BLOCKS - 1, CHUNKS - 1):
-                        cells = tol_end[:, s * P : (s + 1) * P]
-                    else:
-                        cells = tols[b][:, c * BANK + s * P : c * BANK + (s + 1) * P]
-                    nc.tensor.matmul(bank[:, s, :], cells, ident[:], start=(s == 0), stop=False, is_transpose=True)
+                    cells = tols[b][:, c * BANK + s * P : c * BANK + (s + 1) * P]
+                    nc.tensor.matmul(bank[:, s, :], cells, eye[:], start=(s == 0), stop=False, is_transpose=True)
                 banks.append(bank)
             return banks
 
-        def close_turned(b, banks, copies, eye):
-            for c in range(CHUNKS):
-                for s in range(4):
-                    cols = slice(c * BANK + s * P, c * BANK + (s + 1) * P)
-                    nc.tensor.matmul(banks[c][:, s, :], pages[b % 2][:, cols], eye[:], start=False, stop=(s == 3), is_transpose=True)
-                copies[c % 2](
-                    out=z_t[b // 2][c][:, :, :, b % 2, :].rearrange("t u s (p e) -> t u s p e", e=2),
-                    in_=banks[c][:].rearrange("t s (p u e) -> t u s p e", u=2, e=2),
-                )
+        def close_cells(b, banks, c, eye):
+            for s in range(4):
+                cols = slice(c * BANK + s * P, c * BANK + (s + 1) * P)
+                nc.tensor.matmul(banks[c][:, s, :], pages[b % 2][:, cols], eye[:], start=False, stop=(s == 3), is_transpose=True)
+
+        def copy_turned(b, banks, c, copy):
+            copy(
+                out=z_t[b // 2][c][:, :, :, b % 2, :].rearrange("t u s (p e) -> t u s p e", e=2),
+                in_=banks[c][:].rearrange("t s (p u e) -> t u s p e", u=2, e=2),
+            )
+
+        def close_turned(b, banks, copies, eye, chunks=range(CHUNKS)):
+            for c in chunks:
+                close_cells(b, banks, c, eye)
+                copy_turned(b, banks, c, copies[c % 2])
+
+        eyes = []
 
         def identity_on(tag):
-            eye = keep.tile([P, P], F32, name="eye", tag=tag, align_bytes=64)
-            nc.scalar.copy(out=eye[:], in_=ident[:])
-            return eye
+            eyes.append(keep.tile([P, P], F32, name="eye", tag=tag, align_bytes=64))
+            nc.scalar.copy(out=eyes[-1][:], in_=ident[:])
+            return eyes[-1]
 
         def turn_back(h, c, copy, number):
             words = z_t[h][c][:].rearrange("t u s b x -> t (u s b x)").bitcast(F32)
@@ -321,53 +322,31 @@ def tile_list_rework_bay_scores_kernel(
         last = ROW_BLOCKS - 1
         on_scalar = (nc.scalar.copy, nc.scalar.copy)
         features(2, 0, BANK, h2, 0, 5)
-        banks = open_turned(0, (0, 1, 2, 3))
+        banks = open_turned(0, (0, 1, 2, 3), ident)
         close_turned(0, banks, on_scalar, ident)
         features(2, BANK, S, h2, 0, 0)
         fill_cells(2, 0, S, h2, 0)
-        banks = open_turned(1, (6, 1, 2, 3))
+        banks = open_turned(1, (6, 1, 2, 3), ident)
         features(last, 0, BANK, h3, 0, 0)
         close_turned(1, banks, on_scalar, ident)
-        acc = differences(last, BANK, S, 6)
-        nc.scalar.activation(out=h3[:, BANK:LAST_CUT], in_=acc[:, 0 : LAST_CUT - BANK], func=ACT.Abs)
-        fill_cells(last, 0, LAST_CUT, h3, 0)
+        features(last, BANK, S, h3, 0, 6)
+        fill_cells(last, 0, S, h3, 0)
         spare_banks, z_banks = (4, 5, 7, 0), (1, 2, 3, 6)
         z_codes.append(keep.tile([P, WIDE], U32, name="z_codes0", align_bytes=64))
         z_codes.append(keep.tile([P, WIDE], U32, name="z_codes1", align_bytes=64))
         for c in range(CHUNKS):
             turn_back(0, c, nc.scalar.copy, spare_banks[c])
-            if c == 1:
-                for early in range(2):
-                    quantize_z(0, early)
-                h_end = features_tile("h3_end", S - LAST_CUT, "z_t0_1")
-                nc.scalar.activation(out=h_end[:], in_=acc[:, LAST_CUT - BANK : BANK], func=ACT.Abs)
-                fill_cells(last, LAST_CUT, S, h_end, LAST_CUT)
-        banks = open_turned(2, z_banks)
-        last_banks = open_turned(last, spare_banks)
-        eye = identity_on("tol3")
-        close_turned(2, banks, on_scalar, eye)
-        banks = last_banks
-        early_weights = keep.tile([P, 2, PICK], F32, name="early_weights", tag="page0", align_bytes=64)
-        for n in range(2):
-            weigh(early_weights[:, n, :])
-        first = []
-        for c in range(2):
-            for k in range(2 - c):
-                warm = take_bank(z_banks[c], [P, 2 * P])
-                cols = slice(c * 2 * P, (c + 1) * 2 * P)
-                nc.tensor.matmul_mx(
-                    out=warm[:],
-                    lhsT=wo_codes[:, 0:P].bitcast(E4M3),
-                    lhsT_scale=wo_plane[:, 0:P],
-                    rhs=z_codes[0][:, cols].bitcast(E4M3),
-                    rhs_scale=z_plane[0][:, cols],
-                    start=True,
-                    stop=True,
-                )
-            first.append(take_bank(z_banks[c], [P, 2, 2 * P]))
-            half_scores(0, c, first[c])
-        for c in range(2, CHUNKS):
             quantize_z(0, c)
+        banks = open_turned(2, z_banks, ident)
+        close_turned(2, banks, on_scalar, identity_on("z_t0_3"), range(CHUNKS - 1))
+        close_cells(2, banks, CHUNKS - 1, eyes[0])
+        early_weights = keep.tile([P, 2 * PICK], F32, name="early_weights", tag="page0", align_bytes=64)
+        eye = identity_on("z_t0_3")
+        copy_turned(2, banks, CHUNKS - 1, nc.scalar.copy)
+        banks = open_turned(last, spare_banks, eye)
+        for n in range(2):
+            weigh(early_weights[:, n * PICK : (n + 1) * PICK])
+        first = []
         bays = [keep.tile([P, T2], F32, name="bays%d" % i, tag="tol%d" % (i + 1)) for i in range(2)]
         for page in bays:
             nc.gpsimd.memset(page[:], 0.0)
@@ -387,15 +366,15 @@ def tile_list_rework_bay_scores_kernel(
         ys = [keep.tile([P, T2], F32, name="y0", tag="y0")]
         close_turned(last, banks, by_turns, eye)
         for c in range(CHUNKS):
-            turn_back(1, c, by_turns[c == vector_back], spare_banks[c])
+            turn_back(1, c, by_turns[c == vector_back], z_banks[c])
             quantize_z(1, c)
-        for c in range(2, CHUNKS):
-            first.append(take_bank(z_banks[c], [P, 2, 2 * P]))
+        for c in range(CHUNKS):
+            first.append(take_bank(spare_banks[c], [P, 2, 2 * P]))
             half_scores(0, c, first[c])
         for c in range(CHUNKS):
             half_scores(1, c, first[c])
         for c in range(CHUNKS):
-            by_turns[c % 2](
+            by_turns[(c + 1) % 2](
                 out=ys[0][:, c * BANK : (c + 1) * BANK].rearrange("p (m g t) -> p m g t", m=2, g=2),
                 in_=first[c][:].rearrange("p g (m t) -> p m g t", m=2),
             )
@@ -413,7 +392,7 @@ def tile_list_rework_bay_scores_kernel(
             cells = y[:].rearrange("p (k g t) -> p g k t", g=2, t=P)
             for g, (codes, plane) in enumerate(groups):
                 for j in range(2):
-                    acc = take_bank(spare_banks[2 * g + j], [P, 4, P])
+                    acc = take_bank(z_banks[2 * g + j], [P, 4, P])
                     nc.tensor.matmul_mx(
                         out=acc[:].rearrange("p k t -> p (k t)"),
                         lhsT=wo_codes[:, n * P : (n + 1) * P].bitcast(E4M3),

@@ -248,9 +248,9 @@ def tile_list_rework_bay_scores_kernel(
         z_t = [[keep.tile([P, 2, 4, 2, HALF], BF16, name="z_t%d_%d" % (h, c), align_bytes=64) for c in range(CHUNKS)] for h in range(2)]
         z_bf = [[keep.tile([P, WIDE], BF16, name="z_bf%d_%d" % (h, c), align_bytes=64) for c in range(CHUNKS)] for h in range(2)]
 
-        def open_turned(b, numbers, eye):
+        def open_turned(b, numbers, eye, chunks=range(CHUNKS)):
             banks = []
-            for c in range(CHUNKS):
+            for c in chunks:
                 bank = take_bank(numbers[c], [P, 4, P])
                 for s in range(4):
                     cells = tols[b][:, c * BANK + s * P : c * BANK + (s + 1) * P]
@@ -343,7 +343,19 @@ def tile_list_rework_bay_scores_kernel(
         early_weights = keep.tile([P, 2 * PICK], F32, name="early_weights", tag="page0", align_bytes=64)
         eye = identity_on("z_t0_3")
         copy_turned(2, banks, CHUNKS - 1, nc.scalar.copy)
-        banks = open_turned(last, spare_banks, eye)
+        banks = open_turned(last, spare_banks, eye, range(2))
+        for k in range(3):
+            warm = take_bank(z_banks[CHUNKS - 1], [P, 2 * P])
+            nc.tensor.matmul_mx(
+                out=warm[:],
+                lhsT=wa_codes[last][:, 0:P].bitcast(E4M3),
+                lhsT_scale=wa_plane[last][:, 0:P],
+                rhs=wo_codes[:, 0 : 2 * P].bitcast(E4M3),
+                rhs_scale=wo_plane[:, 0 : 2 * P],
+                start=True,
+                stop=True,
+            )
+        banks.extend(open_turned(last, spare_banks, eye, range(2, CHUNKS)))
         for n in range(2):
             weigh(early_weights[:, n * PICK : (n + 1) * PICK])
         first = []

@@ -29,6 +29,7 @@ AHEAD = 1536
 PASS1_ROW = 8
 FIRST, SECOND = 256, 640
 LEAD = 352
+EARLY = 1
 
 
 def tile_list_rework_bay_scores_kernel(
@@ -111,12 +112,12 @@ def tile_list_rework_bay_scores_kernel(
         load_wa(3)
         load_tol(1)
         load_tol(2)
+        load_tol(3)
         wgo_sb = keep.tile([P, PICK], F32, name="wgo_sb")
         nc.sync.dma_start(out=wgo_sb[:], in_=wgo)
         bay_sb = keep.tile([P, OUT_BLOCKS], F32, name="bay_sb")
         with nc.allow_non_contiguous_dma(reason="one value of bay for each partition"):
             nc.sync.dma_start(out=bay_sb[:], in_=bay.rearrange("(n p) -> p n", p=P))
-        load_tol(3)
         wo_codes = keep.tile([P, N], U32, name="wo_codes", align_bytes=64)
         nc.sync.dma_start(out=wo_codes[:].bitcast(I32), in_=wo_words[0].rearrange("p c i -> p (c i)").bitcast(I32))
 
@@ -245,12 +246,13 @@ def tile_list_rework_bay_scores_kernel(
         h2 = h_late[:, S - BANK : 2 * S - BANK]
         h3 = features_tile("h3", S, "h_even")
 
+
         z_t = [[keep.tile([P, 2, 4, 2, HALF], BF16, name="z_t%d_%d" % (h, c), align_bytes=64) for c in range(CHUNKS)] for h in range(2)]
         z_bf = [[keep.tile([P, WIDE], BF16, name="z_bf%d_%d" % (h, c), align_bytes=64) for c in range(CHUNKS)] for h in range(2)]
 
-        def open_turned(b, numbers, eye, chunks=range(CHUNKS)):
+        def open_turned(b, numbers, eye):
             banks = []
-            for c in chunks:
+            for c in range(CHUNKS):
                 bank = take_bank(numbers[c], [P, 4, P])
                 for s in range(4):
                     cells = tols[b][:, c * BANK + s * P : c * BANK + (s + 1) * P]
@@ -329,36 +331,38 @@ def tile_list_rework_bay_scores_kernel(
         banks = open_turned(1, (6, 1, 2, 3), ident)
         features(last, 0, BANK, h3, 0, 0)
         close_turned(1, banks, on_scalar, ident)
-        features(last, BANK, S, h3, 0, 6)
-        fill_cells(last, 0, S, h3, 0)
         spare_banks, z_banks = (4, 5, 7, 0), (1, 2, 3, 6)
         z_codes.append(keep.tile([P, WIDE], U32, name="z_codes0", align_bytes=64))
         z_codes.append(keep.tile([P, WIDE], U32, name="z_codes1", align_bytes=64))
         for c in range(CHUNKS):
             turn_back(0, c, nc.scalar.copy, spare_banks[c])
             quantize_z(0, c)
+            if c == EARLY - 1:
+                features(last, BANK, S, h3, 0, 6)
+                fill_cells(last, 0, S, h3, 0)
         banks = open_turned(2, z_banks, ident)
-        close_turned(2, banks, on_scalar, identity_on("z_t0_3"), range(CHUNKS - 1))
-        close_cells(2, banks, CHUNKS - 1, eyes[0])
-        early_weights = keep.tile([P, 2 * PICK], F32, name="early_weights", tag="page0", align_bytes=64)
         eye = identity_on("z_t0_3")
+        close_turned(2, banks, on_scalar, eye, range(CHUNKS - 1))
+        close_cells(2, banks, CHUNKS - 1, eye)
+        last_banks = open_turned(last, spare_banks, eye)
+        early_weights = keep.tile([P, 2 * PICK], F32, name="early_weights", tag="page0", align_bytes=64)
+        weigh(early_weights[:, 0:PICK])
         copy_turned(2, banks, CHUNKS - 1, nc.scalar.copy)
-        banks = open_turned(last, spare_banks, eye, range(2))
+        eye = identity_on("z_t0_3")
+        weigh(early_weights[:, PICK : 2 * PICK])
+        banks = last_banks
+        first = [take_bank(z_banks[CHUNKS - 1], [P, 2, 2 * P])]
         for k in range(3):
-            warm = take_bank(z_banks[CHUNKS - 1], [P, 2 * P])
             nc.tensor.matmul_mx(
-                out=warm[:],
-                lhsT=wa_codes[last][:, 0:P].bitcast(E4M3),
-                lhsT_scale=wa_plane[last][:, 0:P],
-                rhs=wo_codes[:, 0 : 2 * P].bitcast(E4M3),
-                rhs_scale=wo_plane[:, 0 : 2 * P],
+                out=first[0][:, 0, :],
+                lhsT=wo_codes[:, 0:P].bitcast(E4M3),
+                lhsT_scale=wo_plane[:, 0:P],
+                rhs=z_codes[0][:, 0 : 2 * P].bitcast(E4M3),
+                rhs_scale=z_plane[0][:, 0 : 2 * P],
                 start=True,
                 stop=True,
             )
-        banks.extend(open_turned(last, spare_banks, eye, range(2, CHUNKS)))
-        for n in range(2):
-            weigh(early_weights[:, n * PICK : (n + 1) * PICK])
-        first = []
+        half_scores(0, 0, first[0])
         bays = [keep.tile([P, T2], F32, name="bays%d" % i, tag="tol%d" % (i + 1)) for i in range(2)]
         for page in bays:
             nc.gpsimd.memset(page[:], 0.0)
@@ -378,9 +382,9 @@ def tile_list_rework_bay_scores_kernel(
         ys = [keep.tile([P, T2], F32, name="y0", tag="y0")]
         close_turned(last, banks, by_turns, eye)
         for c in range(CHUNKS):
-            turn_back(1, c, by_turns[c == vector_back], z_banks[c])
+            turn_back(1, c, by_turns[c == vector_back], (z_banks[: CHUNKS - 1] + spare_banks[:1])[c])
             quantize_z(1, c)
-        for c in range(CHUNKS):
+        for c in range(EARLY, CHUNKS):
             first.append(take_bank(spare_banks[c], [P, 2, 2 * P]))
             half_scores(0, c, first[c])
         for c in range(CHUNKS):

@@ -61,7 +61,7 @@ def tile_list_rework_bay_scores_kernel(
         ident = keep.tile([P, P], F32, name="ident")
         make_identity(nc, ident[:])
 
-        tab = [keep.tile([P, T], U32, name="tab0"), shared.tile([P, T], U32, name="tab1", align_bytes=64, offset=0)]
+        tab = [keep.tile([P, T], U32, name="tab0"), keep.tile([P, T], U32, name="tab1", tag="tab1", align_bytes=64)]
         wa_rows = wa.rearrange("(a p j) c -> a p j c", a=PASSES, j=4)
         wa_raw = [keep.tile([P, PASSES, 4, P], F32, name="wa_raw%d" % b, tag="wa_raw%d" % b, align_bytes=64) for b in range(ROW_BLOCKS)]
         wb_codes = [keep.tile([P, PASSES, 2 * w], U8, name="wb_codes%d" % i, align_bytes=64) for i, w in enumerate((P, H - P))]
@@ -127,7 +127,8 @@ def tile_list_rework_bay_scores_kernel(
         def entries(c0, c1):
             return slice(c0 // 16, c1 // 16)
 
-        wa_bf = [keep.tile([P, P * PASSES * 4], BF16, name="wa_bf%d" % b, align_bytes=64) for b in range(ROW_BLOCKS)]
+        wa_bf = [keep.tile([P, P * PASSES * 4], BF16, name="wa_bf%d" % b, tag="wa_bf%d" % b, align_bytes=64) for b in (0, 1, 3)]
+        wa_bf.insert(2, shared.tile([P, P * PASSES * 4], BF16, name="wa_bf2", align_bytes=64, offset=2 * WIDE - 64))
         wa_codes = [keep.tile([P, P * PASSES], U32, name="wa_codes%d" % b, align_bytes=64) for b in range(ROW_BLOCKS)]
         wa_plane = [keep.tile([P, P * PASSES], U8, name="wa_plane%d" % b, align_bytes=64) for b in range(ROW_BLOCKS)]
 
@@ -200,27 +201,8 @@ def tile_list_rework_bay_scores_kernel(
         v_codes.append(keep.tile([P, S], U32, name="v_codes1", align_bytes=64))
         gather_words(1)
         negate_gain(0, FIRST)
-        wo_plane = shared.tile([P, N], U8, name="wo_plane", align_bytes=64, offset=0)
-        pad_plane = shared.tile([P, P], U8, name="pad_plane", align_bytes=64, offset=N)
-        z_plane = [shared.tile([P, WIDE], U8, name="z_plane%d" % h, align_bytes=64, offset=(1 + h) * WIDE) for h in range(2)]
-        pad_codes = shared.tile([P, 4, P], U32, name="pad_codes", align_bytes=64, offset=3 * WIDE)
-        pages.append(shared.tile([P, T2], F32, name="page1", align_bytes=64, offset=5 * WIDE))
+        pages.append(keep.tile([P, T2], F32, name="page1", tag="tab1", align_bytes=64))
         nc.gpsimd.memset(pages[1][:], 0.0)
-        for zeroed in (wo_plane, pad_codes, pad_plane, z_plane[0], z_plane[1]):
-            nc.gpsimd.memset(zeroed[:].bitcast(I32), 0)
-        for q in range(4):
-            nc.sync.dma_start(
-                out=wo_plane[32 * q : 32 * q + 4, :].bitcast(I32),
-                in_=wo_scales[0, 4 * q : 4 * q + 4, :].bitcast(I32),
-            )
-        wo_first = wo_words[0].rearrange("(h p) c i -> p h (c i)", h=2)[:, :, 0 : 4 * P].bitcast(I32)
-        for g in range(2):
-            nc.sync.dma_start(out=pad_codes[g * HALF : (g + 1) * HALF, g:4:2, :].bitcast(I32), in_=wo_first)
-        for q in range(4):
-            r0 = 4 * ((q + 2) % 4)
-            nc.sync.dma_start(out=pad_plane[32 * q : 32 * q + 4, :].bitcast(I32), in_=wo_scales[0, r0 : r0 + 4, 0:P].bitcast(I32))
-        nc.sync.dma_start(idx3[:], offs3)
-        nc.sync.dma_start(idx4[:], offs4)
 
         h_head = features_tile("h0_head", SECOND, "h_even")
         features(0, 0, FIRST, h_head, 0, 4)
@@ -237,6 +219,27 @@ def tile_list_rework_bay_scores_kernel(
         features(1, 0, BANK, h_head, 0, 7)
         round_wa(2)
         quantize_wa(2)
+        z_planes = shared.tile([P, 2 * WIDE], U8, name="z_planes", align_bytes=64, offset=0)
+        z_plane = [z_planes[:, h * WIDE : (h + 1) * WIDE] for h in range(2)]
+        wo_plane = shared.tile([P, N], U8, name="wo_plane", align_bytes=64, offset=2 * WIDE)
+        pad_plane = shared.tile([P, P], U8, name="pad_plane", align_bytes=64, offset=2 * WIDE + N)
+        pad_codes = shared.tile([P, 4, P], U32, name="pad_codes", align_bytes=64, offset=2 * WIDE + N + P)
+        for zeroed in (wo_plane, pad_codes, pad_plane, z_planes):
+            nc.gpsimd.memset(zeroed[:].bitcast(I32), 0)
+        for q in range(4):
+            nc.sync.dma_start(
+                out=wo_plane[32 * q : 32 * q + 4, :].bitcast(I32),
+                in_=wo_scales[0, 4 * q : 4 * q + 4, :].bitcast(I32),
+            )
+        wo_first = wo_words[0].rearrange("(h p) c i -> p h (c i)", h=2)[:, :, 0 : 4 * P].bitcast(I32)
+        for g in range(2):
+            nc.sync.dma_start(out=pad_codes[g * HALF : (g + 1) * HALF, g:4:2, :].bitcast(I32), in_=wo_first)
+        for q in range(4):
+            r0 = 4 * ((q + 2) % 4)
+            nc.sync.dma_start(out=pad_plane[32 * q : 32 * q + 4, :].bitcast(I32), in_=wo_scales[0, r0 : r0 + 4, 0:P].bitcast(I32))
+        nc.sync.dma_start(idx3[:], offs3)
+        nc.sync.dma_start(idx4[:], offs4)
+
         fill_cells(1, 0, BANK, h_head, 0)
         round_wa(3)
         quantize_wa(3)
@@ -363,7 +366,7 @@ def tile_list_rework_bay_scores_kernel(
                 stop=True,
             )
         half_scores(0, 0, first[0])
-        bays = [keep.tile([P, T2], F32, name="bays%d" % i, tag="tol%d" % (i + 1)) for i in range(2)]
+        bays = [keep.tile([P, T2], F32, name="bays0", tag="tol1"), keep.tile([P, T2], F32, name="bays1", tag="wa_bf3", align_bytes=64)]
         for page in bays:
             nc.gpsimd.memset(page[:], 0.0)
 
@@ -404,7 +407,7 @@ def tile_list_rework_bay_scores_kernel(
         squares = keep.tile([P, PICK], F32, name="squares")
 
         def products(n):
-            y = keep.tile([P, T2], F32, name="y%d" % n, tag="y%d" % (n % 4))
+            y = keep.tile([P, T2], F32, name="y%d" % n, tag=("y0", "y1", "tol2", "y3")[n % 4])
             cells = y[:].rearrange("p (k g t) -> p g k t", g=2, t=P)
             for g, (codes, plane) in enumerate(groups):
                 for j in range(2):

@@ -54,8 +54,7 @@ def tile_list_rework_bay_scores_kernel(
         v_plane = keep.tile([P, S], U8, name="v_plane", align_bytes=64)
         v_plane1 = keep.tile([P, S], U8, name="v_plane1", align_bytes=64)
         pages = [keep.tile([P, T2], F32, name="page0", tag="page0", align_bytes=64)]
-        nc.gpsimd.memset(tab_plane[:].bitcast(I32), 0)
-        for zeroed in (wb_plane, v_plane1):
+        for zeroed in (tab_plane, wb_plane, v_plane1):
             nc.vector.memset(zeroed[:].bitcast(I32), 0)
         nc.vector.memset(pages[0][:], 0.0)
         ident = keep.tile([P, P], F32, name="ident")

@@ -60,9 +60,11 @@ def tile_list_rework_bay_scores_kernel(
         ident = keep.tile([P, P], F32, name="ident")
         make_identity(nc, ident[:])
 
-        tab = [keep.tile([P, T], U32, name="tab0"), keep.tile([P, T], U32, name="tab1", tag="tab1", align_bytes=64)]
+        tab = [keep.tile([P, T], U32, name="tab0", tag="tab0", align_bytes=64), keep.tile([P, T], U32, name="tab1", tag="tab1", align_bytes=64)]
         wa_rows = wa.rearrange("(a p j) c -> a p j c", a=PASSES, j=4)
-        wa_raw = [keep.tile([P, PASSES, 4, P], F32, name="wa_raw%d" % b, tag="wa_raw%d" % b, align_bytes=64) for b in range(ROW_BLOCKS)]
+        wa_first = keep.tile([P, PASSES, 4, P], F32, name="wa_first", tag="wa_first", align_bytes=64)
+        wa_rest = keep.tile([P, PASSES, 4, H - P], F32, name="wa_rest")
+        wa_raw = [wa_first[:]] + [wa_rest[:, :, :, c0 : c0 + P] for c0 in range(0, H - P, P)]
         wb_codes = [keep.tile([P, PASSES, 2 * w], U8, name="wb_codes%d" % i, align_bytes=64) for i, w in enumerate((P, H - P))]
         wb_rows = wb_words.rearrange("a p n -> p a n")
         gain = keep.tile([P, S], F32, name="gain")
@@ -72,15 +74,14 @@ def tile_list_rework_bay_scores_kernel(
             words = tab_words[a].rearrange("p t i -> p (t i)").bitcast(I32)
             nc.sync.dma_start(out=tab[a][:, t0:t1].bitcast(I32), in_=words[:, t0:t1])
 
-        def load_wa(b, passes=range(PASSES)):
-            for a in passes:
-                nc.sync.dma_start(out=wa_raw[b][:, a, :, :], in_=wa_rows[a][:, :, b * P : (b + 1) * P])
+        def load_wa(tile, a, c0, c1):
+            nc.sync.dma_start(out=tile[:, a, :, :], in_=wa_rows[a][:, :, c0:c1])
 
         def load_tol(b):
             nc.sync.dma_start(out=tols[b][:], in_=tol[b * P : (b + 1) * P, :])
 
         nc.sync.dma_start(idx[:], offs)
-        load_wa(0, [0])
+        load_wa(wa_first, 0, 0, P)
         nc.sync.dma_start(out=tab_plane[PASS1_ROW : PASS1_ROW + 16, :].bitcast(I32), in_=tab_scales[1].bitcast(I32))
         for q in range(4):
             nc.sync.dma_start(
@@ -93,7 +94,7 @@ def tile_list_rework_bay_scores_kernel(
                 out=wb_plane[32 * q : 32 * q + 4, :, :].bitcast(I32),
                 in_=wb_scales[:, 4 * q : 4 * q + 4, :].rearrange("a r c -> r a c").bitcast(I32),
             )
-        load_wa(0, [1])
+        load_wa(wa_first, 1, 0, P)
         nc.sync.dma_start(out=wb_codes[0][:].bitcast(I32), in_=wb_rows[:, :, 0 : 2 * P].bitcast(I32))
         load_tab(1, 0, AHEAD)
         nc.vector.tensor_copy(v_plane[:], tab_plane[:].indirect(idx[:]))
@@ -101,14 +102,13 @@ def tile_list_rework_bay_scores_kernel(
             r0 = PASS1_ROW + 4 * q
             nc.sync.dma_start(out=v_plane1[32 * q : 32 * q + 4, :].bitcast(I32), in_=v_plane[r0 : r0 + 4, :].bitcast(I32))
         load_tab(1, AHEAD, T)
-        nc.sync.dma_start(out=gain[:, 0:FIRST], in_=wgs[:, 0:FIRST])
+        nc.sync.dma_start(out=gain[:, 0:SECOND], in_=wgs[:, 0:SECOND])
         nc.sync.dma_start(idx2[:], offs2)
-        nc.sync.dma_start(out=gain[:, FIRST:S], in_=wgs[:, FIRST:S])
-        load_wa(1)
         nc.sync.dma_start(out=wb_codes[1][:].bitcast(I32), in_=wb_rows[:, :, 2 * P : 2 * H].bitcast(I32))
-        load_wa(2)
+        for a in range(PASSES):
+            load_wa(wa_rest, a, P, H)
+        nc.sync.dma_start(out=gain[:, SECOND:S], in_=wgs[:, SECOND:S])
         load_tol(0)
-        load_wa(3)
         load_tol(1)
         load_tol(2)
         load_tol(3)
@@ -132,11 +132,11 @@ def tile_list_rework_bay_scores_kernel(
         wa_plane = [keep.tile([P, P * PASSES], U8, name="wa_plane%d" % b, align_bytes=64) for b in range(ROW_BLOCKS)]
 
         def round_wa(b):
-            step = 1 if b == 0 else PASSES
+            step = 1 if b < 2 else PASSES
             for a in range(0, PASSES, step):
                 nc.scalar.activation(
                     out=wa_bf[b][:].rearrange("p (a c j) -> p a c j", a=PASSES, j=4)[:, a : a + step],
-                    in_=wa_raw[b][:].rearrange("p a j c -> p a c j")[:, a : a + step],
+                    in_=wa_raw[b].rearrange("p a j c -> p a c j")[:, a : a + step],
                     func=ACT.Copy,
                     scale=-1.0,
                 )
@@ -207,17 +207,18 @@ def tile_list_rework_bay_scores_kernel(
         features(0, 0, FIRST, h_head, 0, 4)
         fill_cells(0, 0, FIRST, h_head, 0)
         features(0, FIRST, SECOND, h_head, 0, 5)
-        negate_gain(FIRST, S)
+        negate_gain(FIRST, SECOND)
         fill_cells(0, FIRST, SECOND, h_head, 0)
+        h_last = features_tile("h0_last", S - SECOND, "wa_first")
+        features(0, SECOND, S, h_last, SECOND, 6)
         round_wa(1)
         quantize_wa(1)
-        h_last = features_tile("h0_last", S - SECOND, "wa_raw1")
-        features(0, SECOND, S, h_last, SECOND, 6)
+        negate_gain(SECOND, S)
         fill_cells(0, SECOND, S, h_last, SECOND)
-        h_head = features_tile("h1_head", BANK, "h_odd")
-        features(1, 0, BANK, h_head, 0, 7)
         round_wa(2)
         quantize_wa(2)
+        h_head = features_tile("h1_head", BANK, "h_odd")
+        features(1, 0, BANK, h_head, 0, 7)
         z_planes = shared.tile([P, 2 * WIDE], U8, name="z_planes", align_bytes=64, offset=0)
         z_plane = [z_planes[:, h * WIDE : (h + 1) * WIDE] for h in range(2)]
         wo_plane = shared.tile([P, N], U8, name="wo_plane", align_bytes=64, offset=2 * WIDE)
@@ -242,7 +243,7 @@ def tile_list_rework_bay_scores_kernel(
         fill_cells(1, 0, BANK, h_head, 0)
         round_wa(3)
         quantize_wa(3)
-        h_late = features_tile("h_late", 2 * S - BANK, "wa_raw3")
+        h_late = features_tile("h_late", 2 * S - BANK, "tab0")
         features(1, BANK, S, h_late, BANK, 4)
         fill_cells(1, BANK, S, h_late, BANK)
         h2 = h_late[:, S - BANK : 2 * S - BANK]
@@ -326,21 +327,21 @@ def tile_list_rework_bay_scores_kernel(
         last = ROW_BLOCKS - 1
         on_scalar = (nc.scalar.copy, nc.scalar.copy)
         features(2, 0, BANK, h2, 0, 5)
+        features(2, BANK, S, h2, 0, 6)
         banks = open_turned(0, (0, 1, 2, 3), ident)
         close_turned(0, banks, on_scalar, ident)
-        features(2, BANK, S, h2, 0, 0)
         fill_cells(2, 0, S, h2, 0)
-        banks = open_turned(1, (6, 1, 2, 3), ident)
+        banks = open_turned(1, (7, 4, 5, 6), ident)
         features(last, 0, BANK, h3, 0, 0)
         close_turned(1, banks, on_scalar, ident)
-        spare_banks, z_banks = (4, 5, 7, 0), (1, 2, 3, 6)
+        spare_banks, z_banks = (1, 2, 3, 0), (4, 5, 6, 7)
         z_codes.append(keep.tile([P, WIDE], U32, name="z_codes0", align_bytes=64))
         z_codes.append(keep.tile([P, WIDE], U32, name="z_codes1", align_bytes=64))
         for c in range(CHUNKS):
             turn_back(0, c, nc.scalar.copy, spare_banks[c])
             quantize_z(0, c)
             if c == EARLY - 1:
-                features(last, BANK, S, h3, 0, 6)
+                features(last, BANK, S, h3, 0, 7)
                 fill_cells(last, 0, S, h3, 0)
         banks = open_turned(2, z_banks, ident)
         eye = identity_on("z_t0_3")

from contextlib import ExitStack

import concourse.mybir as mybir
from concourse.masks import make_identity

K, H, N, T, S, T2, PICK = 1024, 512, 768, 2048, 1024, 2048, 1024
FLOPS = 2 * 2 * K * H * S + 2 * H * N * T2

F32 = mybir.dt.float32
BF16 = mybir.dt.bfloat16
I32 = mybir.dt.int32
U32 = mybir.dt.uint32
U16 = mybir.dt.uint16
U8 = mybir.dt.uint8
E4M3 = mybir.dt.float8_e4m3fn_x4
E2M1 = mybir.dt.float4_e2m1fn_x4
ACT = mybir.ActivationFunctionType
MULT = mybir.AluOpType.mult

P = 128
BANK = 512
PASSES = K // 512
ROW_BLOCKS = H // P
OUT_BLOCKS = N // P
CHUNKS = T2 // BANK
HALF = P // 2
WIDE = T2 // 2
AHEAD = 1536
PASS1_ROW = 8
FIRST, SECOND = 256, 640
LEAD = 352
EARLY = 1


def tile_list_rework_bay_scores_kernel(
    tc, tab_words, tab_scales, offs, wa, wb_words, wb_scales, offs2, wgs, tol,
    wo_words, wo_scales, offs3, bay, offs4, wgo, out,
):
    nc = tc.nc
    with ExitStack() as ctx:
        lists = ctx.enter_context(tc.tile_pool(name="lists", bufs=1))
        keep = ctx.enter_context(tc.tile_pool(name="keep", bufs=1))
        ring = ctx.enter_context(tc.tile_pool(name="ring", bufs=3))
        shared = ctx.enter_context(tc.tile_pool(name="shared", bufs=1))
        psum = ctx.enter_context(tc.psum_pool(name="psum", bufs=1))

        idx = lists.tile([P, S // 16], U16, name="idx")
        idx2 = lists.tile([P, S // 16], U16, name="idx2")
        idx3 = lists.tile([P, PICK // 16], U16, name="idx3")
        idx4 = lists.tile([P, PICK // 16], U16, name="idx4")

        tab_plane = keep.tile([P, T], U8, name="tab_plane", align_bytes=64)
        wb_plane = keep.tile([P, PASSES, H], U8, name="wb_plane", align_bytes=64)
        v_plane = keep.tile([P, S], U8, name="v_plane", align_bytes=64)
        v_plane1 = keep.tile([P, S], U8, name="v_plane1", align_bytes=64)
        pages = [keep.tile([P, T2], F32, name="page0", tag="page0", align_bytes=64)]
        for zeroed in (tab_plane, wb_plane, v_plane1):
            nc.vector.memset(zeroed[:].bitcast(I32), 0)
        nc.vector.memset(pages[0][:], 0.0)
        ident = keep.tile([P, P], F32, name="ident")
        make_identity(nc, ident[:])

        tab = [keep.tile([P, T], U32, name="tab0", tag="tab0", align_bytes=64), keep.tile([P, T], U32, name="tab1", tag="tab1", align_bytes=64)]
        wa_rows = wa.rearrange("(a p j) c -> a p j c", a=PASSES, j=4)
        wa_first = keep.tile([P, PASSES, 4, P], F32, name="wa_first", tag="wa_first", align_bytes=64)
        wa_rest = keep.tile([P, PASSES, 4, H - P], F32, name="wa_rest")
        wa_raw = [wa_first[:]] + [wa_rest[:, :, :, c0 : c0 + P] for c0 in range(0, H - P, P)]
        wb_codes = [keep.tile([P, PASSES, 2 * w], U8, name="wb_codes%d" % i, align_bytes=64) for i, w in enumerate((P, H - P))]
        wb_rows = wb_words.rearrange("a p n -> p a n")
        gain = keep.tile([P, S], F32, name="gain")
        tols = [keep.tile([P, T2], F32, name="tol%d" % b) for b in range(ROW_BLOCKS)]

        def load_tab(a, t0, t1):
            words = tab_words[a].rearrange("p t i -> p (t i)").bitcast(I32)
            nc.sync.dma_start(out=tab[a][:, t0:t1].bitcast(I32), in_=words[:, t0:t1])

        def load_wa(tile, a, c0, c1):
            nc.sync.dma_start(out=tile[:, a, :, :], in_=wa_rows[a][:, :, c0:c1])

        def load_tol(b):
            nc.sync.dma_start(out=tols[b][:], in_=tol[b * P : (b + 1) * P, :])

        nc.sync.dma_start(idx[:], offs)
        load_wa(wa_first, 0, 0, P)
        nc.sync.dma_start(out=tab_plane[PASS1_ROW : PASS1_ROW + 16, :].bitcast(I32), in_=tab_scales[1].bitcast(I32))
        for q in range(4):
            nc.sync.dma_start(
                out=tab_plane[32 * q : 32 * q + 4, :].bitcast(I32),
                in_=tab_scales[0, 4 * q : 4 * q + 4, :].bitcast(I32),
            )
        load_tab(0, 0, T)
        for q in range(4):
            nc.sync.dma_start(
                out=wb_plane[32 * q : 32 * q + 4, :, :].bitcast(I32),
                in_=wb_scales[:, 4 * q : 4 * q + 4, :].rearrange("a r c -> r a c").bitcast(I32),
            )
        load_wa(wa_first, 1, 0, P)
        nc.sync.dma_start(out=wb_codes[0][:].bitcast(I32), in_=wb_rows[:, :, 0 : 2 * P].bitcast(I32))
        load_tab(1, 0, AHEAD)
        nc.vector.tensor_copy(v_plane[:], tab_plane[:].indirect(idx[:]))
        for q in range(4):
            r0 = PASS1_ROW + 4 * q
            nc.sync.dma_start(out=v_plane1[32 * q : 32 * q + 4, :].bitcast(I32), in_=v_plane[r0 : r0 + 4, :].bitcast(I32))
        load_tab(1, AHEAD, T)
        nc.sync.dma_start(out=gain[:, 0:SECOND], in_=wgs[:, 0:SECOND])
        nc.sync.dma_start(idx2[:], offs2)
        nc.sync.dma_start(out=wb_codes[1][:].bitcast(I32), in_=wb_rows[:, :, 2 * P : 2 * H].bitcast(I32))
        for a in range(PASSES):
            load_wa(wa_rest, a, P, H)
        nc.sync.dma_start(out=gain[:, SECOND:S], in_=wgs[:, SECOND:S])
        load_tol(0)
        load_tol(1)
        load_tol(2)
        load_tol(3)
        wgo_sb = keep.tile([P, PICK], F32, name="wgo_sb")
        nc.sync.dma_start(out=wgo_sb[:], in_=wgo)
        bay_sb = keep.tile([P, OUT_BLOCKS], F32, name="bay_sb")
        with nc.allow_non_contiguous_dma(reason="one value of bay for each partition"):
            nc.sync.dma_start(out=bay_sb[:], in_=bay.rearrange("(n p) -> p n", p=P))
        wo_codes = keep.tile([P, N], U32, name="wo_codes", align_bytes=64)
        nc.sync.dma_start(out=wo_codes[:].bitcast(I32), in_=wo_words[0].rearrange("p c i -> p (c i)").bitcast(I32))

        v_codes = [keep.tile([P, S], U32, name="v_codes0", align_bytes=64)]
        v_planes = (v_plane, v_plane1)

        def entries(c0, c1):
            return slice(c0 // 16, c1 // 16)

        wa_bf = [keep.tile([P, P * PASSES * 4], BF16, name="wa_bf%d" % b, tag="wa_bf%d" % b, align_bytes=64) for b in (0, 1, 3)]
        wa_bf.insert(2, shared.tile([P, P * PASSES * 4], BF16, name="wa_bf2", align_bytes=64, offset=2 * WIDE - 64))
        wa_codes = [keep.tile([P, P * PASSES], U32, name="wa_codes%d" % b, align_bytes=64) for b in range(ROW_BLOCKS)]
        wa_plane = [keep.tile([P, P * PASSES], U8, name="wa_plane%d" % b, align_bytes=64) for b in range(ROW_BLOCKS)]

        def round_wa(b):
            step = 1 if b < 2 else PASSES
            for a in range(0, PASSES, step):
                nc.scalar.activation(
                    out=wa_bf[b][:].rearrange("p (a c j) -> p a c j", a=PASSES, j=4)[:, a : a + step],
                    in_=wa_raw[b].rearrange("p a j c -> p a c j")[:, a : a + step],
                    func=ACT.Copy,
                    scale=-1.0,
                )

        def quantize_wa(b):
            nc.vector.quantize_mx(out=wa_codes[b][:].bitcast(E4M3), scales=wa_plane[b][:], in_=wa_bf[b][:])

        def take_bank(number, shape):
            return psum.tile(shape, F32, name="bank", tag="bank%d" % number)

        def differences(b, c0, c1, number):
            acc = take_bank(number, [P, BANK])
            step = BANK if c1 - c0 == BANK else P
            pairs = [(is_wa, a) for is_wa in (False, True) for a in range(PASSES)]
            if b == 0:
                pairs = sorted(pairs, key=lambda pair: pair[1])
            passes = [(is_wa, a, g0) for is_wa, a in pairs for g0 in range(c0, c1, step)]
            wb_tile, wb_col = (wb_codes[0], 0) if b == 0 else (wb_codes[1], (b - 1) * P)
            for k, (is_wa, a, g0) in enumerate(passes):
                cols = slice(g0, g0 + step)
                if is_wa:
                    codes = wa_codes[b][:, a * P : (a + 1) * P].bitcast(E4M3)
                    scale = wa_plane[b][:, a * P : (a + 1) * P]
                else:
                    codes = wb_tile[:, a, 2 * wb_col : 2 * (wb_col + P)].bitcast(E2M1)
                    scale = wb_plane[:, a, b * P : (b + 1) * P]
                nc.tensor.matmul_mx(
                    out=acc[:, g0 - c0 : g0 - c0 + step],
                    lhsT=codes,
                    lhsT_scale=scale,
                    rhs=v_codes[a][:, cols].bitcast(E4M3),
                    rhs_scale=v_planes[a][:, cols],
                    start=(k == 0),
                    stop=(k == len(passes) - 1),
                )
            return acc

        def features(b, c0, c1, feat, f0, number):
            acc = differences(b, c0, c1, number)
            nc.scalar.activation(out=feat[:, c0 - f0 : c1 - f0], in_=acc[:, 0 : c1 - c0], func=ACT.Abs)

        def negate_gain(c0, c1):
            nc.scalar.activation(out=gain[:, c0:c1], in_=gain[:, c0:c1], func=ACT.Copy, scale=-1.0)

        def fill_cells(b, c0, c1, feat, f0):
            window = pages[b % 2][:].indirect(idx2[:, entries(c0, c1)])
            nc.vector.tensor_tensor(window, feat[:, c0 - f0 : c1 - f0], gain[:, c0:c1], MULT)

        def features_tile(name, width, tag):
            return keep.tile([P, width], F32, name=name, tag=tag, align_bytes=64)

        cuts = (0, FIRST, SECOND, S)

        def gather_words(a):
            for c0, c1 in zip(cuts, cuts[1:]):
                nc.vector.tensor_copy(v_codes[a][:, c0:c1], tab[a][:].indirect(idx[:, entries(c0, c1)]))

        gather_words(0)
        round_wa(0)
        quantize_wa(0)
        v_codes.append(keep.tile([P, S], U32, name="v_codes1", align_bytes=64))
        gather_words(1)
        negate_gain(0, FIRST)
        pages.append(keep.tile([P, T2], F32, name="page1", tag="tab1", align_bytes=64))
        nc.gpsimd.memset(pages[1][:], 0.0)

        h_head = features_tile("h0_head", SECOND, "h_even")
        features(0, 0, FIRST, h_head, 0, 4)
        fill_cells(0, 0, FIRST, h_head, 0)
        features(0, FIRST, SECOND, h_head, 0, 5)
        negate_gain(FIRST, SECOND)
        fill_cells(0, FIRST, SECOND, h_head, 0)
        h_last = features_tile("h0_last", S - SECOND, "wa_first")
        features(0, SECOND, S, h_last, SECOND, 6)
        round_wa(1)
        quantize_wa(1)
        negate_gain(SECOND, S)
        fill_cells(0, SECOND, S, h_last, SECOND)
        round_wa(2)
        quantize_wa(2)
        h_head = features_tile("h1_head", BANK, "h_odd")
        features(1, 0, BANK, h_head, 0, 7)
        z_planes = shared.tile([P, 2 * WIDE], U8, name="z_planes", align_bytes=64, offset=0)
        z_plane = [z_planes[:, h * WIDE : (h + 1) * WIDE] for h in range(2)]
        wo_plane = shared.tile([P, N], U8, name="wo_plane", align_bytes=64, offset=2 * WIDE)
        pad_plane = shared.tile([P, P], U8, name="pad_plane", align_bytes=64, offset=2 * WIDE + N)
        pad_codes = shared.tile([P, 4, P], U32, name="pad_codes", align_bytes=64, offset=2 * WIDE + N + P)
        for zeroed in (wo_plane, pad_codes, pad_plane, z_planes):
            nc.gpsimd.memset(zeroed[:].bitcast(I32), 0)
        for q in range(4):
            nc.sync.dma_start(
                out=wo_plane[32 * q : 32 * q + 4, :].bitcast(I32),
                in_=wo_scales[0, 4 * q : 4 * q + 4, :].bitcast(I32),
            )
        wo_first = wo_words[0].rearrange("(h p) c i -> p h (c i)", h=2)[:, :, 0 : 4 * P].bitcast(I32)
        for g in range(2):
            nc.sync.dma_start(out=pad_codes[g * HALF : (g + 1) * HALF, g:4:2, :].bitcast(I32), in_=wo_first)
        for q in range(4):
            r0 = 4 * ((q + 2) % 4)
            nc.sync.dma_start(out=pad_plane[32 * q : 32 * q + 4, :].bitcast(I32), in_=wo_scales[0, r0 : r0 + 4, 0:P].bitcast(I32))
        nc.sync.dma_start(idx3[:], offs3)
        nc.sync.dma_start(idx4[:], offs4)

        fill_cells(1, 0, BANK, h_head, 0)
        round_wa(3)
        quantize_wa(3)
        h_late = features_tile("h_late", 2 * S - BANK, "tab0")
        features(1, BANK, S, h_late, BANK, 4)
        fill_cells(1, BANK, S, h_late, BANK)
        h2 = h_late[:, S - BANK : 2 * S - BANK]
        h3 = features_tile("h3", S, "h_even")


        z_t = [[keep.tile([P, 2, 4, 2, HALF], BF16, name="z_t%d_%d" % (h, c), align_bytes=64) for c in range(CHUNKS)] for h in range(2)]
        z_bf = [[keep.tile([P, WIDE], BF16, name="z_bf%d_%d" % (h, c), align_bytes=64) for c in range(CHUNKS)] for h in range(2)]

        def open_turned(b, numbers, eye):
            banks = []
            for c in range(CHUNKS):
                bank = take_bank(numbers[c], [P, 4, P])
                for s in range(4):
                    cells = tols[b][:, c * BANK + s * P : c * BANK + (s + 1) * P]
                    nc.tensor.matmul(bank[:, s, :], cells, eye[:], start=(s == 0), stop=False, is_transpose=True)
                banks.append(bank)
            return banks

        def close_cells(b, banks, c, eye):
            for s in range(4):
                cols = slice(c * BANK + s * P, c * BANK + (s + 1) * P)
                nc.tensor.matmul(banks[c][:, s, :], pages[b % 2][:, cols], eye[:], start=False, stop=(s == 3), is_transpose=True)

        def copy_turned(b, banks, c, copy):
            copy(
                out=z_t[b // 2][c][:, :, :, b % 2, :].rearrange("t u s (p e) -> t u s p e", e=2),
                in_=banks[c][:].rearrange("t s (p u e) -> t u s p e", u=2, e=2),
            )

        def close_turned(b, banks, copies, eye, chunks=range(CHUNKS)):
            for c in chunks:
                close_cells(b, banks, c, eye)
                copy_turned(b, banks, c, copies[c % 2])

        eyes = []

        def identity_on(tag):
            eyes.append(keep.tile([P, P], F32, name="eye", tag=tag, align_bytes=64))
            nc.scalar.copy(out=eyes[-1][:], in_=ident[:])
            return eyes[-1]

        def turn_back(h, c, copy, number):
            words = z_t[h][c][:].rearrange("t u s b x -> t (u s b x)").bitcast(F32)
            bank = take_bank(number, [P, 2, 2 * P])
            for u in range(2):
                for m in range(2):
                    w0 = (2 * u + m) * P
                    nc.tensor.transpose(bank[:, u, m * P : (m + 1) * P], words[:, w0 : w0 + P], ident[:])
            copy(
                out=z_bf[h][c][:].bitcast(F32).rearrange("p (t u) -> p t u", u=2),
                in_=bank[:].rearrange("p u t -> p t u"),
            )

        z_codes = []

        def quantize_z(h, c):
            cols = slice(c * 2 * P, (c + 1) * 2 * P)
            nc.vector.quantize_mx(out=z_codes[h][:, cols].bitcast(E4M3), scales=z_plane[h][:, cols], in_=z_bf[h][c][:])

        def half_scores(h, c, acc):
            cols = slice(c * 2 * P, (c + 1) * 2 * P)
            for g in range(2):
                nc.tensor.matmul_mx(
                    out=acc[:, g, :],
                    lhsT=pad_codes[:, 2 * h + g, :].bitcast(E4M3),
                    lhsT_scale=wo_plane[:, 0:P] if h == g else pad_plane[:],
                    rhs=z_codes[h][:, cols].bitcast(E4M3),
                    rhs_scale=z_plane[h][:, cols],
                    start=(h == 0 and g == 0),
                    stop=(h == 1 and g == 1),
                )

        weights = []

        def weigh(w):
            n = len(weights)
            nc.scalar.activation(out=w, in_=wgo_sb[:], func=ACT.Copy, scale=bay_sb[:, n : n + 1])
            weights.append(w)

        last = ROW_BLOCKS - 1
        on_scalar = (nc.scalar.copy, nc.scalar.copy)
        features(2, 0, BANK, h2, 0, 5)
        features(2, BANK, S, h2, 0, 6)
        banks = open_turned(0, (0, 1, 2, 3), ident)
        close_turned(0, banks, on_scalar, ident)
        fill_cells(2, 0, S, h2, 0)
        banks = open_turned(1, (7, 4, 5, 6), ident)
        features(last, 0, BANK, h3, 0, 0)
        close_turned(1, banks, on_scalar, ident)
        spare_banks, z_banks = (1, 2, 3, 0), (4, 5, 6, 7)
        z_codes.append(keep.tile([P, WIDE], U32, name="z_codes0", align_bytes=64))
        z_codes.append(keep.tile([P, WIDE], U32, name="z_codes1", align_bytes=64))
        for c in range(CHUNKS):
            turn_back(0, c, nc.scalar.copy, spare_banks[c])
            quantize_z(0, c)
            if c == EARLY - 1:
                features(last, BANK, S, h3, 0, 7)
                fill_cells(last, 0, S, h3, 0)
        banks = open_turned(2, z_banks, ident)
        eye = identity_on("z_t0_3")
        close_turned(2, banks, on_scalar, eye, range(CHUNKS - 1))
        close_cells(2, banks, CHUNKS - 1, eye)
        last_banks = open_turned(last, spare_banks, eye)
        early_weights = keep.tile([P, 2 * PICK], F32, name="early_weights", tag="page0", align_bytes=64)
        weigh(early_weights[:, 0:PICK])
        copy_turned(2, banks, CHUNKS - 1, nc.scalar.copy)
        eye = identity_on("z_t0_3")
        weigh(early_weights[:, PICK : 2 * PICK])
        banks = last_banks
        first = [take_bank(z_banks[CHUNKS - 1], [P, 2, 2 * P])]
        for k in range(3):
            nc.tensor.matmul_mx(
                out=first[0][:, 0, :],
                lhsT=wo_codes[:, 0:P].bitcast(E4M3),
                lhsT_scale=wo_plane[:, 0:P],
                rhs=z_codes[0][:, 0 : 2 * P].bitcast(E4M3),
                rhs_scale=z_plane[0][:, 0 : 2 * P],
                start=True,
                stop=True,
            )
        half_scores(0, 0, first[0])
        bays = [keep.tile([P, T2], F32, name="bays0", tag="tol1"), keep.tile([P, T2], F32, name="bays1", tag="wa_bf3", align_bytes=64)]
        for page in bays:
            nc.gpsimd.memset(page[:], 0.0)

        joined_codes = keep.tile([P, WIDE], U32, name="joined_codes", align_bytes=64)
        joined_plane = keep.tile([P, WIDE], U8, name="joined_plane", align_bytes=64)
        lower, upper = slice(0, HALF), slice(HALF, P)

        def move(dst, dst_rows, h, src_rows):
            for to, of in zip(dst, (z_codes[h], z_plane[h])):
                nc.sync.dma_start(out=to[dst_rows, :].bitcast(I32), in_=of[src_rows, :].bitcast(I32))

        groups = ((z_codes[0], z_plane[0]), (joined_codes, joined_plane))
        move(groups[1], lower, 0, upper)
        by_turns = (nc.scalar.copy, nc.vector.tensor_copy)
        vector_back = 1
        ys = [keep.tile([P, T2], F32, name="y0", tag="y0")]
        close_turned(last, banks, by_turns, eye)
        for c in range(CHUNKS):
            turn_back(1, c, by_turns[c == vector_back], (z_banks[: CHUNKS - 1] + spare_banks[:1])[c])
            quantize_z(1, c)
        for c in range(EARLY, CHUNKS):
            first.append(take_bank(spare_banks[c], [P, 2, 2 * P]))
            half_scores(0, c, first[c])
        for c in range(CHUNKS):
            half_scores(1, c, first[c])
        for c in range(CHUNKS):
            by_turns[(c + 1) % 2](
                out=ys[0][:, c * BANK : (c + 1) * BANK].rearrange("p (m g t) -> p m g t", m=2, g=2),
                in_=first[c][:].rearrange("p g (m t) -> p m g t", m=2),
            )
        move(groups[0], upper, 1, lower)
        move(groups[1], upper, 1, upper)

        picked = []
        first_squares = keep.tile([P, PICK], F32, name="first_squares", tag="y1")
        early_squares = keep.tile([P, PICK], F32, name="early_squares", tag="y3")
        rest_squares = keep.tile([P, PICK], F32, name="rest_squares", tag="late")
        squares = keep.tile([P, PICK], F32, name="squares")

        def products(n):
            y = keep.tile([P, T2], F32, name="y%d" % n, tag=("y0", "y1", "tol2", "y3")[n % 4])
            cells = y[:].rearrange("p (k g t) -> p g k t", g=2, t=P)
            for g, (codes, plane) in enumerate(groups):
                for j in range(2):
                    acc = take_bank(z_banks[2 * g + j], [P, 4, P])
                    nc.tensor.matmul_mx(
                        out=acc[:].rearrange("p k t -> p (k t)"),
                        lhsT=wo_codes[:, n * P : (n + 1) * P].bitcast(E4M3),
                        lhsT_scale=wo_plane[:, n * P : (n + 1) * P],
                        rhs=codes[:, j * BANK : (j + 1) * BANK].bitcast(E4M3),
                        rhs_scale=plane[:, j * BANK : (j + 1) * BANK],
                        start=True,
                        stop=True,
                    )
                    nc.scalar.copy(out=cells[:, g, 4 * j : 4 * (j + 1), :], in_=acc[:])
            ys.append(y)

        def pick(n, m0, m1):
            nc.vector.tensor_copy(picked[n][:, m0:m1], ys[n][:].indirect(idx3[:, entries(m0, m1)]))

        def bell(n, m0, m1):
            x = picked[n][:, m0:m1]
            whole = squares if n > 1 else first_squares if n == 0 else rest_squares if m0 else early_squares
            scratch = whole[:, 0 : m1 - m0]
            nc.scalar.activation(out=scratch, in_=x, func=ACT.Square)
            nc.scalar.activation(out=x, in_=scratch, func=ACT.Exp, scale=-0.4)

        def place(n, m0, m1):
            nc.vector.tensor_tensor(bays[n % 2][:].indirect(idx4[:, entries(m0, m1)]), picked[n][:, m0:m1], weights[n][:, m0:m1], MULT)

        def store(n):
            if n + 1 < OUT_BLOCKS:
                nc.sync.dma_start(out=out[n * P : (n + 1) * P, :], in_=bays[n % 2][:])
            else:
                for queue, cols in ((nc.sync, slice(0, WIDE)), (nc.scalar, slice(WIDE, T2))):
                    queue.dma_start(out=out[n * P : (n + 1) * P, cols], in_=bays[n % 2][:, cols])

        def pick_block(n):
            picked.append(ring.tile([P, PICK], F32, name="x", tag="x"))
            pieces = ((0, LEAD), (LEAD, PICK)) if n < 2 else ((0, PICK),)
            for m0, m1 in pieces:
                pick(n, m0, m1)
            for m0, m1 in pieces:
                bell(n, m0, m1)

        pick_block(0)
        place(0, 0, LEAD)
        place(0, LEAD, PICK)
        store(0)
        products(1)
        products(2)
        pick_block(1)
        late = keep.tile([P, OUT_BLOCKS - 2, PICK], F32, name="late", tag="late")
        for n in range(1, OUT_BLOCKS):
            if n + 2 < OUT_BLOCKS:
                products(n + 2)
            if n + 1 < OUT_BLOCKS:
                pick_block(n + 1)
            place(n, 0, PICK)
            store(n)
            if n + 1 < OUT_BLOCKS:
                weigh(late[:, n - 1, :])
